import numpy as np, ml_dtypes
CORES = [66,74,82,90,194,202,210,218]
N = 8
import mx_ref
BF = ml_dtypes.bfloat16
def gentries(a):
    return np.ascontiguousarray(a.reshape(8, 16, -1).transpose(0, 2, 1)).reshape(8, -1)
def gtable(e):
    e = np.asarray(e); return np.ascontiguousarray(e.reshape(8, -1, 16).transpose(0, 2, 1)).reshape(128, -1).astype(np.int32)
def gcols(t, e):
    v = np.concatenate([t.reshape(8, 16, -1, 4), np.zeros((8, 16, 1, 4), BF)], axis=2)
    return np.ascontiguousarray(np.stack([v[g][:, e[g]] for g in range(8)])).reshape(128, -1)
def tile(rs):
    return np.stack(rs, axis=2).reshape(128, -1).astype(BF)
def pick(q, e):
    c = np.concatenate([q[0].reshape(128, -1, 4), np.zeros((128, 1, 4), np.uint8)], axis=1); s = np.concatenate([q[1], np.ones((16, 1), np.uint8)], axis=1)
    return (np.ascontiguousarray(c[:, e].reshape(128, -1)), np.ascontiguousarray(s[:, e]))
def join(*qs):
    return (np.concatenate([q[0] for q in qs], axis=1), np.concatenate([q[1] for q in qs], axis=1))
def put(q, e, v):
    c, s = q[0].reshape(128, -1, 4).copy(), q[1].copy(); c[:, e] = v[0].reshape(128, -1, 4); s[:, e] = v[1]
    return (c.reshape(128, -1), s)
def pk(c, s):
    return (np.ascontiguousarray(c), mx_ref.live(s))
def emit(q):
    return q[0], q[1]
def packed(v, rng):
    q = [mx_ref.quantize(np.ascontiguousarray(v[r])) for r in range(N)]
    return np.stack([a for a, b in q]), np.stack([mx_ref.plane(b, rng) for a, b in q])
def values_of_codes():
    e, c = np.zeros((128, 128, 4), np.float32), np.zeros((128, 2, 4), np.uint8)
    e[np.arange(128), np.arange(128), 0] = 1
    c[:127, :, 0] = np.arange(256).reshape(2, 128).T[:127]
    return mx_ref.matmul(mx_ref.quantize(e.reshape(128, 512).astype(BF)), (c.reshape(128, 8), np.full((16, 2), 127, np.uint8))).T.reshape(-1).astype(np.float64)
CODE_VALUE, SCALE_VALUE = values_of_codes(), 2.0 ** (np.arange(256) - 127.0)
def decode(q):
    return (CODE_VALUE[q[0]].reshape(16, 8, -1, 4) * SCALE_VALUE[q[1]][:, None, :, None] + 0.0).reshape(128, -1).astype(np.float32)
def f(rng, *shape):
    return mx_ref.flush((rng.standard_normal(shape, dtype=np.float32) * np.exp2(rng.integers(-2, 3, shape[:-1] + (1,)))).astype(BF))
def wide(rng, *shape, cols=0):
    v = rng.standard_normal(shape, dtype=np.float32) * np.exp2(rng.integers(-12, 13, shape)).astype(np.float32)
    if cols: v *= np.repeat(np.exp2(rng.integers(-cols, cols + 1, shape[:-2] + (1, shape[-1] // 4))) * (rng.random(shape[:-2] + (1, shape[-1] // 4)) > 0.0625), 4, axis=-1).astype(np.float32)
    return mx_ref.flush(v.astype(BF))
C, T, P, A = 320, 20, 7, 7
MASK = [1, 2, 4]
def numbers_of(rng):
    return {"x": np.array(f(rng, N, 128, 4 * C)), "u": np.array(f(rng, N, 128, 512)), "v": np.array(f(rng, N, 128, 512))}
def lists_of(e):
    return np.stack([gtable(e[r]) for r in range(N)])
def places(rng):
    return np.argsort(rng.random((N, 8, C)), axis=2)
def grow(rng, b):
    b[:, 0], b[:, 1] = 1, 0
    o = np.argsort(rng.random(b.shape), axis=1)
    e = np.zeros(b.shape, np.int64)
    np.put_along_axis(e, o, np.take_along_axis(o, b, axis=1), axis=1)
    return lists_of(e.reshape(N, 8, C))
def trees(rng):
    return grow(rng, rng.integers(0, np.maximum(np.arange(16), 1), (N * 8 * T, 16)))
def layers(rng):
    return np.array(f(rng, N, 128, 2048)).reshape(N, 8, 16, 4, 8, 16, 4)
def weights(rng, w, still=[]):
    for i in still:
        w[:, :, i] = 0
        w[:, :, :, :, :, i] = 0
    c, s = packed(np.ascontiguousarray(w).reshape(N, 128, 2048), rng)
    return {"wc": c, "ws": s}
def setup_inputs(rng):
    return {**numbers_of(rng), "nod": lists_of(places(rng)), "par": trees(rng), **weights(rng, layers(rng))}
def setup_inputs_ties(rng):
    d = numbers_of(rng)
    x = d["x"].reshape(N, 8, 16, C, 4)
    x[:, :, 0] = 0
    x[:, :, 0, :, 0] = rng.integers(0, 3, (N, 8, C)).astype(np.float32).astype(BF)
    u = d["u"].reshape(N, 128, 128, 4)
    u[:, :, ::16] = 0
    o = rng.permutation(N)
    for r in range(N):
        for h in range(0, 128, 16): u[r, h, h, 0] = 0.0 if r == o[0] else -1.0 if r == o[1] else 1.0
    return {"x": x.reshape(N, 128, 4 * C), "u": u.reshape(N, 128, 512), "v": d["v"], "nod": lists_of(places(rng)), "par": trees(rng), **weights(rng, layers(rng), [0])}
def setup_inputs_near(rng):
    d = numbers_of(rng)
    e = places(rng)
    o = rng.permutation(N) % 4
    x = d["x"].astype(np.float32).reshape(N, 8, 16, C, 4)
    x[:, :, 0] = 0
    x[:, :, 8:] = 0
    x[:, :, 0, :, 0] = rng.choice([-1.0, 1.0], 8)[None, :, None]
    x[:, :, 8] = ((rng.integers(0, 16, (N, 8, C))[..., None] >> np.arange(4)) & 1) * np.exp2(np.arange(4) - 23.0)
    x[:, :, 11, :, 0] = 2.0 ** -10
    u = d["u"].reshape(N, 128, 128, 4)
    u[:, :, ::16] = 0
    for r in range(N):
        k = 1.0 if o[r] == 0 else 2.0 ** -30
        if o[r] == 2:
            far = np.take_along_axis(e[r].reshape(8, T, 16), np.argsort(rng.random((8, T, 16)), axis=2)[:, :, :2], axis=2)
            x[r, :, 0] = 0
            for g in range(8):
                x[r, g, 0, far[g, :, 0], 0] = 1.0
                x[r, g, 0, far[g, :, 1], 0] = -1.0
        if o[r] == 3:
            x[r, :, 8:] = 0
            x[r, :, 10, :, 0] = rng.choice([1.0, 1.125], (8, C)) * 2.0 ** -27
        for h in range(0, 128, 16):
            if o[r] < 2:
                u[r, h, h, 0] = k
                u[r, h + 11, h, 0] = k
            if o[r] == 2: u[r, h, h, 0] = 1.0
            if o[r] < 3: u[r, h + 8, h] = k
            else: u[r, h + 10, h, 0] = k
    return {"x": x.reshape(N, 128, 4 * C).astype(BF), "u": u.reshape(N, 128, 512), "v": d["v"], "nod": lists_of(e), "par": trees(rng), **weights(rng, layers(rng), [0, 8, 9, 10, 11, 12, 13, 14, 15])}
def setup_inputs_huge(rng):
    d = numbers_of(rng)
    o = rng.permutation(N)
    h = int(np.argmin(o))
    c = rng.choice([-1.0, 1.0], (N, 1, 1, C, 1))
    c[o % 4 == 1] = -1.0
    x = (0.6 + 0.09 * rng.random((N, 8, 16, C, 4))) * c
    x[h] = 0.875 * c[h]
    x[h, 0, 0] = (0.5 + 0.375 * rng.random((C, 4))) * c[h, 0, 0]
    a = 1.0 - 0.1 * rng.random((N, 128, 8, 4))
    a[h] = 1.0
    u = d["u"].reshape(N, 128, 128, 4)
    u[:, :, ::16] = (2.0 ** 30 * a).astype(np.float32).astype(BF)
    w = np.zeros((N, 128, 4, 128, 4), np.float32)
    i = np.arange(128)
    for b in range(4): w[:, i, b, i, b] = -1
    return {"x": (2.0 ** 30 * x).astype(np.float32).reshape(N, 128, 4 * C).astype(BF), "u": u.reshape(N, 128, 512), "v": d["v"], "nod": lists_of(places(rng)), "par": trees(rng), **weights(rng, w.astype(BF))}
def setup_inputs_forms(rng):
    d = numbers_of(rng)
    x = d["x"].reshape(N, 8, 16, C, 4)
    z = (N, 8, 8, C, 4)
    n = rng.integers(8, 15, z)
    n[:, :, 1, :, 0] = (rng.permutation(8) % 7 + 8)[:, None]
    x[:, :, 8:] = ((9 + 2 * rng.integers(0, 4, z)) * np.exp2(-3.0 - n) * rng.choice([-1.0, 1.0], z)).astype(np.float32).astype(BF)
    x[:, :, 8, :, 0] = 1.96875
    i = np.arange(16)
    b = np.stack([0 * i, np.maximum(i - 1, 0), i % 2, np.where(i < 8, np.maximum(i - 1, 0), 7)])
    k = rng.integers(0, 4, (N, 8 * T))
    e = rng.permutation(N)
    k[e[0]] = 0
    k[e[1]] = 1
    u = d["u"].reshape(N, 128, 128, 4)
    for r in e[N // 2:]:
        u[r, :, ::16] = 0
        for h in range(0, 128, 16): u[r, h + 9, h, 0] = 1.0
    w = layers(rng)
    w[:, :, :, :, :, 8:] = 0
    return {"x": x.reshape(N, 128, 4 * C), "u": u.reshape(N, 128, 512), "v": d["v"], "nod": lists_of(places(rng)), "par": grow(rng, b[k.reshape(-1)]), **weights(rng, w)}
def setup_inputs_spread(rng):
    d = setup_inputs(rng)
    d["x"] = wide(rng, N, 128, 4 * C, cols=6)
    return d
def check_inputs(d):
    b = []
    for k in ("x", "u", "v"):
        a = np.abs(d[k].astype(np.float32))
        if not (np.isfinite(a).all() and ((a == 0) | (a >= 2.0 ** -30) & (a <= 2.0 ** 30)).all()): b.append("a value of " + k)
    e = np.stack([gentries(d["nod"][r]) for r in range(N)])
    if (np.sort(e, axis=2) != np.arange(C)).any(): b.append("nod: a group whose entries aren't every column once")
    e = np.stack([gentries(d["par"][r]) for r in range(N)]).reshape(-1, 16).astype(np.int64)
    i = np.arange(16)
    if ((e < 0) | (e > 15)).any(): b.append("an entry of par")
    else:
        two = (np.take_along_axis(e, e, axis=1) == i) & (e != i)
        far = e
        for j in range(4): far = np.take_along_axis(far, far, axis=1)
        if (np.count_nonzero(two, axis=1) != 2).any() or (e == i).any() or not np.take_along_axis(two, far, axis=1).all(): b.append("par: links that aren't a tree's")
    none, least, most = [emit(mx_ref.quantize(np.full((128, 16), k, np.float32).astype(BF)))[1][0, 0] for k in (0.0, 2.0 ** -30, 2.0 ** 30)]
    for r in range(N):
        if ((d["wc"][r] == 0x7F) | (d["wc"][r] == 0xFF)).any(): b.append("wc: a code that is no number")
        s = mx_ref.live(d["ws"][r])
        if ((s != none) & ((s < least) | (s > most))).any(): b.append("ws: a scale out of range")
    return b
def reference(x, u, v, nod, par, wc, ws):
    qu = [mx_ref.quantize(u[r]) for r in range(N)]
    lay = [pk(wc[r], ws[r]) for r in range(N)]
    now = [x[r] for r in range(N)]
    place = np.stack([gentries(nod[r]) for r in range(N)]).reshape(-1, 16).astype(np.int64)
    link = np.stack([gentries(par[r]) for r in range(N)]).reshape(-1, 16).astype(np.int64)
    m = np.arange(N * 8 * T)
    for mask in MASK:
        q = [mx_ref.quantize(now[r]) for r in range(N)]
        own = [decode(q[r]) for r in range(N)]
        s = np.stack([mx_ref.matmul(qu[r], q[r])[::16] for r in range(N)]) + np.float32(0.0)
        s = np.take_along_axis(s, place.reshape(N, 8, C), axis=2).reshape(-1, 16)
        o = np.argsort(-s, axis=1, kind="stable")
        st = np.argsort(o, axis=1)
        col = np.take_along_axis(place, o, axis=1)
        to = np.take_along_axis(st, link, axis=1)
        edge = np.zeros((len(m), 16, 16), bool)
        edge[m[:, None], st, to] = True
        edge[m[:, None], to, st] = True
        word = np.zeros((len(m), 14), np.int64)
        for j in range(14):
            a = np.argmax(np.count_nonzero(edge, axis=2) == 1, axis=1)
            word[:, j] = np.argmax(edge[m, a], axis=1)
            edge[m, a, word[:, j]] = False
            edge[m, word[:, j], a] = False
        give = np.take_along_axis(col, word[:, A:], axis=1).reshape(N, 8, T * P)
        sent = [mx_ref.quantize(gcols(own[r].astype(BF), give[r])) for r in range(N)]
        other = word.reshape(N, 8 * T, 14)[np.arange(N) ^ mask].reshape(-1, 14)
        c = np.concatenate([word[:, :A], other[:, A:]], axis=1)
        free = np.ones((len(m), 16), bool)
        need = np.count_nonzero(c[:, :, None] == np.arange(16), axis=1)
        to, src = np.zeros((len(m), 16), np.int64), np.zeros((len(m), 16), np.int64)
        for j in range(14):
            a = np.argmax(free & (need == 0), axis=1)
            to[m, a] = c[:, j]
            src[m, a] = col[m, c[:, j]] if j < A else C + P * (m % T) + j - A
            free[m, a] = False
            need[m, c[:, j]] -= 1
        a = np.argmax(free, axis=1)
        free[m, a] = False
        b = np.argmax(free, axis=1)
        to[m, a], to[m, b] = b, a
        src[m, a], src[m, b] = col[m, b], col[m, a]
        link = np.zeros((len(m), 16), np.int64)
        np.put_along_axis(link, o, np.take_along_axis(o, to, axis=1), axis=1)
        e = np.zeros((N, 8, C), np.int64)
        np.put_along_axis(e, col.reshape(N, 8, C), src.reshape(N, 8, C), axis=2)
        for r in range(N):
            both = np.concatenate([own[r], decode(sent[r ^ mask])], axis=1).astype(BF)
            z = ((own[r] + gcols(both, e[r]).astype(np.float32)) * np.float32(0.5)).astype(BF)
            qz = mx_ref.quantize(z)
            now[r] = tile([mx_ref.matmul(pick(lay[r], np.arange(128 * k, 128 * k + 128)), qz) * np.float32(0.03125) + z[:, k::4].astype(np.float32) for k in range(4)])
    y = np.zeros((N, 128, C), np.float32)
    oc, osc = np.zeros((N, 128, 4 * C), np.uint8), np.zeros((N, 16, C), np.uint8)
    for r in range(N):
        q = mx_ref.quantize(now[r])
        y[r] = mx_ref.matmul(mx_ref.quantize(v[r]), q)
        oc[r], osc[r] = emit(q)
    return {"y": y, "op": link.reshape(N, 8, C).astype(np.float32), "oc": oc, "osc": osc}

@@ -1,0 +1,600 @@
+import numpy as np
+from concourse.mybir import dt, AluOpType, ActivationFunctionType
+
+A = AluOpType
+AF = ActivationFunctionType
+C, TR, VW = 320, 20, 160
+WW = C + VW
+H = C // 2
+PO, SO = 64.0, 224.0
+MASKS = [1, 2, 4]
+Q4, U8, BF, F32, I32, U16 = "float8_e4m3fn_x4", "uint8", "bfloat16", "float32", "int32", "uint16"
+
+SCRATCH = {}
+
+
+def _decl(dtype, **kw):
+    for k, n in kw.items():
+        SCRATCH[k] = ("sbuf", [128, n], dtype)
+
+
+NF = "self k3 j0f j1f n1 n2 fa fb dla dlb pa pb qa qb szn csz stm own o2f st16 na".split()
+NU = "nodu j0u m2u stu sou keyu idxu pnu ou cgu o2u eu idxp".split()
+_decl(Q4, qx=C, qz=C, qu0=128, qu=128, qv=128, wq=512, qe=512)
+_decl(U8, sx=C, sz=C, su0=128, su=128, sv=128, wsb=512, se=512)
+for _r in range(3):
+    _decl(Q4, **{"qs%d" % _r: VW, "ql%d" % _r: VW})
+    _decl(U8, **{"ss%d" % _r: VW, "sl%d" % _r: VW})
+    _decl(BF, **{"snd%d" % _r: TR, "lnd%d" % _r: TR})
+_decl(BF, xt=4 * C, zt=4 * C, z32=4 * C, x32=4 * C, ut=512, vt0=512, ebuf=528, win=4 * WW, vt=4 * VW, hh=2 * C,
+      loc=C, k16r=C, k64r=C, iob=256, iom=C, ios=C, l32=C, diag=C, sig=C, keep=C, keep32=C, d0s=C, dd=C,
+      maskv=C, tj=256, tw=256, to=256, tm=256, te=2 * C, t16=16, ma=C, mb=C, mc=C, fo=2 * C, cmp=C, sc1=C, sc2=C,
+      scs=C, xx=C, ks=C, cs=C, kb=C, strep=C, stb=C, em=C + 16, yy=C, b1=C, b2=C, b3=C, b4=C, nodrep=C, osrep=C,
+      srcw=WW, lnkj=C, srcj=C, la=C + 32, lb=C + 32, tb=2 * C + 32)
+_decl(F32, iot=512, dtt=C, ssb=C, sn=C + 32, tt=2 * C + 32, neg=C, f1=C, ysb=C, oprep=C, col=32, k64=32, n7=32,
+      lk=TR + 32, nf=TR * len(NF))
+_decl(I32, pi=2, ri=2, nodi=TR, pari=TR)
+_decl(U16, invu=TR, tsel=TR, tsn=2, upk=8, j1u=32, j2u=32, j4u=32, j8u=32, vu=10, tu=TR, idxw=TR, nu=TR * len(NU))
+for _b in range(8):
+    SCRATCH["ps%d" % _b] = ("psum", [128, 512], F32)
+
+_DMAS = ["dx", "du", "dw", "dws", "dv", "dpar", "dnod", "dop", "doc", "dos", "dy"]
+SEMAPHORES = ["cv", "cs", "ct", "cg", "sent"] + _DMAS + ["aw0", "aw1", "aw2", "av0", "av1", "av2"]
+
+SMALL = set(NF + NU + "invu tsel0 tsel1 tsn upk vu tu idxw k64 lka ri0 ri1 pi ks cs t16 emp snd0 snd1 snd2".split())
+LONG = {"qx": 400, "qz": 400, "qs0": 220, "qs1": 220, "qs2": 220, "f1": 360, "tt0": 360, "tt1": 400, "b3": 1300,
+        "qu": 290, "su": 290, "n7": 130, "lkb": 130, "tw": 160, "j1u": 130, "j2u": 130, "j4u": 130, "j8u": 130,
+        "tm": 250, "to": 300, "tj": 250, "iot": 1200, "ebuf": 1200, "iob": 700, "srcwc": 500}
+HOP, FAR, LOAD, TRIES, CHOSEN = 70, 2400, 2000, 500, []
+
+
+def _length(q, rd, wr, picked):
+    k = wr[0] if wr else ""
+    if q == "t":
+        return 250
+    if q == "g":
+        return 150 if k == "pi" else LONG.get(k, 850) if k[:1] != "r" else 300
+    if k in LONG:
+        return LONG[k]
+    if picked:
+        return 340 if k[0] == "v" else 600
+    if k in SMALL or k[:2] == "c_":
+        return 100
+    if q == "s":
+        return 200 if len(wr) > 1 and wr[1][0] == "u" else 360
+    return 360 if any(r[:2] == "ps" for r in rd) else 200
+
+
+def _order(ops):
+    if CHOSEN:
+        return [ops[n][:5] for n in CHOSEN]
+    last, readers, deps, users = {}, {}, [], [[] for o in ops]
+    for n, o in enumerate(ops):
+        d = set(last[k] for k in o[2] + o[3] if k in last)
+        for k in o[3]:
+            d.update(readers.get(k, []))
+        d.discard(n)
+        deps.append(d)
+        for m in d:
+            users[m].append(n)
+        for k in o[2]:
+            readers.setdefault(k, []).append(n)
+        for k in o[3]:
+            last[k] = n
+            readers[k] = []
+
+    def replay(order, pick, hop, far):
+        done, free = {}, {}
+        for n in order:
+            q, c, late = ops[n][0], ops[n][5] * (pick if ops[n][7] else 1.0), ops[n][6] * far
+            t = max([free.get(q, 0)] + [done[m] + hop for m in deps[n]])
+            if q is not None:
+                free[q] = t + c
+            done[n] = t + c + late
+        return max(done.values())
+
+    rng, best = np.random.RandomState(1), None
+    for attempt in range(TRIES):
+        shake = 1.0 + (0.5 if attempt else 0.0) * (rng.rand(len(ops)) - 0.5)
+        slack = (0, 60, 150)[attempt % 3]
+        way = [0] * len(ops)
+        for n in range(len(ops) - 1, -1, -1):
+            way[n] = (ops[n][5] + ops[n][6]) * shake[n] + max([way[m] + HOP for m in users[n]] + [0])
+        left = [len(d) for d in deps]
+        at, free, out = [0] * len(ops), {}, []
+        ready = [n for n in range(len(ops)) if not left[n]]
+        while ready:
+            start = {n: max(at[n], free.get(ops[n][0], 0)) for n in ready}
+            a = min(ready, key=lambda n: (start[n], -way[n]))
+            n = max((m for m in ready if ops[m][0] == ops[a][0] and start[m] <= start[a] + slack), key=lambda m: way[m])
+            ready.remove(n)
+            out.append(n)
+            if ops[n][0] is not None:
+                free[ops[n][0]] = start[n] + ops[n][5]
+            for m in users[n]:
+                at[m] = max(at[m], start[n] + ops[n][5] + ops[n][6] + HOP)
+                left[m] -= 1
+                if not left[m]:
+                    ready.append(m)
+        end = sum(replay(out, *k) for k in ((1.0, HOP, 1.0), (0.75, HOP, 1.3), (1.25, 2 * HOP, 0.7), (1.0, 2 * HOP, 1.4)))
+        if best is None or end < best[0]:
+            best = (end, out)
+    CHOSEN.extend(best[1])
+    return [ops[n][:5] for n in CHOSEN]
+
+
+def _emit(g, T, ops):
+    qs = {"v": g.vector, "s": g.scalar, "t": g.tensor, "g": g, "y": g.sync}
+    last, readers, known, clock, waits, needed, pos = {}, {}, {q: {} for q in qs}, [], [], set(), {}
+    src = []
+    for n, (q, fn, rd, wr, sem) in enumerate(ops):
+        if sem is None:
+            pos[q] = pos.get(q, 0) + 1
+            src.append((q, pos[q]))
+        else:
+            src.append((sem[0], 1))
+        if q is None:
+            clock.append({sem[0]: 1})
+            waits.append([])
+            for k in wr:
+                last[k] = n
+                readers[k] = []
+            continue
+        deps = set()
+        for k in rd:
+            if k in last:
+                deps.add(last[k])
+        for k in wr:
+            if k in last:
+                deps.add(last[k])
+            deps.update(readers.get(k, []))
+        w = []
+        for d in sorted(deps, reverse=True):
+            s, lev = src[d]
+            if known[q].get(s, 0) >= lev:
+                continue
+            w.append(d)
+            needed.add(d)
+            for k, v in clock[d].items():
+                if known[q].get(k, 0) < v:
+                    known[q][k] = v
+        waits.append(w)
+        ck = dict(known[q])
+        ck[src[n][0]] = src[n][1]
+        clock.append(ck)
+        for k in rd:
+            readers.setdefault(k, []).append(n)
+        for k in wr:
+            last[k] = n
+            readers[k] = []
+    count, value = {}, {}
+    for n, (q, fn, rd, wr, sem) in enumerate(ops):
+        if sem is None:
+            if n in needed:
+                count[q] = count.get(q, 0) + 1
+                value[n] = ("c" + q, count[q])
+        else:
+            value[n] = sem
+    for n, (q, fn, rd, wr, sem) in enumerate(ops):
+        if q is None:
+            continue
+        for d in waits[n]:
+            qs[q].wait_ge(T.sem[value[d][0]], value[d][1])
+        ins = fn()
+        if ins is None:
+            continue
+        if sem is None:
+            if n in needed:
+                ins.then_inc(T.sem["c" + q], 1)
+        else:
+            ins.then_inc(T.sem[sem[0]], 16)
+
+
+def rank_program(g, core, T, topo):
+    rank = T.rank_of(core)
+    if rank is None:
+        return
+    ops, picked = [], [False]
+    V, S = g.vector, g.scalar
+
+    def op(q, fn, rd, wr, sem=None, late=0):
+        rd, wr = rd.split(), wr.split()
+        if q is None:
+            ops.append((q, fn, rd, wr, sem, 0, 0, False))
+        elif sem is not None:
+            ops.append((q, fn, rd, wr, sem, 80, LOAD + late, False))
+        else:
+            ops.append((q, fn, rd, wr, sem, _length(q, rd, wr, picked[0]), late, picked[0]))
+        picked[0] = False
+
+    def ts(out, in0, s1, o0, rd, wr, s2=None, o1=None):
+        if o1 is None:
+            op("v", lambda: V.tensor_scalar(out, in0, s1, None, o0), rd, wr)
+        else:
+            op("v", lambda: V.tensor_scalar(out, in0, s1, s2, o0, o1), rd, wr)
+
+    def tt(out, a, b, o, rd, wr):
+        op("v", lambda: V.tensor_tensor(out, a, b, o), rd, wr)
+
+    def cp(out, a, rd, wr):
+        op("v", lambda: V.tensor_copy(out, a), rd, wr)
+
+    def scan(out, d0, d1, o0, o1, rd, wr, ini=0.0):
+        op("v", lambda: V.tensor_tensor_scan(out, d0, d1, ini, o0, o1), rd, wr)
+
+    def seg(out, a, o, rd, wr):
+        scan(out, T.keep[:], a, A.mult, o, rd + " keep", wr)
+
+    def place(out, a, rd, wr):
+        scan(out, T.k64r[:], a, A.max, A.add, rd + " k64r", wr, -PO)
+
+    def mset(out, c, wr):
+        op("v", lambda: V.memset(out, c), "", wr)
+
+    def act(out, a, rd, wr, scale=1.0):
+        op("s", lambda: S.activation(out, a, AF.Copy, scale=scale), rd, wr)
+
+    def lin(out, a, scale, bias, rd, wr, fn=AF.Identity):
+        op("s", lambda: S.activation(out, a, fn, bias=bias, scale=scale), rd, wr)
+
+    def quant(q, s, a, rd, wr):
+        op("v", lambda: V.quantize_mx(q, s, a), rd, wr)
+
+    def mm(out, lq, ls, rq, rs, rd, wr):
+        op("t", lambda: g.tensor.matmul_mx(out, lq, ls, rq, rs, True, True), rd, wr, None, 100)
+
+    def iota(out, pat, base, mul, wr, flt=True):
+        if flt:
+            op("g", lambda: g.iota(out, pat, base, mul, allow_small_or_imprecise_dtypes=True), "", wr)
+        else:
+            op("g", lambda: g.iota(out, pat, base, mul), "", wr)
+
+    def dma(q, out, a, rd, wr, sem, n=16, late=0):
+        e = g.sync if q == "y" else g.scalar
+        op(q, lambda: e.dma_start(out, a), rd, wr, (sem, n), late)
+
+    def by(win, off):
+        picked[0] = True
+        return win.indirect(off)
+
+    def ends(t):
+        return t[:, 15:C:16]
+
+    def starts(t):
+        return t[:, 0:C:16]
+
+    def mid(t):
+        return t[:, 16:C + 16]
+
+    def turn(t, key):
+        op("v", lambda: V.transpose(T.tb[:, 0:C], mid(t)), key, "tb0")
+        op("v", lambda: V.transpose(T.tb[:, C:2 * C + 32], t[:]), "%s c_p%s c_q%s" % (key, key, key), "tb1")
+
+    def nat(out, key):
+        ts(out[:], by(T.tb[:], T.tsn[:]), PO, A.add, "tb0 tb1 tsn", key)
+
+    names = ["r", "nr", "r1", "want", "cap", "msend", "mown", "o16", "vsel", "m7", "k3", "te", "to", "h", "t0", "r8",
+             "r16", "r17", "rh", "rm", "u0", "u1", "o320", "d320", "t1"]
+    cl = {n: T.col[:, i:i + 1] for i, n in enumerate(names)}
+    f = {n: T.nf[:, TR * i:TR * i + TR] for i, n in enumerate(NF)}
+    f2 = {n: T.nf[:, TR * i:TR * i + 2 * TR] for i, n in enumerate(NF[:-1])}
+    u = {n: T.nu[:, TR * i:TR * i + TR] for i, n in enumerate(NU)}
+    iot, k16n = T.iot, T.iot[:, 0:C:16]
+    ps = [T["ps%d" % b] for b in range(8)]
+    fb, ub = [1, 2, 3, 4], [5, 6, 7, 1]
+    j1, j2, j4, j8 = (t[:, 0:TR] for t in (T.j1u, T.j2u, T.j4u, T.j8u))
+    n7 = T.n7[:, 0:TR]
+
+    dma("s", T.pari[:], T.par[:], "", "pari", "dpar")
+    dma("y", T.xt[:], T.x[:], "", "x0 x1 x2 x3", "dx", 16, 1500)
+    dma("s", T.nodi[:], T.nod[:], "", "nodi", "dnod")
+    dma("y", T.ut[:], T.u[:], "", "ut", "du")
+    dma("y", T.wq[:].bitcast(dt.uint8), T.wc[:], "", "wq", "dw", 16, 1500)
+    dma("y", T.wsb[:], T.ws[:], "", "wsb", "dws")
+    dma("y", T.vt0[:], T.v[:], "", "vt0", "dv")
+
+    iota(T.pi[:, 0:1], [[0, 1]], 0, 1, "pi", False)
+    iota(iot[:], [[1, 512]], 0, 0, "iot")
+    iota(T.loc[:], [[0, TR], [1, 16]], 0, 0, "loc")
+    mset(T.ebuf[:], 0.5, "ebuf0 ebuf")
+    iota(T.k16r[:], [[16, TR], [0, 16]], 0, 0, "k16r")
+    op("g", lambda: g.affine_select(T.ebuf[:], T.ebuf[:], [[1, 528]], A.is_equal, 0.0, -3, -4), "ebuf", "ebuf")
+    iota(T.ks[:], [[0, C]], 0, 0, "ks0 ks")
+    iota(T.iob[:], [[1, 256]], 0, 0, "iob")
+    iota(T.k64r[:], [[16, TR], [0, 16]], -int(PO), 0, "k64r")
+    iota(T.ios[:], [[1, C]], -int(SO), 0, "ios")
+    iota(T.l32[:], [[0, TR // 2], [1, 32]], 0, 0, "l32")
+    iota(T.srcw[:, C:WW], [[1, VW]], C - int(SO), 0, "srcwc")
+    iota(T.cs[:], [[0, C]], 0, 0, "cs0 cs")
+    iota(T.te[:, C:2 * C], [[0, C]], -64, 0, "te1")
+    iota(T.dtt[:], [[0, C]], -1, 0, "dtt")
+
+    ts(T.ri[:, 0:1], T.pi[:, 0:1], 15, A.bitwise_and, "pi", "ri0")
+    ts(T.ri[:, 1:2], T.pi[:, 0:1], 16, A.bitwise_and, "pi", "ri1")
+    for t, k in ((T.sn, "sn"), (T.la, "la"), (T.lb, "lb")):
+        mset(t[:, 0:16], 0.0, "c_p" + k)
+        mset(t[:, C + 16:C + 32], 0.0, "c_q" + k)
+    cp(cl["r"], T.ri[:, 0:1], "ri0", "c_r")
+    cp(cl["h"], T.ri[:, 1:2], "ri1", "c_h")
+    lin(cl["t0"], cl["h"], 0.0625, 0.0, "c_h", "c_t0")
+    ts(T.ri[:, 0:1], T.pi[:, 0:1], 1, A.bitwise_and, "pi", "ri0")
+    lin(cl["r16"], cl["r"], 16.0, 0.0, "c_r", "c_r16")
+    ts(cl["u0"], T.ri[:, 0:1], cl["t0"], A.not_equal, "ri0 c_t0", "c_u0", 336.0, A.mult)
+    lin(T.iom[:], iot[:, 0:C], 1.0, -PO, "iot", "iom")
+    lin(cl["nr"], cl["r"], -1.0, 0.0, "c_r", "c_nr")
+    lin(cl["te"], cl["h"], 21.0, cl["r"], "c_h c_r", "c_te")
+    lin(cl["to"], cl["h"], -21.0, cl["r"], "c_h c_r", "c_to")
+    lin(cl["r17"], cl["r"], 17.0, 0.0, "c_r", "c_r17")
+    ts(cl["u1"], cl["r16"], 48.0, A.min, "c_r16", "c_u1", 256.0, A.add)
+    ts(T.tsn[:, 0:1], cl["u0"], cl["r16"], A.add, "c_u0 c_r16", "tsn")
+    tt(f["j0f"], T.pari[:], k16n, A.add, "pari iot", "j0f")
+    ts(T.tsn[:, 1:2], cl["u0"], cl["u1"], A.add, "c_u0 c_u1 tsn", "tsn")
+    cp(u["j0u"], f["j0f"], "j0f", "j0u")
+    lin(f["self"], k16n, 1.0, cl["r"], "iot c_r", "self")
+    act(mid(T.la), by(T.iom[:], u["j0u"]), "iom j0u", "la")
+    act(mid(T.lb), by(mid(T.la), u["j0u"]), "la j0u", "lb")
+    cp(u["nodu"], T.nodi[:], "nodi", "nodu")
+    cp(T.upk[:], iot[:, 0:128:16], "iot", "upk")
+    ts(T.diag[:], T.loc[:], cl["r"], A.is_equal, "loc c_r", "diag")
+    tt(f["n1"], f["self"], f["j0f"], A.subtract, "self j0f", "n1")
+    ts(T.k64[:], iot[:, 0:512:16], cl["r"], A.add, "iot c_r", "k64", -PO, A.add)
+    lin(f["n2"], f["n1"], 1.0, 0.0, "n1", "n2", AF.Relu)
+    ts(T.tsel[:, 0:TR:2], iot[:, 0:C:32], cl["te"], A.add, "iot c_te", "tsel0")
+    ts(T.tsel[:, 1:TR:2], iot[:, 16:C:32], cl["to"], A.add, "iot c_to", "tsel1", 336.0, A.add)
+    quant(T.qx[:], T.sx[:], T.xt[:], "x0 x1 x2 x3", "qx")
+    quant(T.qu0[:], T.su0[:], T.ut[:], "ut", "qu0")
+    lin(T.sig[:], T.loc[:], 1.0, cl["nr"], "loc c_nr", "sig", AF.Sign)
+    turn(T.lb, "lb")
+    cp(T.qu[:].bitcast(dt.uint32), T.qu0[:].bitcast(dt.uint32).indirect(T.upk[:]), "qu0 upk", "qu")
+    op("s", lambda: S.activation(T.su[:], T.su0[:].indirect(T.upk[:]), AF.Copy), "qu0 upk", "su")
+    tt(T.n7[:], by(T.tb[:], T.tsn[:]), T.k64[:], A.is_equal, "tb0 tb1 tsn k64", "n7")
+    ts(T.tm[:], T.k16r[:, 0:256], cl["r16"], A.is_equal, "k16r c_r16", "tm")
+    tt(f["n1"], n7, f["n2"], A.mult, "n7 n2", "n1")
+    tt(T.tm[:], T.tm[:], T.diag[:, 0:256], A.max, "tm diag", "tm")
+    tt(f["j1f"], f["n1"], f["j0f"], A.add, "n1 j0f", "j1f")
+    lin(T.tm[:], T.tm[:], 2.0, -1.0, "tm", "tm")
+    cp(j1, f["j1f"], "j1f", "j1u")
+    tt(n7, f["j1f"], f["self"], A.subtract, "j1f self", "n7")
+    act(mid(T.la), by(T.iom[:], j1), "iom j1u", "la")
+    act(mid(T.lb), by(mid(T.la), j1), "la j1u", "lb")
+    lin(T.keep[:], T.loc[:], 1.0, 0.0, "loc", "keep", AF.Sign)
+    lin(T.d0s[:], T.diag[:], -2.0, 1.0, "diag", "d0s")
+    lin(starts(T.d0s), k16n, 0.0, 0.0, "iot", "c_d0s d0s")
+    for b in range(4):
+        quant(T.qe[:, 128 * b:128 * b + 128], T.se[:, 128 * b:128 * b + 128], T.ebuf[:, 3 - b:515 - b], "ebuf", "qe%d" % b)
+
+    def pair_index():
+        ts(u["m2u"], n7, cl["r17"], A.add, "n7 c_r17", "m2u")
+
+    pair_index()
+    cp(by(T.b3[:], u["nodu"]), T.iom[:], "iom nodu", "b3")
+    tt(T.b2[:], T.b3[:], T.diag[:], A.mult, "b3 diag", "tj0 b2 vb2a vb2b")
+    seg(T.yy[:], T.b2[:], A.add, "b2 vb2a", "yy")
+    ts(T.invu[:], ends(T.yy), PO, A.add, "yy", "invu")
+    lin(T.t16[:], iot[:, 0:16], 16.0, 16.0, "iot", "t16")
+    lin(cl["r1"], cl["r"], 1.0, 1.0, "c_r", "c_r1")
+    lin(cl["o16"], cl["r16"], 1.0, -224.0, "c_r16", "c_o16", AF.Relu)
+    lin(cl["want"], cl["o16"], -0.125, cl["r1"], "c_o16 c_r1", "c_want")
+    lin(cl["cap"], cl["o16"], -0.125, 16.0, "c_o16", "c_cap")
+    lin(cl["rh"], cl["r"], 0.5, 0.0, "c_r", "c_rh")
+    ts(T.tj[:], T.loc[:, 0:256], cl["want"], A.is_equal, "loc c_want", "tj", 0.0625, A.mult)
+    tt(T.tj[:], T.tj[:], T.k16r[:, 0:256], A.mult, "tj k16r", "tj")
+    ts(T.tw[:], T.tj[:], cl["cap"], A.min, "tj c_cap", "tw")
+    tt(T.to[:], T.diag[:, 0:256], T.k16r[:, 0:256], A.mult, "diag k16r", "to")
+    act(T.nodrep[:], by(T.ios[:], u["nodu"]), "ios nodu", "nodrep")
+    ts(cl["t1"], cl["r"], 14.0, A.not_equal, "c_r", "c_t1")
+    ts(cl["msend"], cl["r"], 7.0, A.is_ge, "c_r c_t1", "c_msend", cl["t1"], A.mult)
+    ts(cl["r8"], cl["r"], 8.0, A.is_ge, "c_r", "c_r8", 8.0, A.mult)
+    lin(T.keep32[:], T.l32[:], 1.0, 0.0, "l32", "keep32", AF.Sign)
+    lin(cl["mown"], cl["msend"], -1.0, 1.0, "c_msend", "c_mown")
+    ts(cl["vsel"], cl["r8"], cl["r"], A.add, "c_r8 c_r", "c_vsel", 7.0, A.add)
+    ts(T.maskv[:], T.l32[:], cl["vsel"], A.is_equal, "l32 c_vsel", "maskv")
+    lin(cl["rm"], cl["r"], 1.0, -15.25, "c_r", "c_rm")
+    lin(cl["k3"], cl["r"], 1.0, C - 7 - PO + 1024.0, "c_r", "c_k3")
+    lin(cl["o320"], cl["o16"], 20.0, PO, "c_o16", "c_o320")
+    lin(cl["d320"], cl["o16"], -20.0, float(C), "c_o16", "c_d320")
+    ts(cl["m7"], cl["r"], 14.0, A.is_lt, "c_r c_msend", "c_m7", cl["msend"], A.mult)
+    ts(T.dd[:], T.loc[:], cl["r1"], A.not_equal, "loc c_r1", "dd")
+    ts(f["k3"], iot[:, 0:VW:8], cl["k3"], A.add, "iot c_k3 c_m7", "k3", cl["m7"], A.mult)
+    lin(starts(T.dd), k16n, 0.0, 0.0, "iot", "c_dd dd")
+    lin(ends(T.dd), ends(T.dd), cl["d320"], 0.0, "dd c_d320", "c_dd dd")
+    lin(f["k3"], f["k3"], 1.0, -1024.0, "k3", "k3")
+    lin(T.te[:, 0:C], T.loc[:], -0.5, -0.5, "loc", "te0")
+    lin(ends(T.cs), k16n, 0.0, 1024.0, "iot", "cs")
+    lin(starts(T.dtt), k16n, 0.0, 1024.0, "iot", "c_dt dtt")
+    lin(ends(T.dtt), k16n, 1.0, float(14 - C), "iot", "c_dt dtt")
+    lin(T.em[:, 0:16], iot[:, 0:16], 0.0, -1.0, "iot", "emp")
+    quant(T.qv[:], T.sv[:], T.vt0[:], "vt0", "qv")
+
+    def plane(b):
+        return T.win[:, WW * b:WW * b + C]
+
+    def unpacker(b):
+        return T.qe[:, 128 * b:128 * b + 128], T.se[:, 128 * b:128 * b + 128]
+
+    sent = [0]
+
+    def remote(out, a, sem, peer, rd, late):
+        rid, pid = topo.addr(peer, core)
+        mask = topo.mask(core, peer)
+        sent[0] += len(topo.engines(core, peer))
+
+        def call():
+            g.remote_dma(out, a, T.sem[sem], T.sem.sent, pid, rid, mask)
+        op("g", call, rd, "r%s_%d" % (sem, late), None, late)
+
+    for rnd in range(3):
+        peer = T.cores[rank ^ MASKS[rnd]]
+        ne = len(topo.engines(peer, core))
+        final = rnd == 2
+        snd, lnd = T["snd%d" % rnd], T["lnd%d" % rnd]
+        qs, ss, ql, sl = T["qs%d" % rnd], T["ss%d" % rnd], T["ql%d" % rnd], T["sl%d" % rnd]
+
+        mm(ps[0][:, 0:C], T.qu[:], T.su[:], T.qx[:], T.sx[:], "qu su qx", "ps0")
+        for b in range(4):
+            mm(ps[fb[b]][:, 0:C], *unpacker(b), T.qx[:], T.sx[:], "qe%d qx" % b, "ps%d" % fb[b])
+            act(plane(b), ps[fb[b]][:, 0:C], "ps%d" % fb[b], "ps%d w%d" % (fb[b], b))
+        for b in (0, 1):
+            act(T.fo[:, C * b:C * b + C], plane(b), "w%d" % b, "fo%d" % b)
+        act(T.ssb[:], ps[0][:, 0:C], "ps0", "ps0 ssb")
+
+        act(T.ma[:], by(T.tm[:], u["m2u"]), "tm m2u", "ma")
+        act(T.mc[:], T.ma[:], "ma", "mc")
+        turn(T.lb, "lb")
+        nat(T.j2u, "j2u")
+        act(mid(T.la), by(mid(T.lb), j2), "lb j2u", "la")
+        tt(T.mb[:], by(T.ma[:], j2), T.mc[:], A.max, "ma mc j2u", "mb")
+        act(T.mc[:], T.mb[:], "mb", "mc")
+        turn(T.la, "la")
+        nat(T.j4u, "j4u")
+        act(mid(T.lb), by(mid(T.la), j4), "la j4u", "lb")
+        tt(T.ma[:], by(T.mb[:], j4), T.mc[:], A.max, "mb mc j4u", "ma")
+        act(T.mc[:], T.ma[:], "ma", "mc")
+        turn(T.lb, "lb")
+        nat(T.j8u, "j8u")
+        tt(T.mb[:], by(T.ma[:], j8), T.mc[:], A.max, "ma mc j8u", "mb")
+        seg(T.sc2[:], T.mb[:], A.add, "mb", "sc2")
+        lin(f["szn"], ends(T.sc2), 0.5, 8.0, "sc2", "szn")
+        lin(f["csz"], ends(T.sc2), -0.5, 8.0, "sc2", "csz")
+        lin(f["dla"], n7, -16.0, 0.0, "n7", "dla")
+        lin(T.lk[:, 0:TR], n7, 16.0, cl["r16"], "n7 c_r16", "lka")
+
+        tt(mid(T.sn), by(T.ssb[:], u["nodu"]), T.sig[:], A.mult, "ssb nodu sig", "sn")
+        act(T.neg[:], mid(T.sn), "sn", "neg", -1.0)
+        op("v", lambda: V.transpose(T.tt[:, 0:C], mid(T.sn)), "sn", "tt0")
+        op("v", lambda: V.transpose(T.tt[:, C:2 * C + 32], T.sn[:]), "sn c_psn c_qsn", "tt1")
+        tt(T.cmp[:], by(T.tt[:], T.tsel[:]), T.neg[:], A.is_gt, "tt0 tt1 tsel0 tsel1 neg", "cmp")
+        scan(T.scs[:], T.d0s[:], T.cmp[:], A.mult, A.add, "d0s cmp", "scs")
+        ts(u["stu"], ends(T.scs), cl["r"], A.add, "scs c_r", "stu")
+        ts(u["sou"], ends(T.scs), cl["r17"], A.add, "scs c_r17", "sou")
+        act(T.strep[:], by(T.iob[:, 0:16], u["stu"]), "iob stu", "strep")
+        act(mid(T.la), by(T.strep[:], j1), "strep j1u", "la")
+        lin(f["st16"], ends(T.scs), 16.0, cl["r16"], "scs c_r16", "st16")
+        turn(T.la, "la")
+        ts(T.lk[:, TR:TR + 32], by(T.tb[:], T.tsn[:]), 16.0, A.mult, "tb0 tb1 tsn", "lkb")
+        tt(f["dlb"], f["st16"], T.lk[:, TR:2 * TR], A.subtract, "st16 lkb", "dlb")
+
+        tt(T.xx[:], by(T.t16[:], u["stu"]), T.mb[:], A.mult, "t16 stu mb", "xx")
+        seg(T.sc1[:], T.xx[:], A.max, "xx", "sc1")
+        seg(T.b1[:], T.xx[:], A.min, "xx", "b1")
+        act(T.b4[:], by(T.to[:], u["sou"]), "to sou", "b4", 0.0625)
+        for k in ("fa", "fb"):
+            lin(f[k], ends(T.sc1), 1.0, -255.0, "sc1", k, AF.Relu)
+        tt(f["n1"], ends(T.sc1), f["szn"], A.add, "sc1 szn", "n1")
+        tt(f["n2"], f["csz"], ends(T.b1), A.subtract, "b1 csz", "n2")
+        tt(starts(T.ks), f["n1"], f["n2"], A.min, "n1 n2", "ks")
+        seg(T.kb[:], T.ks[:], A.add, "ks", "kb")
+        ts(u["keyu"], starts(T.ks), 0.0, A.add, "ks", "keyu")
+        tt(T.cmp[:], by(T.iob[:], u["keyu"]), T.kb[:], A.is_lt, "iob keyu kb", "cmp")
+        lin(starts(T.ks), ends(T.scs), 0.5, cl["rh"], "scs c_rh", "ks")
+        seg(T.sc1[:], T.cmp[:], A.add, "cmp", "sc1 vca vcb")
+        tt(f2["pa"], f2["fa"], f2["dla"], A.mult, "fa fb dla dlb", "pa")
+        tt(f2["qa"], f2["pa"], T.lk[:, 0:2 * TR], A.add, "pa lka lkb", "qa")
+        tt(f["na"], ends(T.sc1), f["qb"], A.add, "sc1 qa", "na")
+        cp(T.idxw[:], f["na"], "na", "idxw")
+        act(T.cmp[:, 0:H], by(T.tw[:], T.idxw[:, 0:TR // 2]), "tw idxw cmp", "vca")
+        cp(T.cmp[:, H:C], by(T.tw[:], T.idxw[:, TR // 2:TR]), "tw idxw cmp", "vcb")
+        place(T.sc2[:], T.cmp[:], "vca vcb cmp", "sc2")
+        ts(snd[:], ends(T.sc2), cl["msend"], A.mult, "sc2 c_msend", "snd%d" % rnd)
+        remote(lnd[:], snd[:], "aw%d" % rnd, peer, "snd%d" % rnd, FAR)
+
+        tt(f["n1"], ends(T.sc1), f["qa"], A.add, "sc1 qa", "n1")
+        cp(u["idxp"], f["n1"], "n1", "idxp")
+        act(T.xx[:], by(T.tj[:], u["idxp"]), "tj idxp", "xx")
+        place(T.b2[:], T.b4[:], "b4", "b2 vb2a vb2b")
+        seg(T.stb[:], T.ks[:], A.add, "ks", "stb")
+        ts(u["ou"], ends(T.b2), PO, A.add, "b2 vb2a", "ou")
+        lin(T.stb[:, 14:C:16], k16n, 0.0, 7.25, "iot", "c_stb stb")
+        place(T.b1[:], T.xx[:], "xx", "b1")
+        ts(u["pnu"], ends(T.b1), PO, A.add, "b1", "pnu")
+        tt(T.b1[:], by(T.nodrep[:], u["pnu"]), T.maskv[:], A.mult, "nodrep pnu maskv", "b1")
+        act(T.srcw[:, 0:C], by(T.nodrep[:], u["ou"]), "nodrep ou", "srcw")
+        scan(T.kb[:], T.keep32[:], T.b1[:], A.mult, A.add, "keep32 b1", "kb")
+        ts(T.vu[:], T.kb[:, 31:C:32], SO, A.add, "kb", "vu")
+        for b in (2, 3):
+            act(T.vt[:, b:4 * VW:4], by(plane(b), T.vu[:]), "w%d vu" % b, "v%d" % b, 2.0)
+        for b in (0, 1):
+            ts(T.vt[:, b:4 * VW:4], by(plane(b), T.vu[:]), 2.0, A.mult, "w%d vu" % b, "v%d" % b)
+        lin(f["own"], ends(T.sc2), cl["mown"], 0.0, "sc2 c_mown", "own")
+        lin(f["stm"], ends(T.scs), 1.0, cl["rm"], "scs c_rm", "stm")
+        act(T.osrep[:], by(T.loc[:] if final else T.iom[:], u["ou"]), "iom ou", "osrep")
+        quant(qs[:], ss[:], T.vt[:], "v0 v1 v2 v3", "qs%d" % rnd)
+        remote(ql[:].bitcast(dt.uint8), qs[:].bitcast(dt.uint8), "av%d" % rnd, peer, "qs%d" % rnd, FAR + 1000)
+        remote(sl[:], ss[:], "av%d" % rnd, peer, "qs%d" % rnd, FAR + 300)
+
+        op(None, None, "raw%d_%d" % (rnd, FAR), "lnd", ("aw%d" % rnd, ne))
+        op(None, None, "rav%d_%d rav%d_%d" % (rnd, FAR + 300, rnd, FAR + 1000), "ql", ("av%d" % rnd, 2 * ne))
+        cg = starts(T.cs)
+        tt(cg, f["own"], lnd[:], A.add, "own lnd", "cs")
+        seg(T.kb[:], T.cs[:], A.add, "cs", "kb")
+        ts(u["cgu"], cg, PO, A.add, "cs", "cgu")
+        tt(f["o2f"], cg, f["k3"], A.max, "cs k3", "o2f")
+        tt(T.cmp[:], by(T.iom[:], u["cgu"]), T.kb[:], A.is_equal, "iom cgu kb", "cmp")
+        act(T.lnkj[:], by(T.osrep[:], u["cgu"]), "osrep cgu", "lnkj")
+        if not final:
+            act(ends(T.lnkj), ends(T.osrep), "osrep", "c_lnk lnkj")
+        ts(u["o2u"], f["o2f"], PO, A.add, "o2f", "o2u")
+        scan(T.sc1[:], T.dd[:], T.cmp[:], A.mult, A.max, "dd cmp", "sc1")
+        tt(f["n1"], ends(T.sc1), cg, A.add, "sc1 cs", "n1")
+        ts(u["idxu"], f["n1"], cl["o320"], A.add, "n1 c_o320", "idxu")
+        act(T.srcj[:], by(T.srcw[:], u["o2u"]), "srcw srcwc o2u", "srcj")
+        for b in range(4):
+            mm(ps[ub[b]][:, 0:VW], *unpacker(b), ql[:], sl[:], "qe%d ql" % b, "ps%d" % ub[b])
+            act(T.win[:, WW * b + C:WW * b + WW], ps[ub[b]][:, 0:VW], "ps%d" % ub[b], "ps%d u%d" % (ub[b], b))
+        tt(T.xx[:], by(T.te[:], u["idxu"]), T.stb[:], A.add, "te0 te1 idxu stb", "xx")
+        ts(mid(T.em), T.xx[:], -1.0, A.max, "xx", "em", 0.0, A.min)
+        seg(T.sc1[:], mid(T.em), A.add, "em", "sc1")
+        tt(starts(T.ks), f["stm"], ends(T.sc1), A.subtract, "stm sc1", "ks")
+        scan(T.yy[:], T.ks[:], T.em[:, 15:C + 15], A.max, A.add, "ks em emp", "yy")
+        ts(T.cmp[:], T.yy[:], -0.5, A.not_equal, "yy", "cmp", 15.0, A.mult)
+        scan(T.f1[:], T.dtt[:], T.cmp[:], A.add, A.min, "dtt cmp", "f1")
+        ts(T.tu[:], ends(T.f1), float(C), A.add, "f1", "tu")
+        act(T.b2[:, 0:H], by(T.srcj[:], T.tu[:, 0:TR // 2]), "srcj tu", "vb2a")
+        cp(T.b2[:, H:C], by(T.srcj[:], T.tu[:, TR // 2:TR]), "srcj tu", "vb2b b2")
+        act(T.oprep[:] if final else mid(T.la), by(T.lnkj[:], T.tu[:]), "lnkj tu", "opr" if final else "la")
+        tt(T.b1[:], by(T.b2[:], T.invu[:]), T.diag[:], A.mult, "vb2a vb2b invu diag", "b1")
+        seg(T.kb[:], T.b1[:], A.add, "b1", "kb")
+        ts(u["eu"], ends(T.kb), SO, A.add, "kb", "eu")
+
+        def whole(b):
+            return by(T.win[:, WW * b:WW * b + WW], u["eu"])
+        for b in (3, 2):
+            act(T.hh[:, C * (b - 2):C * (b - 1)], whole(b), "w%d u%d eu" % (b, b), "h%d" % b)
+        for b in (0, 1):
+            tt(T.zt[:, b:4 * C:4], whole(b), T.fo[:, C * b:C * b + C], A.add, "w%d u%d eu fo%d" % (b, b, b), "z%d" % b)
+        for b in (3, 2):
+            tt(T.zt[:, b:4 * C:4], T.hh[:, C * (b - 2):C * (b - 1)], ps[fb[b]][:, 0:C], A.add,
+               "h%d ps%d" % (b, fb[b]), "z%d ps%d" % (b, fb[b]))
+        for b in range(4):
+            act(T.z32[:, C * b:C * b + C], T.zt[:, b:4 * C:4], "z%d" % b, "zz%d" % b, 32.0)
+        quant(T.qz[:], T.sz[:], T.zt[:], "z0 z1 z2 z3", "qz")
+        for b in range(4):
+            mm(ps[fb[b]][:, 0:C], T.wq[:, 128 * b:128 * b + 128], T.wsb[:, 128 * b:128 * b + 128], T.qz[:], T.sz[:],
+               "wq wsb qz", "ps%d" % fb[b])
+        if final:
+            dma("y", T.op[:], T.oprep[0:128:16, :], "opr", "", "dop")
+        else:
+            turn(T.la, "la")
+            nat(T.j1u, "j1u")
+            tt(T.n7[:], by(T.tb[:], T.tsn[:]), T.k64[:], A.subtract, "tb0 tb1 tsn k64", "n7")
+            act(mid(T.lb), by(mid(T.la), j1), "la j1u", "lb")
+            pair_index()
+        for b in range(4):
+            tt(T.x32[:, C * b:C * b + C], ps[fb[b]][:, 0:C], T.z32[:, C * b:C * b + C], A.add,
+               "zz%d ps%d" % (b, fb[b]), "xx%d ps%d" % (b, fb[b]))
+            if b < 3:
+                act(T.xt[:, b:4 * C:4], T.x32[:, C * b:C * b + C], "xx%d" % b, "x%d" % b, 0.03125)
+        ts(T.xt[:, 3:4 * C:4], T.x32[:, 3 * C:4 * C], 0.03125, A.mult, "xx3", "x3")
+        quant(T.qx[:], T.sx[:], T.xt[:], "x0 x1 x2 x3", "qx")
+
+    mm(ps[0][:, 0:C], T.qv[:], T.sv[:], T.qx[:], T.sx[:], "qv qx", "ps0")
+    dma("y", T.oc[:], T.qx[:].bitcast(dt.uint8), "qx", "", "doc", 16, 1000)
+    act(T.ysb[:], ps[0][:, 0:C], "ps0", "ps0 ysb")
+    dma("s", T.y[:], T.ysb[:], "ysb", "", "dy", 16, 1000)
+    for k in range(4):
+        dma("y", T.osc[4 * k:4 * k + 4, :], T.sx[32 * k:32 * k + 4, :], "qx", "", "dos", 64)
+    _emit(g, T, _order(ops))
+    for s, n in (("dop", 16), ("doc", 16), ("dos", 64)):
+        g.sync.wait_ge(T.sem[s], n)
+    g.scalar.wait_ge(T.sem.dy, 16)
+    g.wait_ge(T.sem.sent, sent[0])

@@ -9,6 +9,7 @@ H = C // 2
 PO, SO = 64.0, 224.0
 MASKS = [1, 2, 4]
 Q4, U8, BF, F32, I32, U16 = "float8_e4m3fn_x4", "uint8", "bfloat16", "float32", "int32", "uint16"
+OPT = {"sigc": True, "cap": False, "tries": 240}
 
 SCRATCH = {}
 
@@ -18,583 +19,623 @@ def _decl(dtype, **kw):
         SCRATCH[k] = ("sbuf", [128, n], dtype)
 
 
-NF = "self k3 j0f j1f n1 n2 fa fb dla dlb pa pb qa qb szn csz stm own o2f st16 na".split()
-NU = "nodu j0u m2u stu sou keyu idxu pnu ou cgu o2u eu idxp".split()
 _decl(Q4, qx=C, qz=C, qu0=128, qu=128, qv=128, wq=512, qe=512)
 _decl(U8, sx=C, sz=C, su0=128, su=128, sv=128, wsb=512, se=512)
 for _r in range(3):
     _decl(Q4, **{"qs%d" % _r: VW, "ql%d" % _r: VW})
     _decl(U8, **{"ss%d" % _r: VW, "sl%d" % _r: VW})
-    _decl(BF, **{"snd%d" % _r: TR, "lnd%d" % _r: TR})
-_decl(BF, xt=4 * C, zt=4 * C, z32=4 * C, x32=4 * C, ut=512, vt0=512, ebuf=528, win=4 * WW, vt=4 * VW, hh=2 * C,
-      loc=C, k16r=C, k64r=C, iob=256, iom=C, ios=C, l32=C, diag=C, sig=C, keep=C, keep32=C, d0s=C, dd=C,
-      maskv=C, tj=256, tw=256, to=256, tm=256, te=2 * C, t16=16, ma=C, mb=C, mc=C, fo=2 * C, cmp=C, sc1=C, sc2=C,
-      scs=C, xx=C, ks=C, cs=C, kb=C, strep=C, stb=C, em=C + 16, yy=C, b1=C, b2=C, b3=C, b4=C, nodrep=C, osrep=C,
-      srcw=WW, lnkj=C, srcj=C, la=C + 32, lb=C + 32, tb=2 * C + 32)
-_decl(F32, iot=512, dtt=C, ssb=C, sn=C + 32, tt=2 * C + 32, neg=C, f1=C, ysb=C, oprep=C, col=32, k64=32, n7=32,
-      lk=TR + 32, nf=TR * len(NF))
+    _decl(BF, **{n % _r: TR for n in ("sa%d", "la%d", "sb%d", "lb%d")})
+_decl(BF, xt=4 * C, zt=4 * C, z32=4 * C, x32=4 * C, ut=512, vt0=512, ebuf=528, win=4 * WW, vt=4 * VW, hh=2 * C, fo=2 * C)
 _decl(I32, pi=2, ri=2, nodi=TR, pari=TR)
-_decl(U16, invu=TR, tsel=TR, tsn=2, upk=8, j1u=32, j2u=32, j4u=32, j8u=32, vu=10, tu=TR, idxw=TR, nu=TR * len(NU))
+_decl(BF, pb=28672)
+_decl(F32, pf=4096)
+_decl(U16, pu=1024)
 for _b in range(8):
     SCRATCH["ps%d" % _b] = ("psum", [128, 512], F32)
 
-_DMAS = ["dx", "du", "dw", "dws", "dv", "dpar", "dnod", "dop", "doc", "dos", "dy"]
-SEMAPHORES = ["cv", "cs", "ct", "cg", "sent"] + _DMAS + ["aw0", "aw1", "aw2", "av0", "av1", "av2"]
+_DMAS = ["dx", "du", "dw", "dws", "dv", "dpar", "dnod", "dop", "doc", "dos", "dy0", "dy1"]
+SEMAPHORES = ["cv", "cs", "ct", "cg", "sent"] + _DMAS + [n + str(r) for n in ("aa", "ab", "av") for r in range(3)]
 
-SMALL = set(NF + NU + "invu tsel0 tsel1 tsn upk vu tu idxw k64 lka ri0 ri1 pi ks cs t16 emp snd0 snd1 snd2".split())
-LONG = {"qx": 400, "qz": 400, "qs0": 220, "qs1": 220, "qs2": 220, "f1": 360, "tt0": 360, "tt1": 400, "b3": 1300,
-        "qu": 290, "su": 290, "n7": 130, "lkb": 130, "tw": 160, "j1u": 130, "j2u": 130, "j4u": 130, "j8u": 130,
-        "tm": 250, "to": 300, "tj": 250, "iot": 1200, "ebuf": 1200, "iob": 700, "srcwc": 500}
-HOP, FAR, LOAD, TRIES, CHOSEN = 70, 2400, 2000, 500, []
+TUNES = ((1.0, 70, 1800, 1700), (0.75, 120, 1500, 1500), (1.25, 60, 2400, 2000), (1.0, 160, 1800, 1700))
+CHOSEN = []
 
 
-def _length(q, rd, wr, picked):
-    k = wr[0] if wr else ""
-    if q == "t":
-        return 250
-    if q == "g":
-        return 150 if k == "pi" else LONG.get(k, 850) if k[:1] != "r" else 300
-    if k in LONG:
-        return LONG[k]
-    if picked:
-        return 340 if k[0] == "v" else 600
-    if k in SMALL or k[:2] == "c_":
-        return 100
-    if q == "s":
-        return 200 if len(wr) > 1 and wr[1][0] == "u" else 360
-    return 360 if any(r[:2] == "ps" for r in rd) else 200
+def _n(v):
+    return 16 * _n(v[2]) if v[0] == "by" else len(range(v[1], v[2], v[3]))
 
 
-def _order(ops):
-    if CHOSEN:
-        return [ops[n][:5] for n in CHOSEN]
-    last, readers, deps, users = {}, {}, [], [[] for o in ops]
+def _bits(v):
+    if v[0][:2] == "ps":
+        return 1
+    if v[3] == 1:
+        return ((1 << (v[2] - v[1])) - 1) << v[1]
+    return sum(1 << c for c in range(v[1], v[2], v[3]))
+
+
+def _needs(ops):
+    seen, deps = {}, []
     for n, o in enumerate(ops):
-        d = set(last[k] for k in o[2] + o[3] if k in last)
-        for k in o[3]:
-            d.update(readers.get(k, []))
+        d = set()
+        for views, wr in ((o["rd"], False), (o["wr"], True)):
+            for v in views:
+                m, w = _bits(v), wr or v[0][:2] == "ps"
+                l = seen.setdefault(v[0], [])
+                d.update(e[0] for e in l if e[1] & m and (w or e[2]))
+                if w:
+                    l[:] = [(e[0], e[1] & ~m, e[2]) for e in l if e[1] & ~m]
+                l.append((n, m, w))
         d.discard(n)
         deps.append(d)
+    return deps
+
+
+def _order(ops, deps):
+    if CHOSEN:
+        return CHOSEN
+    users = [[] for o in ops]
+    for n, d in enumerate(deps):
         for m in d:
             users[m].append(n)
-        for k in o[2]:
-            readers.setdefault(k, []).append(n)
-        for k in o[3]:
-            last[k] = n
-            readers[k] = []
 
-    def replay(order, pick, hop, far):
-        done, free = {}, {}
-        for n in order:
-            q, c, late = ops[n][0], ops[n][5] * (pick if ops[n][7] else 1.0), ops[n][6] * far
+    def lengths(pick, hop, far, load):
+        cost = [{q: c[1] * (pick if o["pick"] else 1.0) for q, c in o["q"].items()} for o in ops]
+        late = [o["late"] + (far if o["kind"] == "far" else load if o["kind"] == "dma" else 0) for o in ops]
+        return cost, late, hop
+
+    tunes = [lengths(*k) for k in TUNES]
+
+    def replay(order, cost, late, hop):
+        done, free = [0] * len(ops), {}
+        for n, q in order:
             t = max([free.get(q, 0)] + [done[m] + hop for m in deps[n]])
-            if q is not None:
-                free[q] = t + c
-            done[n] = t + c + late
-        return max(done.values())
+            free[q] = t + cost[n][q]
+            done[n] = free[q] + late[n]
+        return max(done)
 
     rng, best = np.random.RandomState(1), None
-    for attempt in range(TRIES):
-        shake = 1.0 + (0.5 if attempt else 0.0) * (rng.rand(len(ops)) - 0.5)
-        slack = (0, 60, 150)[attempt % 3]
+    for attempt in range(OPT["tries"]):
+        cost, late, hop = tunes[attempt % 2 * 3]
+        shake = 1.0 + (0.4 if attempt else 0.0) * (rng.rand(len(ops)) - 0.5)
+        slack, spare = (0, 60, 150)[attempt % 3], 3.0 * rng.rand()
         way = [0] * len(ops)
         for n in range(len(ops) - 1, -1, -1):
-            way[n] = (ops[n][5] + ops[n][6]) * shake[n] + max([way[m] + HOP for m in users[n]] + [0])
+            way[n] = (min(cost[n].values()) + late[n]) * shake[n] + max([way[m] + hop for m in users[n]] + [0])
         left = [len(d) for d in deps]
         at, free, out = [0] * len(ops), {}, []
         ready = [n for n in range(len(ops)) if not left[n]]
         while ready:
-            start = {n: max(at[n], free.get(ops[n][0], 0)) for n in ready}
-            a = min(ready, key=lambda n: (start[n], -way[n]))
-            n = max((m for m in ready if ops[m][0] == ops[a][0] and start[m] <= start[a] + slack), key=lambda m: way[m])
+            start = {}
+            for n in ready:
+                q = min(cost[n], key=lambda q: max(at[n], free.get(q, 0)) + cost[n][q] * (1.0 + (spare if q == "v" else 0.0)))
+                start[n] = (max(at[n], free.get(q, 0)), q)
+            a = min(ready, key=lambda n: (start[n][0], -way[n]))
+            t, q = start[a]
+            n = max((m for m in ready if q in cost[m] and (start[m][1] == q or m == a) and start[m][0] <= t + slack),
+                    key=lambda m: way[m])
             ready.remove(n)
-            out.append(n)
-            if ops[n][0] is not None:
-                free[ops[n][0]] = start[n] + ops[n][5]
+            out.append((n, q))
+            free[q] = start[n][0] + cost[n][q]
             for m in users[n]:
-                at[m] = max(at[m], start[n] + ops[n][5] + ops[n][6] + HOP)
+                at[m] = max(at[m], free[q] + late[n] + hop)
                 left[m] -= 1
                 if not left[m]:
                     ready.append(m)
-        end = sum(replay(out, *k) for k in ((1.0, HOP, 1.0), (0.75, HOP, 1.3), (1.25, 2 * HOP, 0.7), (1.0, 2 * HOP, 1.4)))
+        end = sum(replay(out, *k) for k in tunes)
         if best is None or end < best[0]:
             best = (end, out)
     CHOSEN.extend(best[1])
-    return [ops[n][:5] for n in CHOSEN]
+    return CHOSEN
 
 
-def _emit(g, T, ops):
+def _emit(g, T, ops, deps, order):
     qs = {"v": g.vector, "s": g.scalar, "t": g.tensor, "g": g, "y": g.sync}
-    last, readers, known, clock, waits, needed, pos = {}, {}, {q: {} for q in qs}, [], [], set(), {}
-    src = []
-    for n, (q, fn, rd, wr, sem) in enumerate(ops):
-        if sem is None:
-            pos[q] = pos.get(q, 0) + 1
-            src.append((q, pos[q]))
-        else:
-            src.append((sem[0], 1))
-        if q is None:
-            clock.append({sem[0]: 1})
-            waits.append([])
-            for k in wr:
-                last[k] = n
-                readers[k] = []
+    known, clock, waits, needed, pos, src, place = {q: {} for q in qs}, {}, {}, set(), {}, {}, {}
+    for i, (n, q) in enumerate(order):
+        place[n] = i
+        sem = ops[n]["sem"]
+        pos[q] = pos.get(q, 0) + (sem is None)
+        src[n] = (q, pos[q]) if sem is None else (sem[0], 1)
+        if q not in qs:
+            clock[n] = {sem[0]: 1}
             continue
-        deps = set()
-        for k in rd:
-            if k in last:
-                deps.add(last[k])
-        for k in wr:
-            if k in last:
-                deps.add(last[k])
-            deps.update(readers.get(k, []))
-        w = []
-        for d in sorted(deps, reverse=True):
-            s, lev = src[d]
-            if known[q].get(s, 0) >= lev:
+        waits[n] = []
+        for d in sorted(deps[n], key=lambda d: -place[d]):
+            if known[q].get(src[d][0], 0) >= src[d][1]:
                 continue
-            w.append(d)
+            waits[n].append(d)
             needed.add(d)
             for k, v in clock[d].items():
-                if known[q].get(k, 0) < v:
-                    known[q][k] = v
-        waits.append(w)
-        ck = dict(known[q])
-        ck[src[n][0]] = src[n][1]
-        clock.append(ck)
-        for k in rd:
-            readers.setdefault(k, []).append(n)
-        for k in wr:
-            last[k] = n
-            readers[k] = []
+                known[q][k] = max(known[q].get(k, 0), v)
+        clock[n] = dict(known[q])
+        clock[n][src[n][0]] = src[n][1]
     count, value = {}, {}
-    for n, (q, fn, rd, wr, sem) in enumerate(ops):
-        if sem is None:
-            if n in needed:
-                count[q] = count.get(q, 0) + 1
-                value[n] = ("c" + q, count[q])
-        else:
-            value[n] = sem
-    for n, (q, fn, rd, wr, sem) in enumerate(ops):
-        if q is None:
+    for n, q in order:
+        value[n] = ops[n]["sem"]
+        if value[n] is None and n in needed:
+            count[q] = count.get(q, 0) + 1
+            value[n] = ("c" + q, count[q])
+    for n, q in order:
+        if q not in qs:
             continue
         for d in waits[n]:
             qs[q].wait_ge(T.sem[value[d][0]], value[d][1])
-        ins = fn()
-        if ins is None:
-            continue
-        if sem is None:
-            if n in needed:
-                ins.then_inc(T.sem["c" + q], 1)
-        else:
-            ins.then_inc(T.sem[sem[0]], 16)
+        ins = ops[n]["q"][q][0]()
+        if ins is not None and value[n] is not None:
+            ins.then_inc(T.sem[value[n][0]], 1 if ops[n]["sem"] is None else 16)
 
 
 def rank_program(g, core, T, topo):
     rank = T.rank_of(core)
     if rank is None:
         return
-    ops, picked = [], [False]
+    ops, used = [], {"pb": 0, "pf": 0, "pu": 0}
     V, S = g.vector, g.scalar
 
-    def op(q, fn, rd, wr, sem=None, late=0):
-        rd, wr = rd.split(), wr.split()
-        if q is None:
-            ops.append((q, fn, rd, wr, sem, 0, 0, False))
-        elif sem is not None:
-            ops.append((q, fn, rd, wr, sem, 80, LOAD + late, False))
-        else:
-            ops.append((q, fn, rd, wr, sem, _length(q, rd, wr, picked[0]), late, picked[0]))
-        picked[0] = False
+    def new(pool, n):
+        used[pool] += (n + 15) // 16 * 16
+        assert used[pool] <= SCRATCH[pool][1][1]
+        return (pool, used[pool] - (n + 15) // 16 * 16, used[pool] - (n + 15) // 16 * 16 + n, 1)
 
-    def ts(out, in0, s1, o0, rd, wr, s2=None, o1=None):
-        if o1 is None:
-            op("v", lambda: V.tensor_scalar(out, in0, s1, None, o0), rd, wr)
-        else:
-            op("v", lambda: V.tensor_scalar(out, in0, s1, s2, o0, o1), rd, wr)
+    def news(pool, n, names):
+        return [new(pool, n) for k in names.split()]
 
-    def tt(out, a, b, o, rd, wr):
-        op("v", lambda: V.tensor_tensor(out, a, b, o), rd, wr)
+    def whole(name):
+        return (name, 0, SCRATCH[name][1][1], 1)
 
-    def cp(out, a, rd, wr):
-        op("v", lambda: V.tensor_copy(out, a), rd, wr)
+    def cut(v, a, b, step=1):
+        return (v[0], v[1] + a, v[1] + b, step)
 
-    def scan(out, d0, d1, o0, o1, rd, wr, ini=0.0):
-        op("v", lambda: V.tensor_tensor_scan(out, d0, d1, ini, o0, o1), rd, wr)
+    def ends(v):
+        return cut(v, 15, _n(v), 16)
 
-    def seg(out, a, o, rd, wr):
-        scan(out, T.keep[:], a, A.mult, o, rd + " keep", wr)
+    def starts(v):
+        return cut(v, 0, _n(v), 16)
 
-    def place(out, a, rd, wr):
-        scan(out, T.k64r[:], a, A.max, A.add, rd + " k64r", wr, -PO)
+    def by(win, off):
+        return ("by", win, off)
 
-    def mset(out, c, wr):
-        op("v", lambda: V.memset(out, c), "", wr)
+    def ap(v):
+        if not isinstance(v, tuple):
+            return v
+        if v[0] == "by":
+            return ap(v[1]).indirect(ap(v[2]))
+        return T[v[0]][:, v[1]:v[2]:v[3]] if v[3] > 1 else T[v[0]][:, v[1]:v[2]]
 
-    def act(out, a, rd, wr, scale=1.0):
-        op("s", lambda: S.activation(out, a, AF.Copy, scale=scale), rd, wr)
+    def flat(views):
+        out = []
+        for v in views:
+            if isinstance(v, tuple):
+                out.extend(v[1:] if v[0] == "by" else [v])
+        return out
 
-    def lin(out, a, scale, bias, rd, wr, fn=AF.Identity):
-        op("s", lambda: S.activation(out, a, fn, bias=bias, scale=scale), rd, wr)
+    def op(q, rd, wr, kind="", late=0, sem=None):
+        pick = any(isinstance(v, tuple) and v[0] == "by" for v in rd + wr)
+        ops.append({"q": q, "rd": flat(rd), "wr": flat(wr), "kind": kind, "late": late, "sem": sem, "pick": pick})
 
-    def quant(q, s, a, rd, wr):
-        op("v", lambda: V.quantize_mx(q, s, a), rd, wr)
+    def length(out, ins, base, rate=None):
+        n = _n(out)
+        if out[0] == "by":
+            return base + 3.2 * n
+        if ins[0][0] == "by":
+            return base + 1.3 * n
+        if rate is None:
+            rate = 0.5 if all(SCRATCH[v[0]][2] in (BF, U16) for v in ins + [out]) else 1.0
+        return 0.83 * max(64, n * rate)
 
-    def mm(out, lq, ls, rq, rs, rd, wr):
-        op("t", lambda: g.tensor.matmul_mx(out, lq, ls, rq, rs, True, True), rd, wr, None, 100)
+    def ts(out, a, s1, o0, s2=None, o1=None):
+        more = (o0,) if o1 is None else (o0, o1)
+        op({"v": (lambda: V.tensor_scalar(ap(out), ap(a), ap(s1), ap(s2), *more), length(out, [a], 50))}, [a, s1, s2], [out])
 
-    def iota(out, pat, base, mul, wr, flt=True):
-        if flt:
-            op("g", lambda: g.iota(out, pat, base, mul, allow_small_or_imprecise_dtypes=True), "", wr)
-        else:
-            op("g", lambda: g.iota(out, pat, base, mul), "", wr)
+    def tt(out, a, b, o):
+        rate = 1.0 if "ps" in (a[0][:2], b[0][:2]) or SCRATCH[out[0]][2] == BF == SCRATCH[b[0]][2] else 2.0
+        op({"v": (lambda: V.tensor_tensor(ap(out), ap(a), ap(b), o), length(out, [a, b], 50, rate))}, [a, b], [out])
+
+    def cp(out, a):
+        op({"v": (lambda: V.tensor_copy(ap(out), ap(a)), length(out, [a], 50))}, [a], [out])
+
+    def scan(out, d0, d1, o0, o1, ini=0.0):
+        op({"v": (lambda: V.tensor_tensor_scan(ap(out), ap(d0), ap(d1), ini, o0, o1), length(out, [d0, d1], 50))}, [d0, d1], [out])
+
+    def turn(out, a):
+        op({"v": (lambda: V.transpose(ap(out), ap(a)), length(out, [a], 50))}, [a], [out])
+
+    def mset(out, c):
+        op({"v": (lambda: V.memset(ap(out), c), length(out, [out], 50))}, [], [out])
+
+    def act(out, a, fn, scale=1.0, bias=0.0):
+        op({"s": (lambda: S.activation(ap(out), ap(a), fn, bias=ap(bias), scale=ap(scale)), length(out, [a], 65, 1.0))},
+           [a, scale, bias], [out])
+
+    def lin(out, a, scale=1.0, bias=0.0):
+        plain = bias == 0.0
+
+        def vec():
+            if plain:
+                return V.tensor_copy(ap(out), ap(a)) if scale == 1.0 else V.tensor_scalar(ap(out), ap(a), ap(scale), None, A.mult)
+            return V.tensor_scalar(ap(out), ap(a), ap(scale), ap(bias), A.mult, A.add)
+
+        def sca():
+            if plain and not isinstance(scale, tuple):
+                return S.activation(ap(out), ap(a), AF.Copy, scale=scale)
+            return S.activation(ap(out), ap(a), AF.Identity, bias=ap(bias), scale=ap(scale))
+        op({"v": (vec, length(out, [a], 50)), "s": (sca, length(out, [a], 65, 1.0))}, [a, scale, bias], [out])
+
+    def pick(out, win, off, scale=1.0, bias=0.0, split=True, halves=False):
+        if not split and not halves:
+            return lin(out, by(win, off), scale, bias)
+        for h in (0, 1):
+            lin(cut(out, H * h, H * h + H), by(cut(win, H * h, H * h + H) if halves else win, cut(off, 10 * h, 10 * h + 10)), scale, bias)
+
+    def quant(q, s, a):
+        op({"v": (lambda: V.quantize_mx(ap(q), ap(s), ap(a)), 12 + 0.22 * _n(a))}, [a], [q, s])
+
+    def mm(out, lq, ls, rq, rs):
+        op({"t": (lambda: g.tensor.matmul_mx(ap(out), ap(lq), ap(ls), ap(rq), ap(rs), True, True), 0.6 * (_n(out) + 16))},
+           [lq, ls, rq, rs], [out], "", 60)
+
+    def iota(out, pat, base, mul=0):
+        flt = {} if SCRATCH[out[0]][2] == I32 else {"allow_small_or_imprecise_dtypes": True}
+        op({"g": (lambda: g.iota(ap(out), pat, base, mul, **flt), 130 + 1.66 * _n(out))}, [], [out])
 
     def dma(q, out, a, rd, wr, sem, n=16, late=0):
         e = g.sync if q == "y" else g.scalar
-        op(q, lambda: e.dma_start(out, a), rd, wr, (sem, n), late)
-
-    def by(win, off):
-        picked[0] = True
-        return win.indirect(off)
-
-    def ends(t):
-        return t[:, 15:C:16]
-
-    def starts(t):
-        return t[:, 0:C:16]
-
-    def mid(t):
-        return t[:, 16:C + 16]
-
-    def turn(t, key):
-        op("v", lambda: V.transpose(T.tb[:, 0:C], mid(t)), key, "tb0")
-        op("v", lambda: V.transpose(T.tb[:, C:2 * C + 32], t[:]), "%s c_p%s c_q%s" % (key, key, key), "tb1")
-
-    def nat(out, key):
-        ts(out[:], by(T.tb[:], T.tsn[:]), PO, A.add, "tb0 tb1 tsn", key)
-
-    names = ["r", "nr", "r1", "want", "cap", "msend", "mown", "o16", "vsel", "m7", "k3", "te", "to", "h", "t0", "r8",
-             "r16", "r17", "rh", "rm", "u0", "u1", "o320", "d320", "t1"]
-    cl = {n: T.col[:, i:i + 1] for i, n in enumerate(names)}
-    f = {n: T.nf[:, TR * i:TR * i + TR] for i, n in enumerate(NF)}
-    f2 = {n: T.nf[:, TR * i:TR * i + 2 * TR] for i, n in enumerate(NF[:-1])}
-    u = {n: T.nu[:, TR * i:TR * i + TR] for i, n in enumerate(NU)}
-    iot, k16n = T.iot, T.iot[:, 0:C:16]
-    ps = [T["ps%d" % b] for b in range(8)]
-    fb, ub = [1, 2, 3, 4], [5, 6, 7, 1]
-    j1, j2, j4, j8 = (t[:, 0:TR] for t in (T.j1u, T.j2u, T.j4u, T.j8u))
-    n7 = T.n7[:, 0:TR]
-
-    dma("s", T.pari[:], T.par[:], "", "pari", "dpar")
-    dma("y", T.xt[:], T.x[:], "", "x0 x1 x2 x3", "dx", 16, 1500)
-    dma("s", T.nodi[:], T.nod[:], "", "nodi", "dnod")
-    dma("y", T.ut[:], T.u[:], "", "ut", "du")
-    dma("y", T.wq[:].bitcast(dt.uint8), T.wc[:], "", "wq", "dw", 16, 1500)
-    dma("y", T.wsb[:], T.ws[:], "", "wsb", "dws")
-    dma("y", T.vt0[:], T.v[:], "", "vt0", "dv")
-
-    iota(T.pi[:, 0:1], [[0, 1]], 0, 1, "pi", False)
-    iota(iot[:], [[1, 512]], 0, 0, "iot")
-    iota(T.loc[:], [[0, TR], [1, 16]], 0, 0, "loc")
-    mset(T.ebuf[:], 0.5, "ebuf0 ebuf")
-    iota(T.k16r[:], [[16, TR], [0, 16]], 0, 0, "k16r")
-    op("g", lambda: g.affine_select(T.ebuf[:], T.ebuf[:], [[1, 528]], A.is_equal, 0.0, -3, -4), "ebuf", "ebuf")
-    iota(T.ks[:], [[0, C]], 0, 0, "ks0 ks")
-    iota(T.iob[:], [[1, 256]], 0, 0, "iob")
-    iota(T.k64r[:], [[16, TR], [0, 16]], -int(PO), 0, "k64r")
-    iota(T.ios[:], [[1, C]], -int(SO), 0, "ios")
-    iota(T.l32[:], [[0, TR // 2], [1, 32]], 0, 0, "l32")
-    iota(T.srcw[:, C:WW], [[1, VW]], C - int(SO), 0, "srcwc")
-    iota(T.cs[:], [[0, C]], 0, 0, "cs0 cs")
-    iota(T.te[:, C:2 * C], [[0, C]], -64, 0, "te1")
-    iota(T.dtt[:], [[0, C]], -1, 0, "dtt")
-
-    ts(T.ri[:, 0:1], T.pi[:, 0:1], 15, A.bitwise_and, "pi", "ri0")
-    ts(T.ri[:, 1:2], T.pi[:, 0:1], 16, A.bitwise_and, "pi", "ri1")
-    for t, k in ((T.sn, "sn"), (T.la, "la"), (T.lb, "lb")):
-        mset(t[:, 0:16], 0.0, "c_p" + k)
-        mset(t[:, C + 16:C + 32], 0.0, "c_q" + k)
-    cp(cl["r"], T.ri[:, 0:1], "ri0", "c_r")
-    cp(cl["h"], T.ri[:, 1:2], "ri1", "c_h")
-    lin(cl["t0"], cl["h"], 0.0625, 0.0, "c_h", "c_t0")
-    ts(T.ri[:, 0:1], T.pi[:, 0:1], 1, A.bitwise_and, "pi", "ri0")
-    lin(cl["r16"], cl["r"], 16.0, 0.0, "c_r", "c_r16")
-    ts(cl["u0"], T.ri[:, 0:1], cl["t0"], A.not_equal, "ri0 c_t0", "c_u0", 336.0, A.mult)
-    lin(T.iom[:], iot[:, 0:C], 1.0, -PO, "iot", "iom")
-    lin(cl["nr"], cl["r"], -1.0, 0.0, "c_r", "c_nr")
-    lin(cl["te"], cl["h"], 21.0, cl["r"], "c_h c_r", "c_te")
-    lin(cl["to"], cl["h"], -21.0, cl["r"], "c_h c_r", "c_to")
-    lin(cl["r17"], cl["r"], 17.0, 0.0, "c_r", "c_r17")
-    ts(cl["u1"], cl["r16"], 48.0, A.min, "c_r16", "c_u1", 256.0, A.add)
-    ts(T.tsn[:, 0:1], cl["u0"], cl["r16"], A.add, "c_u0 c_r16", "tsn")
-    tt(f["j0f"], T.pari[:], k16n, A.add, "pari iot", "j0f")
-    ts(T.tsn[:, 1:2], cl["u0"], cl["u1"], A.add, "c_u0 c_u1 tsn", "tsn")
-    cp(u["j0u"], f["j0f"], "j0f", "j0u")
-    lin(f["self"], k16n, 1.0, cl["r"], "iot c_r", "self")
-    act(mid(T.la), by(T.iom[:], u["j0u"]), "iom j0u", "la")
-    act(mid(T.lb), by(mid(T.la), u["j0u"]), "la j0u", "lb")
-    cp(u["nodu"], T.nodi[:], "nodi", "nodu")
-    cp(T.upk[:], iot[:, 0:128:16], "iot", "upk")
-    ts(T.diag[:], T.loc[:], cl["r"], A.is_equal, "loc c_r", "diag")
-    tt(f["n1"], f["self"], f["j0f"], A.subtract, "self j0f", "n1")
-    ts(T.k64[:], iot[:, 0:512:16], cl["r"], A.add, "iot c_r", "k64", -PO, A.add)
-    lin(f["n2"], f["n1"], 1.0, 0.0, "n1", "n2", AF.Relu)
-    ts(T.tsel[:, 0:TR:2], iot[:, 0:C:32], cl["te"], A.add, "iot c_te", "tsel0")
-    ts(T.tsel[:, 1:TR:2], iot[:, 16:C:32], cl["to"], A.add, "iot c_to", "tsel1", 336.0, A.add)
-    quant(T.qx[:], T.sx[:], T.xt[:], "x0 x1 x2 x3", "qx")
-    quant(T.qu0[:], T.su0[:], T.ut[:], "ut", "qu0")
-    lin(T.sig[:], T.loc[:], 1.0, cl["nr"], "loc c_nr", "sig", AF.Sign)
-    turn(T.lb, "lb")
-    cp(T.qu[:].bitcast(dt.uint32), T.qu0[:].bitcast(dt.uint32).indirect(T.upk[:]), "qu0 upk", "qu")
-    op("s", lambda: S.activation(T.su[:], T.su0[:].indirect(T.upk[:]), AF.Copy), "qu0 upk", "su")
-    tt(T.n7[:], by(T.tb[:], T.tsn[:]), T.k64[:], A.is_equal, "tb0 tb1 tsn k64", "n7")
-    ts(T.tm[:], T.k16r[:, 0:256], cl["r16"], A.is_equal, "k16r c_r16", "tm")
-    tt(f["n1"], n7, f["n2"], A.mult, "n7 n2", "n1")
-    tt(T.tm[:], T.tm[:], T.diag[:, 0:256], A.max, "tm diag", "tm")
-    tt(f["j1f"], f["n1"], f["j0f"], A.add, "n1 j0f", "j1f")
-    lin(T.tm[:], T.tm[:], 2.0, -1.0, "tm", "tm")
-    cp(j1, f["j1f"], "j1f", "j1u")
-    tt(n7, f["j1f"], f["self"], A.subtract, "j1f self", "n7")
-    act(mid(T.la), by(T.iom[:], j1), "iom j1u", "la")
-    act(mid(T.lb), by(mid(T.la), j1), "la j1u", "lb")
-    lin(T.keep[:], T.loc[:], 1.0, 0.0, "loc", "keep", AF.Sign)
-    lin(T.d0s[:], T.diag[:], -2.0, 1.0, "diag", "d0s")
-    lin(starts(T.d0s), k16n, 0.0, 0.0, "iot", "c_d0s d0s")
-    for b in range(4):
-        quant(T.qe[:, 128 * b:128 * b + 128], T.se[:, 128 * b:128 * b + 128], T.ebuf[:, 3 - b:515 - b], "ebuf", "qe%d" % b)
-
-    def pair_index():
-        ts(u["m2u"], n7, cl["r17"], A.add, "n7 c_r17", "m2u")
-
-    pair_index()
-    cp(by(T.b3[:], u["nodu"]), T.iom[:], "iom nodu", "b3")
-    tt(T.b2[:], T.b3[:], T.diag[:], A.mult, "b3 diag", "tj0 b2 vb2a vb2b")
-    seg(T.yy[:], T.b2[:], A.add, "b2 vb2a", "yy")
-    ts(T.invu[:], ends(T.yy), PO, A.add, "yy", "invu")
-    lin(T.t16[:], iot[:, 0:16], 16.0, 16.0, "iot", "t16")
-    lin(cl["r1"], cl["r"], 1.0, 1.0, "c_r", "c_r1")
-    lin(cl["o16"], cl["r16"], 1.0, -224.0, "c_r16", "c_o16", AF.Relu)
-    lin(cl["want"], cl["o16"], -0.125, cl["r1"], "c_o16 c_r1", "c_want")
-    lin(cl["cap"], cl["o16"], -0.125, 16.0, "c_o16", "c_cap")
-    lin(cl["rh"], cl["r"], 0.5, 0.0, "c_r", "c_rh")
-    ts(T.tj[:], T.loc[:, 0:256], cl["want"], A.is_equal, "loc c_want", "tj", 0.0625, A.mult)
-    tt(T.tj[:], T.tj[:], T.k16r[:, 0:256], A.mult, "tj k16r", "tj")
-    ts(T.tw[:], T.tj[:], cl["cap"], A.min, "tj c_cap", "tw")
-    tt(T.to[:], T.diag[:, 0:256], T.k16r[:, 0:256], A.mult, "diag k16r", "to")
-    act(T.nodrep[:], by(T.ios[:], u["nodu"]), "ios nodu", "nodrep")
-    ts(cl["t1"], cl["r"], 14.0, A.not_equal, "c_r", "c_t1")
-    ts(cl["msend"], cl["r"], 7.0, A.is_ge, "c_r c_t1", "c_msend", cl["t1"], A.mult)
-    ts(cl["r8"], cl["r"], 8.0, A.is_ge, "c_r", "c_r8", 8.0, A.mult)
-    lin(T.keep32[:], T.l32[:], 1.0, 0.0, "l32", "keep32", AF.Sign)
-    lin(cl["mown"], cl["msend"], -1.0, 1.0, "c_msend", "c_mown")
-    ts(cl["vsel"], cl["r8"], cl["r"], A.add, "c_r8 c_r", "c_vsel", 7.0, A.add)
-    ts(T.maskv[:], T.l32[:], cl["vsel"], A.is_equal, "l32 c_vsel", "maskv")
-    lin(cl["rm"], cl["r"], 1.0, -15.25, "c_r", "c_rm")
-    lin(cl["k3"], cl["r"], 1.0, C - 7 - PO + 1024.0, "c_r", "c_k3")
-    lin(cl["o320"], cl["o16"], 20.0, PO, "c_o16", "c_o320")
-    lin(cl["d320"], cl["o16"], -20.0, float(C), "c_o16", "c_d320")
-    ts(cl["m7"], cl["r"], 14.0, A.is_lt, "c_r c_msend", "c_m7", cl["msend"], A.mult)
-    ts(T.dd[:], T.loc[:], cl["r1"], A.not_equal, "loc c_r1", "dd")
-    ts(f["k3"], iot[:, 0:VW:8], cl["k3"], A.add, "iot c_k3 c_m7", "k3", cl["m7"], A.mult)
-    lin(starts(T.dd), k16n, 0.0, 0.0, "iot", "c_dd dd")
-    lin(ends(T.dd), ends(T.dd), cl["d320"], 0.0, "dd c_d320", "c_dd dd")
-    lin(f["k3"], f["k3"], 1.0, -1024.0, "k3", "k3")
-    lin(T.te[:, 0:C], T.loc[:], -0.5, -0.5, "loc", "te0")
-    lin(ends(T.cs), k16n, 0.0, 1024.0, "iot", "cs")
-    lin(starts(T.dtt), k16n, 0.0, 1024.0, "iot", "c_dt dtt")
-    lin(ends(T.dtt), k16n, 1.0, float(14 - C), "iot", "c_dt dtt")
-    lin(T.em[:, 0:16], iot[:, 0:16], 0.0, -1.0, "iot", "emp")
-    quant(T.qv[:], T.sv[:], T.vt0[:], "vt0", "qv")
-
-    def plane(b):
-        return T.win[:, WW * b:WW * b + C]
-
-    def unpacker(b):
-        return T.qe[:, 128 * b:128 * b + 128], T.se[:, 128 * b:128 * b + 128]
+        op({q: (lambda: e.dma_start(out, a), 60)}, rd, wr, "dma", late, (sem, n))
 
     sent = [0]
 
-    def remote(out, a, sem, peer, rd, late):
+    def remote(out, a, sem, peer, late):
         rid, pid = topo.addr(peer, core)
         mask = topo.mask(core, peer)
         sent[0] += len(topo.engines(core, peer))
+        cast = (lambda v: ap(v).bitcast(dt.uint8)) if SCRATCH[a[0]][2] == Q4 else ap
 
         def call():
-            g.remote_dma(out, a, T.sem[sem], T.sem.sent, pid, rid, mask)
-        op("g", call, rd, "r%s_%d" % (sem, late), None, late)
+            g.remote_dma(cast(out), cast(a), T.sem[sem], T.sem.sent, pid, rid, mask)
+        op({"g": (call, 300)}, [a], [("r" + out[0], 0, 1, 1)], "far", late)
+
+    def arrive(views, sem, n):
+        op({"far": (None, 0)}, [("r" + v[0], 0, 1, 1) for v in views], views, "", 0, (sem, n))
+
+    W = {k: whole(k) for k in SCRATCH}
+    ps = [cut(W["ps%d" % b], 0, C) for b in range(8)]
+    fb, ub = [1, 2, 3, 4], [5, 6, 7, 1]
+
+    (loc, k16r, k64r, iom, ios, l32, diag, sig, sigc, keep, keep32, d0s, maskv, mkg, mkl, mkc, mt, nodrep, b3, ks, ks2,
+     fsd) = news("pb", C, "loc k16r k64r iom ios l32 diag sig sigc keep keep32 d0s maskv mkg mkl mkc mt nodrep b3 ks ks2 fsd")
+    iob, tm, tw, th, tl, ti, to, ta, tb = news("pb", 256, "iob tm tw th tl ti to ta tb")
+    t16, srcw = new("pb", 16), new("pb", WW)
+    col = new("pf", 32)
+    names = "r nr r1 rm1 want cap msend mown o16 vsel m7 k3 te to h t0 r8 r16 r17 rh rm t1 nz".split()
+    cl = {k: cut(col, i, i + 1) for i, k in enumerate(names)}
+    i32, k16n, k32n, self_, kpair, k3 = new("pf", 32), new("pf", TR), new("pf", 10), new("pf", TR), new("pf", TR), new("pf", TR)
+    nodu, invu, tsel, upk = new("pu", TR), new("pu", TR), new("pu", TR), new("pu", 8)
+    (la, lb, lc, cv1, cv2, cv4, m1, m2, m4, mm_, g2, g4, g8, g9, msum, cmp1, scs, strep, pst, cvp, xx, sc1, sc2, kb, cmp2, rk,
+     hi, his, wd, wds, lo, los, b4, ov, osrep, fs0, fs, vb, vs, inv, invs, em, ems, yy, flag, tsc, lnkj, srcj, b2, b1,
+     b1s) = news("pb", C, "la lb lc cv1 cv2 cv4 m1 m2 m4 mm g2 g4 g8 g9 msum cmp1 scs strep pst cvp xx sc1 sc2 kb cmp2 rk "
+                          "hi his wd wds lo los b4 ov osrep fs0 fs vb vs inv invs em ems yy flag tsc lnkj srcj b2 b1 b1s")
+    ssb, neg, oprep, ysb, b1f = news("pf", C, "ssb neg oprep ysb b1f")
+    sn, tt2 = new("pf", C + 32), new("pf", 2 * C + 32)
+    (j0f, j1f, n1, n2, n3, n4, szn, csz, st16, stm, nf, dl, pa, qb, na, own, rel, cg, o2f,
+     pr) = news("pf", TR, "j0f j1f n1 n2 n3 n4 szn csz st16 stm nf dl pa qb na own rel cg o2f pr")
+    (j0, j1, j2, j4, m2u, stu, sou, keyu, idxw, cwu, ou, relu, idxu, tu, cgu, o2u,
+     eu) = news("pu", TR, "j0 j1 j2 j4 m2u stu sou keyu idxw cwu ou relu idxu tu cgu o2u eu")
+    vu = new("pu", 10)
+    snm = cut(sn, 16, C + 16)
+
+    def seg(out, a, o):
+        scan(out, keep, a, A.mult, o)
+
+    def place(out, a):
+        scan(out, k64r, a, A.max, A.add, -PO)
+
+    def take(out, a, mask):
+        scan(out, a, mask, A.max, A.add, -1024.0)
+
+    dma("s", T.pari[:], T.par[:], [], [W["pari"]], "dpar")
+    dma("y", T.ut[:], T.u[:], [], [W["ut"]], "du", 16, 500)
+    dma("s", T.nodi[:], T.nod[:], [], [W["nodi"]], "dnod")
+    dma("y", T.xt[:], T.x[:], [], [W["xt"]], "dx", 16, 1500)
+    dma("y", T.wq[:].bitcast(dt.uint8), T.wc[:], [], [W["wq"]], "dw", 16, 2500)
+    dma("y", T.wsb[:], T.ws[:], [], [W["wsb"]], "dws", 16, 2500)
+    dma("y", T.vt0[:], T.v[:], [], [W["vt0"]], "dv", 16, 3000)
+
+    pi, r0, r1 = cut(W["pi"], 0, 1), cut(W["ri"], 0, 1), cut(W["ri"], 1, 2)
+    iota(pi, [[0, 1]], 0, 1)
+    iota(i32, [[1, 32]], 0)
+    iota(loc, [[0, TR], [1, 16]], 0)
+    iota(k16r, [[16, TR], [0, 16]], 0)
+    mset(W["ebuf"], 0.5)
+    op({"g": (lambda: g.affine_select(T.ebuf[:], T.ebuf[:], [[1, 528]], A.is_equal, 0.0, -3, -4), 1050)}, [W["ebuf"]], [W["ebuf"]])
+    iota(iob, [[1, 256]], 0)
+    iota(ios, [[1, C]], -int(SO))
+    iota(ks, [[0, C]], 0)
+    iota(k64r, [[16, TR], [0, 16]], -int(PO))
+    iota(l32, [[0, TR // 2], [1, 32]], 0)
+    iota(cut(srcw, C, WW), [[1, VW]], C - int(SO))
+    iota(ks2, [[0, C]], 0)
+    iota(mt, [[0, C]], -1)
+
+    mset(b3, 1.0)
+    scan(iom, b3, b3, A.mult, A.add, -PO - 1.0)
+    mset(fsd, 0.5)
+    mset(cut(sn, 0, 16), 0.0)
+    mset(cut(sn, C + 16, C + 32), 0.0)
+    ts(r0, pi, 15, A.bitwise_and)
+    ts(r1, pi, 16, A.bitwise_and)
+    cp(cl["r"], r0)
+    cp(cl["h"], r1)
+    lin(k16n, cut(i32, 0, TR), 16.0)
+    lin(k32n, cut(i32, 0, 10), 32.0)
+    lin(cl["r16"], cl["r"], 16.0)
+    lin(cl["rm1"], cl["r"], 1.0, -1.0)
+    lin(cl["nr"], cl["r"], -1.0)
+    lin(cl["r17"], cl["r"], 17.0)
+    lin(cl["te"], cl["h"], 21.0, cl["r"])
+    lin(cl["to"], cl["h"], -21.0, cl["r"])
+    lin(self_, k16n, 1.0, cl["r"])
+    ts(kpair, k16n, -1.0, A.mult, cl["r16"], A.add)
+    ts(diag, loc, cl["r"], A.is_equal)
+    ts(mkl, loc, cl["rm1"], A.is_equal, -512.0, A.mult)
+    lin(mkc, diag, 16.0)
+    tt(mkg, mkl, mkc, A.add)
+    lin(ends(mkg), ends(mkg), 1.0, -16.0)
+    lin(mkl, mkg, 16.0)
+    lin(ends(mkl), ends(mkl), 1.0, -256.0)
+    if OPT["cap"]:
+        lin(mkc, mkl, 2.0)
+    ts(cut(tsel, 0, TR, 2), k32n, cl["te"], A.add)
+    ts(cut(tsel, 1, TR, 2), k32n, cl["to"], A.add, 352.0, A.add)
+    cp(upk, cut(k16n, 0, 8))
+    cp(nodu, W["nodi"])
+    act(sig, loc, AF.Sign, 1.0, cl["nr"])
+    ts(keep, loc, 1.0, A.min)
+    lin(d0s, diag, -2.0, 1.0)
+    lin(starts(d0s), k16n, 0.0)
+    tt(j0f, W["pari"], k16n, A.add)
+    cp(j0, j0f)
+    pick(lc, iom, j0)
+    pick(lb, lc, j0)
+    take(cv1, lb, mkg)
+    tt(n1, self_, j0f, A.subtract)
+    act(n2, n1, AF.Relu)
+    ts(n3, self_, -PO, A.add)
+    tt(n4, ends(cv1), n3, A.is_equal)
+    tt(n1, n4, n2, A.mult)
+    tt(j1f, n1, j0f, A.add)
+    cp(j1, j1f)
+    tt(pr, j1f, kpair, A.add)
+    cp(m2u, pr)
+    pick(la, iom, j1)
+    ts(ta, cut(k16r, 0, 256), cl["r16"], A.is_equal)
+    tt(tm, ta, cut(diag, 0, 256), A.max)
+    lin(tm, tm, -2.0, 64.0)
+    quant(W["qu0"], W["su0"], W["ut"])
+    quant(W["qx"], W["sx"], W["xt"])
+    op({"v": (lambda: V.tensor_copy(T.qu[:].bitcast(dt.uint32), T.qu0[:].bitcast(dt.uint32).indirect(ap(upk))), 220)},
+       [W["qu0"], upk], [W["qu"]])
+    op({"s": (lambda: S.activation(T.su[:], T.su0[:].indirect(ap(upk)), AF.Copy), 230)}, [W["su0"], upk], [W["su"]])
+    for b in range(4):
+        quant(cut(W["qe"], 128 * b, 128 * b + 128), cut(W["se"], 128 * b, 128 * b + 128), cut(W["ebuf"], 3 - b, 515 - b))
+    cp(by(b3, nodu), iom)
+    tt(b1, b3, diag, A.mult)
+    seg(b1s, b1, A.add)
+    ts(invu, ends(b1s), PO, A.add)
+    if OPT["sigc"]:
+        pick(sigc, sig, invu, split=False)
+    pick(nodrep, ios, nodu, split=False)
+    lin(t16, cut(i32, 0, 16), 16.0, 16.0)
+    lin(cl["r1"], cl["r"], 1.0, 1.0)
+    act(cl["o16"], cl["r16"], AF.Relu, 1.0, -224.0)
+    lin(cl["want"], cl["o16"], -0.125, cl["r1"])
+    lin(cl["cap"], cl["o16"], -0.125, 16.0)
+    lin(cl["rh"], cl["r"], 0.5, -8.0)
+    lin(cl["rm"], cl["r"], 1.0, -15.5)
+    lin(cl["t0"], cl["r16"], 1.0, -256.0)
+    ts(tw, cut(loc, 0, 256), cl["want"], A.is_equal, 0.0625, A.mult)
+    tt(tw, tw, cut(k16r, 0, 256), A.mult)
+    ts(tw, tw, cl["cap"], A.min)
+    tt(to, cut(diag, 0, 256), cut(k16r, 0, 256), A.mult)
+    tt(tb, ta, cut(loc, 0, 256), A.mult)
+    ts(th, tb, 8.0, A.is_ge)
+    tt(th, th, tb, A.mult)
+    tt(tl, tb, th, A.subtract)
+    lin(th, th, 1.0, cl["r16"])
+    lin(tl, tl, 1.0, cl["r16"])
+    ts(cl["nz"], cl["r"], 1.0, A.min)
+    lin(ti, cut(k16r, 0, 256), -0.0625, 15.0)
+    tt(ti, ti, cut(diag, 0, 256), A.mult)
+    lin(ti, ti, cl["nz"])
+    ts(cl["t1"], cl["r"], 14.0, A.not_equal)
+    ts(cl["msend"], cl["r"], 7.0, A.is_ge, cl["t1"], A.mult)
+    ts(cl["r8"], cl["r"], 8.0, A.is_ge, 8.0, A.mult)
+    ts(keep32, l32, 1.0, A.min)
+    lin(cl["mown"], cl["msend"], -1.0, 1.0)
+    ts(cl["vsel"], cl["r8"], cl["r"], A.add, 7.0, A.add)
+    ts(maskv, l32, cl["vsel"], A.is_equal)
+    lin(cl["k3"], cl["r"], 1.0, C - 7 - PO + 1024.0)
+    ts(cl["m7"], cl["r"], 14.0, A.is_lt, cl["msend"], A.mult)
+    lin(k3, k16n, 0.5, cl["k3"])
+    lin(k3, k3, cl["m7"], -1024.0)
+    for h in (0, 1):
+        lin(ends(cut(mt, H * h, H * h + H)), cut(k16n, 0, 10), 1.0, 31.0)
+    quant(W["qv"], W["sv"], W["vt0"])
+
+    def plane(b):
+        return cut(W["win"], WW * b, WW * b + C)
+
+    def lane(name, b):
+        return cut(W[name], b, _n(W[name]), 4)
+
+    def block(name, b, n):
+        return cut(W[name], n * b, n * b + n)
 
     for rnd in range(3):
         peer = T.cores[rank ^ MASKS[rnd]]
         ne = len(topo.engines(peer, core))
-        final = rnd == 2
-        snd, lnd = T["snd%d" % rnd], T["lnd%d" % rnd]
-        qs, ss, ql, sl = T["qs%d" % rnd], T["ss%d" % rnd], T["ql%d" % rnd], T["sl%d" % rnd]
+        first, final = rnd == 0, rnd == 2
+        sa, lda, sb, ldb, qs, ss, ql, sl = (W[k + str(rnd)] for k in ("sa", "la", "sb", "lb", "qs", "ss", "ql", "sl"))
 
-        mm(ps[0][:, 0:C], T.qu[:], T.su[:], T.qx[:], T.sx[:], "qu su qx", "ps0")
+        mm(ps[0], W["qu"], W["su"], W["qx"], W["sx"])
         for b in range(4):
-            mm(ps[fb[b]][:, 0:C], *unpacker(b), T.qx[:], T.sx[:], "qe%d qx" % b, "ps%d" % fb[b])
-            act(plane(b), ps[fb[b]][:, 0:C], "ps%d" % fb[b], "ps%d w%d" % (fb[b], b))
+            mm(ps[fb[b]], block("qe", b, 128), block("se", b, 128), W["qx"], W["sx"])
+            lin(plane(b), ps[fb[b]])
         for b in (0, 1):
-            act(T.fo[:, C * b:C * b + C], plane(b), "w%d" % b, "fo%d" % b)
-        act(T.ssb[:], ps[0][:, 0:C], "ps0", "ps0 ssb")
+            lin(block("fo", b, C), plane(b))
 
-        act(T.ma[:], by(T.tm[:], u["m2u"]), "tm m2u", "ma")
-        act(T.mc[:], T.ma[:], "ma", "mc")
-        turn(T.lb, "lb")
-        nat(T.j2u, "j2u")
-        act(mid(T.la), by(mid(T.lb), j2), "lb j2u", "la")
-        tt(T.mb[:], by(T.ma[:], j2), T.mc[:], A.max, "ma mc j2u", "mb")
-        act(T.mc[:], T.mb[:], "mb", "mc")
-        turn(T.la, "la")
-        nat(T.j4u, "j4u")
-        act(mid(T.lb), by(mid(T.la), j4), "la j4u", "lb")
-        tt(T.ma[:], by(T.mb[:], j4), T.mc[:], A.max, "mb mc j4u", "ma")
-        act(T.mc[:], T.ma[:], "ma", "mc")
-        turn(T.lb, "lb")
-        nat(T.j8u, "j8u")
-        tt(T.mb[:], by(T.ma[:], j8), T.mc[:], A.max, "ma mc j8u", "mb")
-        seg(T.sc2[:], T.mb[:], A.add, "mb", "sc2")
-        lin(f["szn"], ends(T.sc2), 0.5, 8.0, "sc2", "szn")
-        lin(f["csz"], ends(T.sc2), -0.5, 8.0, "sc2", "csz")
-        lin(f["dla"], n7, -16.0, 0.0, "n7", "dla")
-        lin(T.lk[:, 0:TR], n7, 16.0, cl["r16"], "n7 c_r16", "lka")
+        pick(lb, la, j1, split=first)
+        pick(m1, tm, m2u, split=first)
+        take(cv2, lb, mkg)
+        ts(j2, ends(cv2), PO, A.add)
+        pick(lc, lb, j2, split=first)
+        pick(g2, m1, j2, -1.0, 192.0, split=first)
+        take(cv4, lc, mkg)
+        ts(j4, ends(cv4), PO, A.add)
+        scan(m2, g2, m1, A.max, A.subtract)
+        pick(g4, m2, j4, -1.0, 192.0, split=first)
+        scan(m4, g4, m2, A.max, A.subtract)
+        pick(g8, m4, j4, split=first)
+        pick(g9, g8, j4, -1.0, 127.0, split=first)
+        scan(mm_, g9, m4, A.max, A.subtract)
+        seg(msum, mm_, A.add)
+        lin(szn, ends(msum), 0.5, 8.0)
+        lin(csz, ends(msum), -0.5, 8.0)
 
-        tt(mid(T.sn), by(T.ssb[:], u["nodu"]), T.sig[:], A.mult, "ssb nodu sig", "sn")
-        act(T.neg[:], mid(T.sn), "sn", "neg", -1.0)
-        op("v", lambda: V.transpose(T.tt[:, 0:C], mid(T.sn)), "sn", "tt0")
-        op("v", lambda: V.transpose(T.tt[:, C:2 * C + 32], T.sn[:]), "sn c_psn c_qsn", "tt1")
-        tt(T.cmp[:], by(T.tt[:], T.tsel[:]), T.neg[:], A.is_gt, "tt0 tt1 tsel0 tsel1 neg", "cmp")
-        scan(T.scs[:], T.d0s[:], T.cmp[:], A.mult, A.add, "d0s cmp", "scs")
-        ts(u["stu"], ends(T.scs), cl["r"], A.add, "scs c_r", "stu")
-        ts(u["sou"], ends(T.scs), cl["r17"], A.add, "scs c_r17", "sou")
-        act(T.strep[:], by(T.iob[:, 0:16], u["stu"]), "iob stu", "strep")
-        act(mid(T.la), by(T.strep[:], j1), "strep j1u", "la")
-        lin(f["st16"], ends(T.scs), 16.0, cl["r16"], "scs c_r16", "st16")
-        turn(T.la, "la")
-        ts(T.lk[:, TR:TR + 32], by(T.tb[:], T.tsn[:]), 16.0, A.mult, "tb0 tb1 tsn", "lkb")
-        tt(f["dlb"], f["st16"], T.lk[:, TR:2 * TR], A.subtract, "st16 lkb", "dlb")
-
-        tt(T.xx[:], by(T.t16[:], u["stu"]), T.mb[:], A.mult, "t16 stu mb", "xx")
-        seg(T.sc1[:], T.xx[:], A.max, "xx", "sc1")
-        seg(T.b1[:], T.xx[:], A.min, "xx", "b1")
-        act(T.b4[:], by(T.to[:], u["sou"]), "to sou", "b4", 0.0625)
-        for k in ("fa", "fb"):
-            lin(f[k], ends(T.sc1), 1.0, -255.0, "sc1", k, AF.Relu)
-        tt(f["n1"], ends(T.sc1), f["szn"], A.add, "sc1 szn", "n1")
-        tt(f["n2"], f["csz"], ends(T.b1), A.subtract, "b1 csz", "n2")
-        tt(starts(T.ks), f["n1"], f["n2"], A.min, "n1 n2", "ks")
-        seg(T.kb[:], T.ks[:], A.add, "ks", "kb")
-        ts(u["keyu"], starts(T.ks), 0.0, A.add, "ks", "keyu")
-        tt(T.cmp[:], by(T.iob[:], u["keyu"]), T.kb[:], A.is_lt, "iob keyu kb", "cmp")
-        lin(starts(T.ks), ends(T.scs), 0.5, cl["rh"], "scs c_rh", "ks")
-        seg(T.sc1[:], T.cmp[:], A.add, "cmp", "sc1 vca vcb")
-        tt(f2["pa"], f2["fa"], f2["dla"], A.mult, "fa fb dla dlb", "pa")
-        tt(f2["qa"], f2["pa"], T.lk[:, 0:2 * TR], A.add, "pa lka lkb", "qa")
-        tt(f["na"], ends(T.sc1), f["qb"], A.add, "sc1 qa", "na")
-        cp(T.idxw[:], f["na"], "na", "idxw")
-        act(T.cmp[:, 0:H], by(T.tw[:], T.idxw[:, 0:TR // 2]), "tw idxw cmp", "vca")
-        cp(T.cmp[:, H:C], by(T.tw[:], T.idxw[:, TR // 2:TR]), "tw idxw cmp", "vcb")
-        place(T.sc2[:], T.cmp[:], "vca vcb cmp", "sc2")
-        ts(snd[:], ends(T.sc2), cl["msend"], A.mult, "sc2 c_msend", "snd%d" % rnd)
-        remote(lnd[:], snd[:], "aw%d" % rnd, peer, "snd%d" % rnd, FAR)
-
-        tt(f["n1"], ends(T.sc1), f["qa"], A.add, "sc1 qa", "n1")
-        cp(u["idxp"], f["n1"], "n1", "idxp")
-        act(T.xx[:], by(T.tj[:], u["idxp"]), "tj idxp", "xx")
-        place(T.b2[:], T.b4[:], "b4", "b2 vb2a vb2b")
-        seg(T.stb[:], T.ks[:], A.add, "ks", "stb")
-        ts(u["ou"], ends(T.b2), PO, A.add, "b2 vb2a", "ou")
-        lin(T.stb[:, 14:C:16], k16n, 0.0, 7.25, "iot", "c_stb stb")
-        place(T.b1[:], T.xx[:], "xx", "b1")
-        ts(u["pnu"], ends(T.b1), PO, A.add, "b1", "pnu")
-        tt(T.b1[:], by(T.nodrep[:], u["pnu"]), T.maskv[:], A.mult, "nodrep pnu maskv", "b1")
-        act(T.srcw[:, 0:C], by(T.nodrep[:], u["ou"]), "nodrep ou", "srcw")
-        scan(T.kb[:], T.keep32[:], T.b1[:], A.mult, A.add, "keep32 b1", "kb")
-        ts(T.vu[:], T.kb[:, 31:C:32], SO, A.add, "kb", "vu")
-        for b in (2, 3):
-            act(T.vt[:, b:4 * VW:4], by(plane(b), T.vu[:]), "w%d vu" % b, "v%d" % b, 2.0)
-        for b in (0, 1):
-            ts(T.vt[:, b:4 * VW:4], by(plane(b), T.vu[:]), 2.0, A.mult, "w%d vu" % b, "v%d" % b)
-        lin(f["own"], ends(T.sc2), cl["mown"], 0.0, "sc2 c_mown", "own")
-        lin(f["stm"], ends(T.scs), 1.0, cl["rm"], "scs c_rm", "stm")
-        act(T.osrep[:], by(T.loc[:] if final else T.iom[:], u["ou"]), "iom ou", "osrep")
-        quant(qs[:], ss[:], T.vt[:], "v0 v1 v2 v3", "qs%d" % rnd)
-        remote(ql[:].bitcast(dt.uint8), qs[:].bitcast(dt.uint8), "av%d" % rnd, peer, "qs%d" % rnd, FAR + 1000)
-        remote(sl[:], ss[:], "av%d" % rnd, peer, "qs%d" % rnd, FAR + 300)
-
-        op(None, None, "raw%d_%d" % (rnd, FAR), "lnd", ("aw%d" % rnd, ne))
-        op(None, None, "rav%d_%d rav%d_%d" % (rnd, FAR + 300, rnd, FAR + 1000), "ql", ("av%d" % rnd, 2 * ne))
-        cg = starts(T.cs)
-        tt(cg, f["own"], lnd[:], A.add, "own lnd", "cs")
-        seg(T.kb[:], T.cs[:], A.add, "cs", "kb")
-        ts(u["cgu"], cg, PO, A.add, "cs", "cgu")
-        tt(f["o2f"], cg, f["k3"], A.max, "cs k3", "o2f")
-        tt(T.cmp[:], by(T.iom[:], u["cgu"]), T.kb[:], A.is_equal, "iom cgu kb", "cmp")
-        act(T.lnkj[:], by(T.osrep[:], u["cgu"]), "osrep cgu", "lnkj")
-        if not final:
-            act(ends(T.lnkj), ends(T.osrep), "osrep", "c_lnk lnkj")
-        ts(u["o2u"], f["o2f"], PO, A.add, "o2f", "o2u")
-        scan(T.sc1[:], T.dd[:], T.cmp[:], A.mult, A.max, "dd cmp", "sc1")
-        tt(f["n1"], ends(T.sc1), cg, A.add, "sc1 cs", "n1")
-        ts(u["idxu"], f["n1"], cl["o320"], A.add, "n1 c_o320", "idxu")
-        act(T.srcj[:], by(T.srcw[:], u["o2u"]), "srcw srcwc o2u", "srcj")
-        for b in range(4):
-            mm(ps[ub[b]][:, 0:VW], *unpacker(b), ql[:], sl[:], "qe%d ql" % b, "ps%d" % ub[b])
-            act(T.win[:, WW * b + C:WW * b + WW], ps[ub[b]][:, 0:VW], "ps%d" % ub[b], "ps%d u%d" % (ub[b], b))
-        tt(T.xx[:], by(T.te[:], u["idxu"]), T.stb[:], A.add, "te0 te1 idxu stb", "xx")
-        ts(mid(T.em), T.xx[:], -1.0, A.max, "xx", "em", 0.0, A.min)
-        seg(T.sc1[:], mid(T.em), A.add, "em", "sc1")
-        tt(starts(T.ks), f["stm"], ends(T.sc1), A.subtract, "stm sc1", "ks")
-        scan(T.yy[:], T.ks[:], T.em[:, 15:C + 15], A.max, A.add, "ks em emp", "yy")
-        ts(T.cmp[:], T.yy[:], -0.5, A.not_equal, "yy", "cmp", 15.0, A.mult)
-        scan(T.f1[:], T.dtt[:], T.cmp[:], A.add, A.min, "dtt cmp", "f1")
-        ts(T.tu[:], ends(T.f1), float(C), A.add, "f1", "tu")
-        act(T.b2[:, 0:H], by(T.srcj[:], T.tu[:, 0:TR // 2]), "srcj tu", "vb2a")
-        cp(T.b2[:, H:C], by(T.srcj[:], T.tu[:, TR // 2:TR]), "srcj tu", "vb2b b2")
-        act(T.oprep[:] if final else mid(T.la), by(T.lnkj[:], T.tu[:]), "lnkj tu", "opr" if final else "la")
-        tt(T.b1[:], by(T.b2[:], T.invu[:]), T.diag[:], A.mult, "vb2a vb2b invu diag", "b1")
-        seg(T.kb[:], T.b1[:], A.add, "b1", "kb")
-        ts(u["eu"], ends(T.kb), SO, A.add, "kb", "eu")
-
-        def whole(b):
-            return by(T.win[:, WW * b:WW * b + WW], u["eu"])
-        for b in (3, 2):
-            act(T.hh[:, C * (b - 2):C * (b - 1)], whole(b), "w%d u%d eu" % (b, b), "h%d" % b)
-        for b in (0, 1):
-            tt(T.zt[:, b:4 * C:4], whole(b), T.fo[:, C * b:C * b + C], A.add, "w%d u%d eu fo%d" % (b, b, b), "z%d" % b)
-        for b in (3, 2):
-            tt(T.zt[:, b:4 * C:4], T.hh[:, C * (b - 2):C * (b - 1)], ps[fb[b]][:, 0:C], A.add,
-               "h%d ps%d" % (b, fb[b]), "z%d ps%d" % (b, fb[b]))
-        for b in range(4):
-            act(T.z32[:, C * b:C * b + C], T.zt[:, b:4 * C:4], "z%d" % b, "zz%d" % b, 32.0)
-        quant(T.qz[:], T.sz[:], T.zt[:], "z0 z1 z2 z3", "qz")
-        for b in range(4):
-            mm(ps[fb[b]][:, 0:C], T.wq[:, 128 * b:128 * b + 128], T.wsb[:, 128 * b:128 * b + 128], T.qz[:], T.sz[:],
-               "wq wsb qz", "ps%d" % fb[b])
-        if final:
-            dma("y", T.op[:], T.oprep[0:128:16, :], "opr", "", "dop")
+        if OPT["sigc"] and not first:
+            tt(ssb, ps[0], sigc, A.mult)
+            pick(snm, ssb, nodu)
         else:
-            turn(T.la, "la")
-            nat(T.j1u, "j1u")
-            tt(T.n7[:], by(T.tb[:], T.tsn[:]), T.k64[:], A.subtract, "tb0 tb1 tsn k64", "n7")
-            act(mid(T.lb), by(mid(T.la), j1), "la j1u", "lb")
-            pair_index()
-        for b in range(4):
-            tt(T.x32[:, C * b:C * b + C], ps[fb[b]][:, 0:C], T.z32[:, C * b:C * b + C], A.add,
-               "zz%d ps%d" % (b, fb[b]), "xx%d ps%d" % (b, fb[b]))
-            if b < 3:
-                act(T.xt[:, b:4 * C:4], T.x32[:, C * b:C * b + C], "xx%d" % b, "x%d" % b, 0.03125)
-        ts(T.xt[:, 3:4 * C:4], T.x32[:, 3 * C:4 * C], 0.03125, A.mult, "xx3", "x3")
-        quant(T.qx[:], T.sx[:], T.xt[:], "x0 x1 x2 x3", "qx")
+            lin(ssb, ps[0])
+            tt(snm, by(ssb, nodu), sig, A.mult)
+        lin(neg, snm, -1.0)
+        turn(cut(tt2, 0, C), snm)
+        turn(cut(tt2, C, 2 * C + 32), sn)
+        tt(cmp1, by(tt2, tsel), neg, A.is_gt)
+        scan(scs, d0s, cmp1, A.mult, A.add)
+        ts(stu, ends(scs), cl["r"], A.add)
+        ts(sou, ends(scs), cl["r17"], A.add)
+        lin(st16, ends(scs), 16.0, cl["t0"])
+        lin(stm, ends(scs), 1.0, cl["rm"])
+        lin(starts(fsd), ends(scs), 0.5, cl["rh"])
+        pick(strep, t16, stu, 1.0, -16.0, split=False)
+        pick(pst, strep, j1, split=False)
+        take(cvp, pst, mkl)
+        tt(dl, ends(cvp), st16, A.subtract)
 
-    mm(ps[0][:, 0:C], T.qv[:], T.sv[:], T.qx[:], T.sx[:], "qv qx", "ps0")
-    dma("y", T.oc[:], T.qx[:].bitcast(dt.uint8), "qx", "", "doc", 16, 1000)
-    act(T.ysb[:], ps[0][:, 0:C], "ps0", "ps0 ysb")
-    dma("s", T.y[:], T.ysb[:], "ysb", "", "dy", 16, 1000)
+        tt(xx, by(t16, stu), mm_, A.mult)
+        seg(sc1, xx, A.max)
+        seg(sc2, xx, A.min)
+        tt(n1, ends(sc1), szn, A.add)
+        tt(n2, csz, ends(sc2), A.subtract)
+        tt(starts(ks), n1, n2, A.min)
+        ts(keyu, starts(ks), 0.0, A.add)
+        seg(kb, ks, A.add)
+        tt(cmp2, by(iob, keyu), kb, A.is_lt)
+        seg(rk, cmp2, A.add)
+        act(nf, ends(sc2), AF.Relu, -1.0, -255.0)
+        tt(pa, nf, dl, A.mult)
+        tt(qb, pa, st16, A.add)
+        tt(na, ends(rk), qb, A.add)
+        ts(idxw, na, 256.0, A.add)
+        pick(hi, th, idxw)
+        seg(his, hi, A.max)
+        lin(sa, ends(his))
+        remote(lda, sa, "aa%d" % rnd, peer, 0)
+        pick(wd, tw, idxw)
+        place(wds, wd)
+        lin(sb, ends(wds), cl["msend"])
+        remote(ldb, sb, "ab%d" % rnd, peer, 0)
+
+        pick(lo, tl, idxw, split=False)
+        seg(los, lo, A.max)
+        pick(b4, to, sou, 0.0625, split=False)
+        place(ov, b4)
+        ts(ou, ends(ov), PO, A.add)
+        pick(cut(srcw, 0, C), nodrep, ou, split=False)
+        pick(osrep, loc if final else iom, ou, split=False)
+        seg(fs0, fsd, A.add)
+        ts(fs, fs0, -1.0, A.max, 0.0, A.min)
+        ts(cwu, ends(wds), PO, A.add)
+        lin(own, ends(wds), cl["mown"])
+        tt(vb, by(cut(srcw, 0, C), cwu), maskv, A.mult)
+        scan(vs, keep32, vb, A.mult, A.add)
+        ts(vu, cut(vs, 31, C, 32), SO, A.add)
+        for b in range(4):
+            lin(lane("vt", b), by(plane(b), vu), 2.0)
+        quant(qs, ss, W["vt"])
+        remote(ql, qs, "av%d" % rnd, peer, 1200)
+        remote(sl, ss, "av%d" % rnd, peer, 400)
+
+        arrive([lda], "aa%d" % rnd, ne)
+        arrive([ldb], "ab%d" % rnd, ne)
+        arrive([ql, sl], "av%d" % rnd, 2 * ne)
+        tt(rel, ends(los), lda, A.max)
+        cp(relu, rel)
+        pick(inv, ti, relu)
+        place(invs, inv)
+        ts(idxu, ends(invs), PO, A.add)
+        pick(em, fs, idxu)
+        seg(ems, em, A.add)
+        tt(starts(ks2), stm, ends(ems), A.subtract)
+        scan(yy, ks2, em, A.max, A.add)
+        ts(flag, yy, -0.5, A.not_equal, 15.0, A.mult)
+        scan(tsc, flag, mt, A.min, A.add, 64.0)
+        ts(tu, ends(tsc), -16.0, A.add)
+        tt(cg, own, ldb, A.add)
+        tt(o2f, cg, k3, A.max)
+        ts(o2u, o2f, PO, A.add)
+        ts(cgu, cg, PO, A.add)
+        pick(srcj, srcw, o2u, split=False)
+        pick(lnkj, osrep, cgu, split=False)
+        if not final:
+            lin(ends(lnkj), ends(osrep))
+        for b in range(4):
+            mm(cut(ps[ub[b]], 0, VW), block("qe", b, 128), block("se", b, 128), ql, sl)
+            lin(cut(W["win"], WW * b + C, WW * b + WW), cut(ps[ub[b]], 0, VW))
+        pick(b2, srcj, tu, halves=True)
+        if OPT["cap"]:
+            pick(b1, b2, invu)
+            take(b1f, b1, mkc)
+            ts(eu, ends(b1f), SO + 512.0, A.add)
+        else:
+            tt(b1, by(b2, invu), diag, A.mult)
+            seg(b1s, b1, A.add)
+            ts(eu, ends(b1s), SO, A.add)
+        pick(oprep if final else la, lnkj, tu, halves=True)
+        if final:
+            dma("y", T.op[:], T.pf[0:128:16, oprep[1]:oprep[2]], [oprep], [], "dop")
+        else:
+            take(cv1, la, mkg)
+            ts(j1, ends(cv1), PO, A.add)
+            tt(pr, ends(cv1), kpair, A.add)
+            ts(m2u, pr, PO, A.add)
+
+        for b in (3, 2):
+            lin(block("hh", b - 2, C), by(block("win", b, WW), eu))
+        for b in (0, 1):
+            tt(lane("zt", b), by(block("win", b, WW), eu), block("fo", b, C), A.add)
+        for b in (3, 2):
+            tt(lane("zt", b), block("hh", b - 2, C), ps[fb[b]], A.add)
+        for b in range(4):
+            lin(block("z32", b, C), lane("zt", b), 32.0)
+        quant(W["qz"], W["sz"], W["zt"])
+        for b in range(4):
+            mm(ps[fb[b]], block("wq", b, 128), block("wsb", b, 128), W["qz"], W["sz"])
+        for b in range(4):
+            tt(block("x32", b, C), ps[fb[b]], block("z32", b, C), A.add)
+            lin(lane("xt", b), block("x32", b, C), 0.03125)
+        quant(W["qx"], W["sx"], W["xt"])
+
+    dma("y", T.oc[:], T.qx[:].bitcast(dt.uint8), [W["qx"]], [], "doc", 16, 1000)
+    for h in (0, 1):
+        half = cut(ysb, H * h, H * h + H)
+        mm(cut(ps[5 + h], 0, H), W["qv"], W["sv"], block("qx", h, H), block("sx", h, H))
+        lin(half, cut(ps[5 + h], 0, H))
+        dma("ys"[h], T.y[:, H * h:H * h + H], ap(half), [half], [], "dy%d" % h, 16, 500)
     for k in range(4):
-        dma("y", T.osc[4 * k:4 * k + 4, :], T.sx[32 * k:32 * k + 4, :], "qx", "", "dos", 64)
-    _emit(g, T, _order(ops))
-    for s, n in (("dop", 16), ("doc", 16), ("dos", 64)):
+        dma("y", T.osc[4 * k:4 * k + 4, :], T.sx[32 * k:32 * k + 4, :], [W["sx"]], [], "dos", 64)
+    deps = _needs(ops)
+    _emit(g, T, ops, deps, _order(ops, deps))
+    for s, n in (("dop", 16), ("doc", 16), ("dos", 64), ("dy0", 16)):
         g.sync.wait_ge(T.sem[s], n)
-    g.scalar.wait_ge(T.sem.dy, 16)
+    g.scalar.wait_ge(T.sem.dy1, 16)
     g.wait_ge(T.sem.sent, sent[0])

@@ -9,7 +9,8 @@ H = C // 2
 PO, SO = 64.0, 224.0
 MASKS = [1, 2, 4]
 Q4, U8, BF, F32, I32, U16 = "float8_e4m3fn_x4", "uint8", "bfloat16", "float32", "int32", "uint16"
-OPT = {"sigc": True, "cap": False, "tries": 240}
+OPT = {"sigc": True, "cap": True, "vcap": True, "st": 1, "wd": 1, "dec": 2, "bl": 1, "xl": 2, "sc": 2,
+       "tries": 60, "turns": 6, "mend": 8000}
 
 SCRATCH = {}
 
@@ -28,15 +29,15 @@ for _r in range(3):
 _decl(BF, xt=4 * C, zt=4 * C, z32=4 * C, x32=4 * C, ut=512, vt0=512, ebuf=528, win=4 * WW, vt=4 * VW, hh=2 * C, fo=2 * C)
 _decl(I32, pi=2, ri=2, nodi=TR, pari=TR)
 _decl(BF, pb=28672)
-_decl(F32, pf=4096)
+_decl(F32, pf=6144)
 _decl(U16, pu=1024)
 for _b in range(8):
     SCRATCH["ps%d" % _b] = ("psum", [128, 512], F32)
 
-_DMAS = ["dx", "du", "dw", "dws", "dv", "dpar", "dnod", "dop", "doc", "dos", "dy0", "dy1"]
-SEMAPHORES = ["cv", "cs", "ct", "cg", "sent"] + _DMAS + [n + str(r) for n in ("aa", "ab", "av") for r in range(3)]
+_DMAS = ["dx0", "dx1", "du", "dw", "dws", "dv", "dpar", "dnod", "dop", "doc", "dos", "dy0", "dy1"]
+SEMAPHORES = ["cv", "cs", "ct", "cg", "sent"] + _DMAS + [n + str(r) for n in ("aa", "ab", "av", "dfa", "dfb") for r in range(3)]
 
-TUNES = ((1.0, 70, 1800, 1700), (0.75, 120, 1500, 1500), (1.25, 60, 2400, 2000), (1.0, 160, 1800, 1700))
+TUNES = ((1.0, 60, 1400, 1400), (0.75, 110, 1100, 1200), (1.25, 45, 1900, 1600), (1.0, 80, 700, 700))
 CHOSEN = []
 
 
@@ -70,8 +71,6 @@ def _needs(ops):
 
 
 def _order(ops, deps):
-    if CHOSEN:
-        return CHOSEN
     users = [[] for o in ops]
     for n, d in enumerate(deps):
         for m in d:
@@ -92,39 +91,81 @@ def _order(ops, deps):
             done[n] = free[q] + late[n]
         return max(done)
 
+    def lay(seq, before, back, spare, cost, late, hop):
+        done, at, busy = [0] * len(ops), [None] * len(ops), {}
+        for n in seq:
+            t = max([0] + [done[m] + hop for m in before[n]]) + (late[n] if back else 0)
+            best = None
+            for q, c in cost[n].items():
+                s, l = t, busy.setdefault(q, [])
+                i = len(l)
+                while i and l[i - 1][1] > t:
+                    i -= 1
+                while i < len(l) and l[i][0] < s + c:
+                    s = max(s, l[i][1])
+                    i += 1
+                if best is None or s + c * (1.0 + spare * (q == "v")) < best[0]:
+                    best = (s + c * (1.0 + spare * (q == "v")), s, q, i)
+            s, q, i = best[1:]
+            busy[q].insert(i, (s, s + cost[n][q]))
+            at[n], done[n] = (s, q), s + cost[n][q] + (0 if back else late[n])
+        return at, done
+
     rng, best = np.random.RandomState(1), None
     for attempt in range(OPT["tries"]):
-        cost, late, hop = tunes[attempt % 2 * 3]
-        shake = 1.0 + (0.4 if attempt else 0.0) * (rng.rand(len(ops)) - 0.5)
-        slack, spare = (0, 60, 150)[attempt % 3], 3.0 * rng.rand()
+        tune = tunes[attempt % len(tunes)]
+        cost, late, hop = tune
+        shake, spare = 1.0 + (0.3 if attempt else 0.0) * (rng.rand(len(ops)) - 0.5), 4.0 * rng.rand()
         way = [0] * len(ops)
         for n in range(len(ops) - 1, -1, -1):
-            way[n] = (min(cost[n].values()) + late[n]) * shake[n] + max([way[m] + hop for m in users[n]] + [0])
-        left = [len(d) for d in deps]
-        at, free, out = [0] * len(ops), {}, []
-        ready = [n for n in range(len(ops)) if not left[n]]
-        while ready:
-            start = {}
-            for n in ready:
-                q = min(cost[n], key=lambda q: max(at[n], free.get(q, 0)) + cost[n][q] * (1.0 + (spare if q == "v" else 0.0)))
-                start[n] = (max(at[n], free.get(q, 0)), q)
-            a = min(ready, key=lambda n: (start[n][0], -way[n]))
-            t, q = start[a]
-            n = max((m for m in ready if q in cost[m] and (start[m][1] == q or m == a) and start[m][0] <= t + slack),
-                    key=lambda m: way[m])
-            ready.remove(n)
-            out.append((n, q))
-            free[q] = start[n][0] + cost[n][q]
-            for m in users[n]:
-                at[m] = max(at[m], free[q] + late[n] + hop)
-                left[m] -= 1
-                if not left[m]:
-                    ready.append(m)
-        end = sum(replay(out, *k) for k in tunes)
-        if best is None or end < best[0]:
-            best = (end, out)
-    CHOSEN.extend(best[1])
-    return CHOSEN
+            way[n] = 1 + (min(cost[n].values()) + late[n]) * shake[n] + max([way[m] + hop for m in users[n]] + [0])
+        for turn in range(OPT["turns"]):
+            at, done = lay(sorted(range(len(ops)), key=lambda n: -way[n]), deps, False, spare, *tune)
+            out = [(n, at[n][1]) for n in sorted(range(len(ops)), key=lambda n: at[n][0])]
+            end = sum(replay(out, *k) for k in tunes)
+            if best is None or end < best[0]:
+                best = (end, out)
+            way = lay(sorted(range(len(ops)), key=lambda n: -done[n]), users, True, spare, *tune)[1]
+    return _mend(best[1], best[0], deps, users, tunes, rng)
+
+
+def _mend(order, score, deps, users, tunes, rng):
+    def replay(order, cost, late, hop):
+        done, why, free, last = [0] * len(order), [None] * len(order), {}, {}
+        for n, q in order:
+            t, w = free.get(q, 0), (last.get(q), True)
+            for m in deps[n]:
+                if done[m] + hop > t:
+                    t, w = done[m] + hop, (m, False)
+            free[q], last[q], why[n] = t + cost[n][q], n, w
+            done[n] = free[q] + late[n]
+        n, chain = max(range(len(order)), key=lambda n: done[n]), []
+        end = done[n]
+        while n is not None:
+            if why[n][1] and why[n][0] is not None:
+                chain.append((why[n][0], n))
+            n = why[n][0]
+        return end, chain
+
+    chains = [replay(order, *k)[1] for k in tunes]
+    for step in range(OPT["mend"]):
+        chain = chains[rng.randint(len(chains))]
+        m, n = chain[rng.randint(len(chain))]
+        at = {k[0]: i for i, k in enumerate(order)}
+        a, b, trial, how = at[m], at[n], list(order), rng.randint(4)
+        if how == 0 and max([at[d] for d in deps[n]] + [-1]) < a:
+            trial.insert(a, trial.pop(b))
+        elif how == 1 and min([at[d] for d in users[m]] + [len(order)]) > b:
+            trial.insert(b, trial.pop(a))
+        elif how > 1 and len(tunes[0][0][(m, n)[how - 2]]) > 1:
+            i = (a, b)[how - 2]
+            trial[i] = (trial[i][0], [q for q in tunes[0][0][trial[i][0]] if q != trial[i][1]][0])
+        else:
+            continue
+        ends = [replay(trial, *k) for k in tunes]
+        if sum(e[0] for e in ends) <= score:
+            order, score, chains = trial, sum(e[0] for e in ends), [e[1] for e in ends]
+    return order
 
 
 def _emit(g, T, ops, deps, order):
@@ -172,15 +213,13 @@ def rank_program(g, core, T, topo):
     V, S = g.vector, g.scalar
 
     def new(pool, n):
+        a = used[pool]
         used[pool] += (n + 15) // 16 * 16
         assert used[pool] <= SCRATCH[pool][1][1]
-        return (pool, used[pool] - (n + 15) // 16 * 16, used[pool] - (n + 15) // 16 * 16 + n, 1)
+        return (pool, a, a + n, 1)
 
-    def news(pool, n, names):
-        return [new(pool, n) for k in names.split()]
-
-    def whole(name):
-        return (name, 0, SCRATCH[name][1][1], 1)
+    def news(pool, n, count):
+        return [new(pool, n) for k in range(count)]
 
     def cut(v, a, b, step=1):
         return (v[0], v[1] + a, v[1] + b, step)
@@ -239,8 +278,18 @@ def rank_program(g, core, T, topo):
     def turn(out, a):
         op({"v": (lambda: V.transpose(ap(out), ap(a)), length(out, [a], 50))}, [a], [out])
 
-    def mset(out, c):
-        op({"v": (lambda: V.memset(ap(out), c), length(out, [out], 50))}, [], [out])
+    def ramp(out, pat, base, mul=0):
+        flt = {} if SCRATCH[out[0]][2] == I32 else {"allow_small_or_imprecise_dtypes": True}
+        return (lambda: g.iota(ap(out), pat, base, mul, **flt), 130 + 1.66 * _n(out))
+
+    def iota(out, pat, base, mul=0):
+        op({"g": ramp(out, pat, base, mul)}, [], [out])
+
+    def fill(out, c):
+        q = {"v": (lambda: V.memset(ap(out), c), length(out, [out], 50))}
+        if c == int(c):
+            q["g"] = ramp(out, [[0, _n(out)]], int(c))
+        op(q, [], [out])
 
     def act(out, a, fn, scale=1.0, bias=0.0):
         op({"s": (lambda: S.activation(ap(out), ap(a), fn, bias=ap(bias), scale=ap(scale)), length(out, [a], 65, 1.0))},
@@ -260,8 +309,12 @@ def rank_program(g, core, T, topo):
             return S.activation(ap(out), ap(a), AF.Identity, bias=ap(bias), scale=ap(scale))
         op({"v": (vec, length(out, [a], 50)), "s": (sca, length(out, [a], 65, 1.0))}, [a, scale, bias], [out])
 
+    def either(out, a, vec, sca):
+        op({"v": (lambda: V.tensor_scalar(ap(out), ap(a), *vec), length(out, [a], 50)),
+            "s": (lambda: S.activation(ap(out), ap(a), sca[0], bias=sca[2], scale=sca[1]), length(out, [a], 65, 1.0))}, [a], [out])
+
     def pick(out, win, off, scale=1.0, bias=0.0, split=True, halves=False):
-        if not split and not halves:
+        if _n(out) < C or not (split or halves):
             return lin(out, by(win, off), scale, bias)
         for h in (0, 1):
             lin(cut(out, H * h, H * h + H), by(cut(win, H * h, H * h + H) if halves else win, cut(off, 10 * h, 10 * h + 10)), scale, bias)
@@ -272,10 +325,6 @@ def rank_program(g, core, T, topo):
     def mm(out, lq, ls, rq, rs):
         op({"t": (lambda: g.tensor.matmul_mx(ap(out), ap(lq), ap(ls), ap(rq), ap(rs), True, True), 0.6 * (_n(out) + 16))},
            [lq, ls, rq, rs], [out], "", 60)
-
-    def iota(out, pat, base, mul=0):
-        flt = {} if SCRATCH[out[0]][2] == I32 else {"allow_small_or_imprecise_dtypes": True}
-        op({"g": (lambda: g.iota(ap(out), pat, base, mul, **flt), 130 + 1.66 * _n(out))}, [], [out])
 
     def dma(q, out, a, rd, wr, sem, n=16, late=0):
         e = g.sync if q == "y" else g.scalar
@@ -291,89 +340,97 @@ def rank_program(g, core, T, topo):
 
         def call():
             g.remote_dma(cast(out), cast(a), T.sem[sem], T.sem.sent, pid, rid, mask)
-        op({"g": (call, 300)}, [a], [("r" + out[0], 0, 1, 1)], "far", late)
+        op({"g": (call, 250 if sent[0] > len(topo.engines(core, peer)) else 1400)}, [a], [("r" + out[0], 0, 1, 1)], "far", late)
 
     def arrive(views, sem, n):
         op({"far": (None, 0)}, [("r" + v[0], 0, 1, 1) for v in views], views, "", 0, (sem, n))
 
-    W = {k: whole(k) for k in SCRATCH}
+    W = {k: (k, 0, SCRATCH[k][1][1], 1) for k in SCRATCH}
     ps = [cut(W["ps%d" % b], 0, C) for b in range(8)]
-    fb, ub = [1, 2, 3, 4], [5, 6, 7, 1]
+    fb, ub, wb = [1, 2, 3, 4], [5, 6, 7, 1], [5, 6, 7, 0]
 
-    (loc, k16r, k64r, iom, ios, l32, diag, sig, sigc, keep, keep32, d0s, maskv, mkg, mkl, mkc, mt, nodrep, b3, ks, ks2,
-     fsd) = news("pb", C, "loc k16r k64r iom ios l32 diag sig sigc keep keep32 d0s maskv mkg mkl mkc mt nodrep b3 ks ks2 fsd")
-    iob, tm, tw, th, tl, ti, to, ta, tb = news("pb", 256, "iob tm tw th tl ti to ta tb")
-    t16, srcw = new("pb", 16), new("pb", WW)
+    def parts(key):
+        return [(0, TR)] if OPT[key] == 1 else [(0, TR // 2), (TR // 2, TR)]
+
+    (loc, k64r, iom, ios, l32, diag, sig, sigc, keep, keep32, d0s, maskv, mkg, mkl, mkc, mt, nodrep, b3, ks, ks2,
+     fsd) = news("pb", C, 21)
+    a1, iob, tm, tw, th, to, ta, tb = news("pb", 256, 8)
+    t16, srcw, fs = new("pb", 16), new("pb", WW), new("pb", C + 16)
     col = new("pf", 32)
-    names = "r nr r1 rm1 want cap msend mown o16 vsel m7 k3 te to h t0 r8 r16 r17 rh rm t1 nz".split()
+    names = "r nr r1 rm1 want cap msend mown o16 vsel m7 k3 te to h t0 r8 r16 r17 rh rm t1 nz v1".split()
     cl = {k: cut(col, i, i + 1) for i, k in enumerate(names)}
-    i32, k16n, k32n, self_, kpair, k3 = new("pf", 32), new("pf", TR), new("pf", 10), new("pf", TR), new("pf", TR), new("pf", TR)
+    i32, k32n = new("pf", 32), new("pf", 10)
+    k16n, self_, kpair, k3 = news("pf", TR, 4)
     nodu, invu, tsel, upk = new("pu", TR), new("pu", TR), new("pu", TR), new("pu", 8)
-    (la, lb, lc, cv1, cv2, cv4, m1, m2, m4, mm_, g2, g4, g8, g9, msum, cmp1, scs, strep, pst, cvp, xx, sc1, sc2, kb, cmp2, rk,
-     hi, his, wd, wds, lo, los, b4, ov, osrep, fs0, fs, vb, vs, inv, invs, em, ems, yy, flag, tsc, lnkj, srcj, b2, b1,
-     b1s) = news("pb", C, "la lb lc cv1 cv2 cv4 m1 m2 m4 mm g2 g4 g8 g9 msum cmp1 scs strep pst cvp xx sc1 sc2 kb cmp2 rk "
-                          "hi his wd wds lo los b4 ov osrep fs0 fs vb vs inv invs em ems yy flag tsc lnkj srcj b2 b1 b1s")
-    ssb, neg, oprep, ysb, b1f = news("pf", C, "ssb neg oprep ysb b1f")
-    sn, tt2 = new("pf", C + 32), new("pf", 2 * C + 32)
-    (j0f, j1f, n1, n2, n3, n4, szn, csz, st16, stm, nf, dl, pa, qb, na, own, rel, cg, o2f,
-     pr) = news("pf", TR, "j0f j1f n1 n2 n3 n4 szn csz st16 stm nf dl pa qb na own rel cg o2f pr")
-    (j0, j1, j2, j4, m2u, stu, sou, keyu, idxw, cwu, ou, relu, idxu, tu, cgu, o2u,
-     eu) = news("pu", TR, "j0 j1 j2 j4 m2u stu sou keyu idxw cwu ou relu idxu tu cgu o2u eu")
+    (la, lb, lc, cv1, cv2, cv4, m1, m2, m4, mm_, g2, g4, g8, g9, msum, cmp1, scs, pst, cvp, xx, sc1, sc2, kb, cmp2, rk,
+     hi, his, wd, wds, los, b4, ov, osrep, fs0, vb, vs, inv, invs, em, ems, yy, flag, tsc, lnkj, srcj, b2, b1,
+     b1s) = news("pb", C, 48)
+    ssb, neg, oprep, ysb, b1f, vsf = news("pf", C, 6)
+    sn = {p: new("pf", 16 * (p[1] - p[0]) + 32) for p in parts("st")}
+    tt2 = {p: new("pf", 32 * (p[1] - p[0]) + 32) for p in parts("st")}
+    j0f, j1f, n1, n2, n3, n4, szn, csz, st16, stm, nf, dl, pa, qb, na, own, lon, rel, cg, o2f, pr = news("pf", TR, 21)
+    j0, j1, j2, j4, m2u, stu, sou, keyu, idxw, cwu, ou, relu, idxu, tu, cgu, o2u, eu = news("pu", TR, 17)
     vu = new("pu", 10)
-    snm = cut(sn, 16, C + 16)
+
+    def first(v, like):
+        return cut(v, 0, _n(like))
 
     def seg(out, a, o):
-        scan(out, keep, a, A.mult, o)
+        scan(out, first(keep, a), a, A.mult, o)
 
-    def place(out, a):
-        scan(out, k64r, a, A.max, A.add, -PO)
+    def place(out, a, at):
+        scan(out, at, a, A.max, A.add, -PO)
 
     def take(out, a, mask):
-        scan(out, a, mask, A.max, A.add, -1024.0)
+        scan(out, a, first(mask, a), A.max, A.add, -1024.0)
 
     dma("s", T.pari[:], T.par[:], [], [W["pari"]], "dpar")
-    dma("y", T.ut[:], T.u[:], [], [W["ut"]], "du", 16, 500)
+    dma("y", T.ut[:], T.u[:], [], [W["ut"]], "du", 16, 400)
     dma("s", T.nodi[:], T.nod[:], [], [W["nodi"]], "dnod")
-    dma("y", T.xt[:], T.x[:], [], [W["xt"]], "dx", 16, 1500)
-    dma("y", T.wq[:].bitcast(dt.uint8), T.wc[:], [], [W["wq"]], "dw", 16, 2500)
-    dma("y", T.wsb[:], T.ws[:], [], [W["wsb"]], "dws", 16, 2500)
-    dma("y", T.vt0[:], T.v[:], [], [W["vt0"]], "dv", 16, 3000)
+    for h in (0, 1):
+        dma("y", T.xt[:, 4 * H * h:4 * H * h + 4 * H], T.x[:, 4 * H * h:4 * H * h + 4 * H], [], [cut(W["xt"], 4 * H * h, 4 * H * h + 4 * H)],
+            "dx%d" % h, 16, 900 + 500 * h)
+    dma("y", T.wq[:].bitcast(dt.uint8), T.wc[:], [W["pari"]], [W["wq"]], "dw", 16, 2000)
+    dma("y", T.wsb[:], T.ws[:], [W["pari"]], [W["wsb"]], "dws", 16, 2000)
+    dma("y", T.vt0[:], T.v[:], [W["pari"]], [W["vt0"]], "dv", 16, 2000)
 
     pi, r0, r1 = cut(W["pi"], 0, 1), cut(W["ri"], 0, 1), cut(W["ri"], 1, 2)
+    l256, d256 = cut(loc, 0, 256), cut(diag, 0, 256)
     iota(pi, [[0, 1]], 0, 1)
     iota(i32, [[1, 32]], 0)
     iota(loc, [[0, TR], [1, 16]], 0)
-    iota(k16r, [[16, TR], [0, 16]], 0)
-    mset(W["ebuf"], 0.5)
+    iota(iom, [[1, C]], -int(PO))
+    iota(a1, [[1, 16], [0, 16]], 1)
+    fill(W["ebuf"], 0.5)
     op({"g": (lambda: g.affine_select(T.ebuf[:], T.ebuf[:], [[1, 528]], A.is_equal, 0.0, -3, -4), 1050)}, [W["ebuf"]], [W["ebuf"]])
     iota(iob, [[1, 256]], 0)
     iota(ios, [[1, C]], -int(SO))
-    iota(ks, [[0, C]], 0)
     iota(k64r, [[16, TR], [0, 16]], -int(PO))
     iota(l32, [[0, TR // 2], [1, 32]], 0)
     iota(cut(srcw, C, WW), [[1, VW]], C - int(SO))
-    iota(ks2, [[0, C]], 0)
+    fill(ks, 0.0)
     iota(mt, [[0, C]], -1)
-
-    mset(b3, 1.0)
-    scan(iom, b3, b3, A.mult, A.add, -PO - 1.0)
-    mset(fsd, 0.5)
-    mset(cut(sn, 0, 16), 0.0)
-    mset(cut(sn, C + 16, C + 32), 0.0)
+    iota(fsd, [[0, C]], 16)
+    iota(fs0, [[0, C]], 8)
+    iota(cut(fs, C, C + 16), [[0, 16]], 16)
+    for p in sn:
+        fill(cut(sn[p], 0, 16), 0.0)
+        fill(cut(sn[p], _n(sn[p]) - 16, _n(sn[p])), 0.0)
     ts(r0, pi, 15, A.bitwise_and)
     ts(r1, pi, 16, A.bitwise_and)
     cp(cl["r"], r0)
     cp(cl["h"], r1)
     lin(k16n, cut(i32, 0, TR), 16.0)
     lin(k32n, cut(i32, 0, 10), 32.0)
+    for i in (0, 1):
+        lin(cut(fs0, i, C, 16), k16n, 0.0, 1024.0)
     lin(cl["r16"], cl["r"], 16.0)
     lin(cl["rm1"], cl["r"], 1.0, -1.0)
+    lin(cl["r1"], cl["r"], 1.0, 1.0)
     lin(cl["nr"], cl["r"], -1.0)
     lin(cl["r17"], cl["r"], 17.0)
-    lin(cl["te"], cl["h"], 21.0, cl["r"])
-    lin(cl["to"], cl["h"], -21.0, cl["r"])
     lin(self_, k16n, 1.0, cl["r"])
-    ts(kpair, k16n, -1.0, A.mult, cl["r16"], A.add)
+    lin(kpair, k16n, -1.0, cl["r16"])
     ts(diag, loc, cl["r"], A.is_equal)
     ts(mkl, loc, cl["rm1"], A.is_equal, -512.0, A.mult)
     lin(mkc, diag, 16.0)
@@ -381,10 +438,13 @@ def rank_program(g, core, T, topo):
     lin(ends(mkg), ends(mkg), 1.0, -16.0)
     lin(mkl, mkg, 16.0)
     lin(ends(mkl), ends(mkl), 1.0, -256.0)
-    if OPT["cap"]:
-        lin(mkc, mkl, 2.0)
-    ts(cut(tsel, 0, TR, 2), k32n, cl["te"], A.add)
-    ts(cut(tsel, 1, TR, 2), k32n, cl["to"], A.add, 352.0, A.add)
+    lin(mkc, mkl, 2.0)
+    wide = C // len(sn)
+    lin(cl["te"], cl["h"], wide / 16 + 1.0, cl["r"])
+    lin(cl["to"], cl["h"], -wide / 16 - 1.0, cl["r"])
+    for a, b in sn:
+        ts(cut(tsel, a, b, 2), cut(k32n, 0, (b - a) // 2), cl["te"], A.add)
+        ts(cut(tsel, a + 1, b, 2), cut(k32n, 0, (b - a) // 2), cl["to"], A.add, wide + 32.0, A.add)
     cp(upk, cut(k16n, 0, 8))
     cp(nodu, W["nodi"])
     act(sig, loc, AF.Sign, 1.0, cl["nr"])
@@ -398,7 +458,7 @@ def rank_program(g, core, T, topo):
     take(cv1, lb, mkg)
     tt(n1, self_, j0f, A.subtract)
     act(n2, n1, AF.Relu)
-    ts(n3, self_, -PO, A.add)
+    lin(n3, self_, 1.0, -PO)
     tt(n4, ends(cv1), n3, A.is_equal)
     tt(n1, n4, n2, A.mult)
     tt(j1f, n1, j0f, A.add)
@@ -406,52 +466,51 @@ def rank_program(g, core, T, topo):
     tt(pr, j1f, kpair, A.add)
     cp(m2u, pr)
     pick(la, iom, j1)
-    ts(ta, cut(k16r, 0, 256), cl["r16"], A.is_equal)
-    tt(tm, ta, cut(diag, 0, 256), A.max)
+    ts(ta, a1, cl["r1"], A.is_equal)
+    tt(tm, ta, d256, A.max)
     lin(tm, tm, -2.0, 64.0)
     quant(W["qu0"], W["su0"], W["ut"])
-    quant(W["qx"], W["sx"], W["xt"])
+    for h in (0, 1):
+        quant(cut(W["qx"], H * h, H * h + H), cut(W["sx"], H * h, H * h + H), cut(W["xt"], 4 * H * h, 4 * H * h + 4 * H))
     op({"v": (lambda: V.tensor_copy(T.qu[:].bitcast(dt.uint32), T.qu0[:].bitcast(dt.uint32).indirect(ap(upk))), 220)},
        [W["qu0"], upk], [W["qu"]])
     op({"s": (lambda: S.activation(T.su[:], T.su0[:].indirect(ap(upk)), AF.Copy), 230)}, [W["su0"], upk], [W["su"]])
     for b in range(4):
         quant(cut(W["qe"], 128 * b, 128 * b + 128), cut(W["se"], 128 * b, 128 * b + 128), cut(W["ebuf"], 3 - b, 515 - b))
     cp(by(b3, nodu), iom)
-    tt(b1, b3, diag, A.mult)
-    seg(b1s, b1, A.add)
-    ts(invu, ends(b1s), PO, A.add)
+    take(b1f, b3, mkc)
+    ts(invu, ends(b1f), PO + 512.0, A.add)
     if OPT["sigc"]:
         pick(sigc, sig, invu, split=False)
     pick(nodrep, ios, nodu, split=False)
     lin(t16, cut(i32, 0, 16), 16.0, 16.0)
-    lin(cl["r1"], cl["r"], 1.0, 1.0)
     act(cl["o16"], cl["r16"], AF.Relu, 1.0, -224.0)
     lin(cl["want"], cl["o16"], -0.125, cl["r1"])
     lin(cl["cap"], cl["o16"], -0.125, 16.0)
-    lin(cl["rh"], cl["r"], 0.5, -8.0)
-    lin(cl["rm"], cl["r"], 1.0, -15.5)
-    lin(cl["t0"], cl["r16"], 1.0, -256.0)
-    ts(tw, cut(loc, 0, 256), cl["want"], A.is_equal, 0.0625, A.mult)
-    tt(tw, tw, cut(k16r, 0, 256), A.mult)
-    ts(tw, tw, cl["cap"], A.min)
-    tt(to, cut(diag, 0, 256), cut(k16r, 0, 256), A.mult)
-    tt(tb, ta, cut(loc, 0, 256), A.mult)
-    ts(th, tb, 8.0, A.is_ge)
-    tt(th, th, tb, A.mult)
-    tt(tl, tb, th, A.subtract)
-    lin(th, th, 1.0, cl["r16"])
-    lin(tl, tl, 1.0, cl["r16"])
+    lin(cl["rh"], cl["r"], -8.0, 8.0)
+    lin(cl["t0"], cl["r16"], 1.0, -248.0)
+    ts(tw, l256, cl["want"], A.is_equal)
+    ts(tb, a1, -1.0, A.add, cl["cap"], A.min)
+    tt(tw, tw, tb, A.mult)
+    tt(to, d256, a1, A.mult)
+    act(th, l256, AF.Sign, 1.0, -7.5)
+    tt(ta, ta, l256, A.mult)
+    tt(th, th, ta, A.mult)
     ts(cl["nz"], cl["r"], 1.0, A.min)
-    lin(ti, cut(k16r, 0, 256), -0.0625, 15.0)
-    tt(ti, ti, cut(diag, 0, 256), A.mult)
-    lin(ti, ti, cl["nz"])
     ts(cl["t1"], cl["r"], 14.0, A.not_equal)
     ts(cl["msend"], cl["r"], 7.0, A.is_ge, cl["t1"], A.mult)
     ts(cl["r8"], cl["r"], 8.0, A.is_ge, 8.0, A.mult)
-    ts(keep32, l32, 1.0, A.min)
     lin(cl["mown"], cl["msend"], -1.0, 1.0)
     ts(cl["vsel"], cl["r8"], cl["r"], A.add, 7.0, A.add)
-    ts(maskv, l32, cl["vsel"], A.is_equal)
+    if OPT["vcap"]:
+        lin(cl["v1"], cl["vsel"], 1.0, -1.0)
+        ts(keep32, l32, cl["v1"], A.is_equal, -2048.0, A.mult)
+        ts(maskv, l32, cl["vsel"], A.is_equal, 512.0, A.mult)
+        tt(maskv, maskv, keep32, A.add)
+        lin(cut(maskv, 31, C, 32), k32n, 0.0, -1024.0)
+    else:
+        ts(keep32, l32, 1.0, A.min)
+        ts(maskv, l32, cl["vsel"], A.is_equal)
     lin(cl["k3"], cl["r"], 1.0, C - 7 - PO + 1024.0)
     ts(cl["m7"], cl["r"], 14.0, A.is_lt, cl["msend"], A.mult)
     lin(k3, k16n, 0.5, cl["k3"])
@@ -472,114 +531,114 @@ def rank_program(g, core, T, topo):
     for rnd in range(3):
         peer = T.cores[rank ^ MASKS[rnd]]
         ne = len(topo.engines(peer, core))
-        first, final = rnd == 0, rnd == 2
+        start, final = rnd == 0, rnd == 2
         sa, lda, sb, ldb, qs, ss, ql, sl = (W[k + str(rnd)] for k in ("sa", "la", "sb", "lb", "qs", "ss", "ql", "sl"))
 
-        mm(ps[0], W["qu"], W["su"], W["qx"], W["sx"])
         for b in range(4):
             mm(ps[fb[b]], block("qe", b, 128), block("se", b, 128), W["qx"], W["sx"])
             lin(plane(b), ps[fb[b]])
         for b in (0, 1):
-            lin(block("fo", b, C), plane(b))
+            dma("y", ap(block("fo", b, C)), ap(plane(b)), [plane(b)], [block("fo", b, C)], "df" + "ab"[b] + str(rnd))
 
-        pick(lb, la, j1, split=first)
-        pick(m1, tm, m2u, split=first)
+        pick(lb, la, j1, split=start)
+        pick(m1, tm, m2u, split=start)
         take(cv2, lb, mkg)
         ts(j2, ends(cv2), PO, A.add)
-        pick(lc, lb, j2, split=first)
-        pick(g2, m1, j2, -1.0, 192.0, split=first)
+        pick(lc, lb, j2, split=start)
+        pick(g2, m1, j2, -1.0, 192.0, split=start)
         take(cv4, lc, mkg)
         ts(j4, ends(cv4), PO, A.add)
         scan(m2, g2, m1, A.max, A.subtract)
-        pick(g4, m2, j4, -1.0, 192.0, split=first)
+        pick(g4, m2, j4, -1.0, 192.0, split=start)
         scan(m4, g4, m2, A.max, A.subtract)
-        pick(g8, m4, j4, split=first)
-        pick(g9, g8, j4, -1.0, 127.0, split=first)
+        pick(g8, m4, j4, split=start)
+        pick(g9, g8, j4, -1.0, 127.0, split=start)
         scan(mm_, g9, m4, A.max, A.subtract)
         seg(msum, mm_, A.add)
         lin(szn, ends(msum), 0.5, 8.0)
         lin(csz, ends(msum), -0.5, 8.0)
 
-        if OPT["sigc"] and not first:
-            tt(ssb, ps[0], sigc, A.mult)
-            pick(snm, ssb, nodu)
-        else:
-            lin(ssb, ps[0])
-            tt(snm, by(ssb, nodu), sig, A.mult)
-        lin(neg, snm, -1.0)
-        turn(cut(tt2, 0, C), snm)
-        turn(cut(tt2, C, 2 * C + 32), sn)
-        tt(cmp1, by(tt2, tsel), neg, A.is_gt)
-        scan(scs, d0s, cmp1, A.mult, A.add)
-        ts(stu, ends(scs), cl["r"], A.add)
+        signed = OPT["sigc"] and not start
+        for c, d in parts("sc"):
+            R, out = (lambda v: cut(v, 16 * c, 16 * d)), cut(ps[0 if d == TR else 5], 0, 16 * (d - c))
+            mm(out, W["qu"], W["su"], R(W["qx"]), R(W["sx"]))
+            if signed:
+                tt(R(ssb), out, R(sigc), A.mult)
+            else:
+                lin(R(ssb), out)
+        for a, b in parts("st"):
+            R, N, n = (lambda v: cut(v, 16 * a, 16 * b)), (lambda v: cut(v, a, b)), 16 * (b - a)
+            snm, both = cut(sn[a, b], 16, n + 16), tt2[a, b]
+            if signed:
+                pick(snm, ssb, N(nodu))
+            else:
+                tt(snm, by(ssb, N(nodu)), R(sig), A.mult)
+            lin(R(neg), snm, -1.0)
+            turn(cut(both, 0, n), snm)
+            turn(cut(both, n, 2 * n + 32), sn[a, b])
+            tt(R(cmp1), by(both, N(tsel)), R(neg), A.is_gt)
+            scan(R(scs), R(d0s), R(cmp1), A.mult, A.add)
+            ts(N(stu), ends(R(scs)), cl["r"], A.add)
         ts(sou, ends(scs), cl["r17"], A.add)
         lin(st16, ends(scs), 16.0, cl["t0"])
-        lin(stm, ends(scs), 1.0, cl["rm"])
-        lin(starts(fsd), ends(scs), 0.5, cl["rh"])
-        pick(strep, t16, stu, 1.0, -16.0, split=False)
-        pick(pst, strep, j1, split=False)
-        take(cvp, pst, mkl)
-        tt(dl, ends(cvp), st16, A.subtract)
+        lin(cut(fsd, 1, C, 16), ends(scs), -8.0, cl["rh"])
 
-        tt(xx, by(t16, stu), mm_, A.mult)
-        seg(sc1, xx, A.max)
-        seg(sc2, xx, A.min)
-        tt(n1, ends(sc1), szn, A.add)
-        tt(n2, csz, ends(sc2), A.subtract)
-        tt(starts(ks), n1, n2, A.min)
-        ts(keyu, starts(ks), 0.0, A.add)
-        seg(kb, ks, A.add)
-        tt(cmp2, by(iob, keyu), kb, A.is_lt)
-        seg(rk, cmp2, A.add)
-        act(nf, ends(sc2), AF.Relu, -1.0, -255.0)
-        tt(pa, nf, dl, A.mult)
-        tt(qb, pa, st16, A.add)
-        tt(na, ends(rk), qb, A.add)
-        ts(idxw, na, 256.0, A.add)
-        pick(hi, th, idxw)
-        seg(his, hi, A.max)
+        for a, b in parts("wd"):
+            R, N = (lambda v: cut(v, 16 * a, 16 * b)), (lambda v: cut(v, a, b))
+            tt(R(xx), by(t16, N(stu)), R(mm_), A.mult)
+            pick(R(pst), cut(xx, 0, 16 * b), N(j1), -1.0, -8.0, split=False)
+            take(R(cvp), R(pst), mkl)
+            tt(N(dl), ends(R(cvp)), N(st16), A.subtract)
+            seg(R(sc1), R(xx), A.max)
+            seg(R(sc2), R(xx), A.min)
+            tt(N(n1), ends(R(sc1)), N(szn), A.add)
+            tt(N(n2), N(csz), ends(R(sc2)), A.subtract)
+            tt(starts(R(ks)), N(n1), N(n2), A.min)
+            ts(N(keyu), starts(R(ks)), 0.0, A.add)
+            seg(R(kb), R(ks), A.add)
+            tt(R(cmp2), by(iob, N(keyu)), R(kb), A.is_lt)
+            seg(R(rk), R(cmp2), A.add)
+            act(N(nf), ends(R(sc2)), AF.Relu, -1.0, -255.0)
+            tt(N(pa), N(nf), N(dl), A.mult)
+            tt(N(qb), N(pa), N(st16), A.add)
+            tt(N(na), ends(R(rk)), N(qb), A.add)
+            ts(N(idxw), N(na), 248.0, A.add)
+            pick(R(hi), th, N(idxw))
+            seg(R(his), R(hi), A.max)
         lin(sa, ends(his))
         remote(lda, sa, "aa%d" % rnd, peer, 0)
         pick(wd, tw, idxw)
-        place(wds, wd)
+        place(wds, wd, k64r)
         lin(sb, ends(wds), cl["msend"])
         remote(ldb, sb, "ab%d" % rnd, peer, 0)
 
-        pick(lo, tl, idxw, split=False)
-        seg(los, lo, A.max)
-        pick(b4, to, sou, 0.0625, split=False)
-        place(ov, b4)
-        ts(ou, ends(ov), PO, A.add)
+        seg(los, hi, A.min)
+        lin(lon, ends(los), -1.0)
+        pick(b4, to, sou, split=False)
+        place(ov, b4, k64r)
+        ts(ou, ends(ov), PO - 1.0, A.add)
         pick(cut(srcw, 0, C), nodrep, ou, split=False)
         pick(osrep, loc if final else iom, ou, split=False)
-        seg(fs0, fsd, A.add)
-        ts(fs, fs0, -1.0, A.max, 0.0, A.min)
+        scan(cut(fs, 0, C), fs0, fsd, A.add, A.min)
         ts(cwu, ends(wds), PO, A.add)
         lin(own, ends(wds), cl["mown"])
-        tt(vb, by(cut(srcw, 0, C), cwu), maskv, A.mult)
-        scan(vs, keep32, vb, A.mult, A.add)
-        ts(vu, cut(vs, 31, C, 32), SO, A.add)
+        if OPT["vcap"]:
+            pick(vb, cut(srcw, 0, C), cwu)
+            take(vsf, vb, maskv)
+            ts(vu, cut(vsf, 31, C, 32), SO + 512.0, A.add)
+        else:
+            tt(vb, by(cut(srcw, 0, C), cwu), maskv, A.mult)
+            scan(vs, keep32, vb, A.mult, A.add)
+            ts(vu, cut(vs, 31, C, 32), SO, A.add)
         for b in range(4):
             lin(lane("vt", b), by(plane(b), vu), 2.0)
         quant(qs, ss, W["vt"])
-        remote(ql, qs, "av%d" % rnd, peer, 1200)
+        remote(ql, qs, "av%d" % rnd, peer, 1100)
         remote(sl, ss, "av%d" % rnd, peer, 400)
 
         arrive([lda], "aa%d" % rnd, ne)
         arrive([ldb], "ab%d" % rnd, ne)
         arrive([ql, sl], "av%d" % rnd, 2 * ne)
-        tt(rel, ends(los), lda, A.max)
-        cp(relu, rel)
-        pick(inv, ti, relu)
-        place(invs, inv)
-        ts(idxu, ends(invs), PO, A.add)
-        pick(em, fs, idxu)
-        seg(ems, em, A.add)
-        tt(starts(ks2), stm, ends(ems), A.subtract)
-        scan(yy, ks2, em, A.max, A.add)
-        ts(flag, yy, -0.5, A.not_equal, 15.0, A.mult)
-        scan(tsc, flag, mt, A.min, A.add, 64.0)
-        ts(tu, ends(tsc), -16.0, A.add)
         tt(cg, own, ldb, A.add)
         tt(o2f, cg, k3, A.max)
         ts(o2u, o2f, PO, A.add)
@@ -588,6 +647,21 @@ def rank_program(g, core, T, topo):
         pick(lnkj, osrep, cgu, split=False)
         if not final:
             lin(ends(lnkj), ends(osrep))
+        tt(rel, lon, lda, A.max)
+        ts(relu, rel, cl["r16"], A.add)
+        for a, b in parts("dec"):
+            R, N = (lambda v: cut(v, 16 * a, 16 * b)), (lambda v: cut(v, a, b))
+            pick(R(inv), to, N(relu), cl["nz"])
+            place(R(invs), R(inv), R(k64r))
+            ts(N(idxu), ends(R(invs)), PO, A.add)
+            for c, d in ((a, b),) if b - a < TR else ((0, TR // 2), (TR // 2, TR)):
+                either(cut(em, 16 * c, 16 * d), by(fs, cut(idxu, c, d)), (0.0, None, A.max), (AF.Relu, 1.0, 0.0))
+            seg(R(ems), R(em), A.add)
+            tt(starts(R(ks)), N(st16), ends(R(ems)), A.add)
+            scan(R(yy), R(ks), R(em), A.max, A.subtract)
+            either(R(flag), R(yy), (-8.0, 15.0, A.not_equal, A.mult), (AF.Abs, 2.0, 16.0))
+            scan(R(tsc), R(flag), R(mt), A.min, A.add, 64.0)
+            ts(N(tu), ends(R(tsc)), -16.0, A.add)
         for b in range(4):
             mm(cut(ps[ub[b]], 0, VW), block("qe", b, 128), block("se", b, 128), ql, sl)
             lin(cut(W["win"], WW * b + C, WW * b + WW), cut(ps[ub[b]], 0, VW))
@@ -609,33 +683,39 @@ def rank_program(g, core, T, topo):
             tt(pr, ends(cv1), kpair, A.add)
             ts(m2u, pr, PO, A.add)
 
-        for b in (3, 2):
-            lin(block("hh", b - 2, C), by(block("win", b, WW), eu))
-        for b in (0, 1):
-            tt(lane("zt", b), by(block("win", b, WW), eu), block("fo", b, C), A.add)
-        for b in (3, 2):
-            tt(lane("zt", b), block("hh", b - 2, C), ps[fb[b]], A.add)
-        for b in range(4):
-            lin(block("z32", b, C), lane("zt", b), 32.0)
-        quant(W["qz"], W["sz"], W["zt"])
-        for b in range(4):
-            mm(ps[fb[b]], block("wq", b, 128), block("wsb", b, 128), W["qz"], W["sz"])
-        for b in range(4):
-            tt(block("x32", b, C), ps[fb[b]], block("z32", b, C), A.add)
-            lin(lane("xt", b), block("x32", b, C), 0.03125)
-        quant(W["qx"], W["sx"], W["xt"])
+        for c, d in parts("bl"):
+            R, L = (lambda v: cut(v, 16 * c, 16 * d)), (lambda k, b: cut(W[k], 64 * c + b, 64 * d, 4))
+            for b in (3, 2):
+                lin(R(block("hh", b - 2, C)), by(block("win", b, WW), cut(eu, c, d)))
+            for b in (0, 1):
+                tt(L("zt", b), by(block("win", b, WW), cut(eu, c, d)), R(block("fo", b, C)), A.add)
+            for b in (3, 2):
+                tt(L("zt", b), R(block("hh", b - 2, C)), R(ps[fb[b]]), A.add)
+            for b in range(4):
+                lin(R(block("z32", b, C)), L("zt", b), 32.0)
+            quant(R(W["qz"]), R(W["sz"]), cut(W["zt"], 64 * c, 64 * d))
+        for c, d in parts("xl"):
+            R, L = (lambda v: cut(v, 16 * c, 16 * d)), (lambda k, b: cut(W[k], 64 * c + b, 64 * d, 4))
+            for b in range(4):
+                out = cut(ps[(fb if d == TR else wb)[b]], 0, 16 * (d - c))
+                mm(out, block("wq", b, 128), block("wsb", b, 128), R(W["qz"]), R(W["sz"]))
+                tt(R(block("x32", b, C)), out, R(block("z32", b, C)), A.add)
+                lin(L("xt", b), R(block("x32", b, C)), 0.03125)
+            quant(R(W["qx"]), R(W["sx"]), cut(W["xt"], 64 * c, 64 * d))
 
-    dma("y", T.oc[:], T.qx[:].bitcast(dt.uint8), [W["qx"]], [], "doc", 16, 1000)
     for h in (0, 1):
+        dma("y", T.oc[:, 4 * H * h:4 * H * h + 4 * H], ap(block("qx", h, H)).bitcast(dt.uint8), [block("qx", h, H)], [], "doc", 32, 500)
         half = cut(ysb, H * h, H * h + H)
         mm(cut(ps[5 + h], 0, H), W["qv"], W["sv"], block("qx", h, H), block("sx", h, H))
         lin(half, cut(ps[5 + h], 0, H))
         dma("ys"[h], T.y[:, H * h:H * h + H], ap(half), [half], [], "dy%d" % h, 16, 500)
     for k in range(4):
         dma("y", T.osc[4 * k:4 * k + 4, :], T.sx[32 * k:32 * k + 4, :], [W["sx"]], [], "dos", 64)
-    deps = _needs(ops)
-    _emit(g, T, ops, deps, _order(ops, deps))
-    for s, n in (("dop", 16), ("doc", 16), ("dos", 64), ("dy0", 16)):
+    if not CHOSEN:
+        deps = _needs(ops)
+        CHOSEN.extend([deps, _order(ops, deps)])
+    _emit(g, T, ops, *CHOSEN)
+    for s, n in (("dop", 16), ("doc", 32), ("dos", 64), ("dy0", 16)):
         g.sync.wait_ge(T.sem[s], n)
     g.scalar.wait_ge(T.sem.dy1, 16)
     g.wait_ge(T.sem.sent, sent[0])

@@ -6,11 +6,11 @@ AF = ActivationFunctionType
 C, TR, VW = 320, 20, 160
 WW = C + VW
 H = C // 2
+WHOLE, HALVES = ((0, TR),), ((0, TR // 2), (TR // 2, TR))
 PO, SO = 64.0, 224.0
 MASKS = [1, 2, 4]
-Q4, U8, BF, F32, I32, U16 = "float8_e4m3fn_x4", "uint8", "bfloat16", "float32", "int32", "uint16"
-OPT = {"sigc": True, "cap": True, "vcap": True, "st": 1, "wd": 1, "dec": 2, "bl": 1, "xl": 2, "sc": 2,
-       "tries": 60, "turns": 6, "mend": 8000}
+Q4, U8, BF, F16, F32, I32, U16 = "float8_e4m3fn_x4", "uint8", "bfloat16", "float16", "float32", "int32", "uint16"
+OPT = {"seed": 1, "tries": 10, "turns": 6, "mend": 6000, "give": 150}
 
 SCRATCH = {}
 
@@ -25,11 +25,13 @@ _decl(U8, sx=C, sz=C, su0=128, su=128, sv=128, wsb=512, se=512)
 for _r in range(3):
     _decl(Q4, **{"qs%d" % _r: VW, "ql%d" % _r: VW})
     _decl(U8, **{"ss%d" % _r: VW, "sl%d" % _r: VW})
-    _decl(BF, **{n % _r: TR for n in ("sa%d", "la%d", "sb%d", "lb%d")})
+    _decl(U16, **{"sa%d" % _r: TR, "la%d" % _r: TR})
+    _decl(BF, **{"sb%d" % _r: TR, "lb%d" % _r: TR})
 _decl(BF, xt=4 * C, zt=4 * C, z32=4 * C, x32=4 * C, ut=512, vt0=512, ebuf=528, win=4 * WW, vt=4 * VW, hh=2 * C, fo=2 * C)
 _decl(I32, pi=2, ri=2, nodi=TR, pari=TR)
-_decl(BF, pb=28672)
-_decl(F32, pf=6144)
+_decl(BF, pb=32768)
+_decl(F16, ph=C)
+_decl(F32, pf=4608)
 _decl(U16, pu=1024)
 for _b in range(8):
     SCRATCH["ps%d" % _b] = ("psum", [128, 512], F32)
@@ -37,7 +39,8 @@ for _b in range(8):
 _DMAS = ["dx0", "dx1", "du", "dw", "dws", "dv", "dpar", "dnod", "dop", "doc", "dos", "dy0", "dy1"]
 SEMAPHORES = ["cv", "cs", "ct", "cg", "sent"] + _DMAS + [n + str(r) for n in ("aa", "ab", "av", "dfa", "dfb") for r in range(3)]
 
-TUNES = ((1.0, 60, 1400, 1400), (0.75, 110, 1100, 1200), (1.25, 45, 1900, 1600), (1.0, 80, 700, 700))
+TUNES = ((1.0, (210, 210), 1100, 1300, 1.0), (0.8, (150, 290), 900, 1000, 0.8), (1.2, (240, 150), 1500, 1700, 1.4),
+         (1.0, (120, 140), 1200, 1300, 1.0))
 CHOSEN = []
 
 
@@ -71,32 +74,50 @@ def _needs(ops):
 
 
 def _order(ops, deps):
-    users = [[] for o in ops]
+    count, users = len(ops), [[] for o in ops]
     for n, d in enumerate(deps):
         for m in d:
             users[m].append(n)
 
-    def lengths(pick, hop, far, load):
+    def lengths(pick, hop, far, load, slow):
         cost = [{q: c[1] * (pick if o["pick"] else 1.0) for q, c in o["q"].items()} for o in ops]
-        late = [o["late"] + (far if o["kind"] == "far" else load if o["kind"] == "dma" else 0) for o in ops]
+        late = [o["late"] * slow + (far if o["kind"] == "far" else load if o["kind"] == "dma" else 0) for o in ops]
         return cost, late, hop
 
     tunes = [lengths(*k) for k in TUNES]
 
     def replay(order, cost, late, hop):
-        done, free = [0] * len(ops), {}
+        done, why, free, last, on = [0] * count, [None] * count, {}, {}, [None] * count
         for n, q in order:
-            t = max([free.get(q, 0)] + [done[m] + hop for m in deps[n]])
-            free[q] = t + cost[n][q]
+            t, w = free.get(q, 0), (last.get(q), True)
+            for m in deps[n]:
+                if done[m] + hop[on[m] != q] > t:
+                    t, w = done[m] + hop[on[m] != q], (m, False)
+            free[q], last[q], why[n], on[n] = t + cost[n][q], n, w, q
             done[n] = free[q] + late[n]
-        return max(done)
+        n, chain = max(range(count), key=lambda n: done[n]), []
+        end = done[n]
+        while n is not None:
+            if why[n][1] and why[n][0] is not None:
+                chain.append((why[n][0], n))
+            n = why[n][0]
+        return end, chain
 
-    def lay(seq, before, back, spare, cost, late, hop):
-        done, at, busy = [0] * len(ops), [None] * len(ops), {}
-        for n in seq:
-            t = max([0] + [done[m] + hop for m in before[n]]) + (late[n] if back else 0)
+    def judge(order, bound):
+        ends, total = [], 0
+        for k in tunes:
+            ends.append(replay(order, *k))
+            total += ends[-1][0]
+            if bound and total > sum(bound[:len(ends)]) + OPT["give"]:
+                return None
+        return ends
+
+    def lay(way, before, back, spare, cost, late, hop):
+        done, at, busy = [0] * count, [None] * count, {}
+        for n in sorted(range(count), key=lambda n: -way[n]):
             best = None
             for q, c in cost[n].items():
+                t = max([0] + [done[m] + hop[at[m][1] != q] for m in before[n]]) + (late[n] if back else 0)
                 s, l = t, busy.setdefault(q, [])
                 i = len(l)
                 while i and l[i - 1][1] > t:
@@ -109,62 +130,42 @@ def _order(ops, deps):
             s, q, i = best[1:]
             busy[q].insert(i, (s, s + cost[n][q]))
             at[n], done[n] = (s, q), s + cost[n][q] + (0 if back else late[n])
-        return at, done
+        return [(n, at[n][1]) for n in sorted(range(count), key=lambda n: at[n][0])], done
 
-    rng, best = np.random.RandomState(1), None
+    rng, best = np.random.RandomState(OPT["seed"]), None
     for attempt in range(OPT["tries"]):
         tune = tunes[attempt % len(tunes)]
         cost, late, hop = tune
-        shake, spare = 1.0 + (0.3 if attempt else 0.0) * (rng.rand(len(ops)) - 0.5), 4.0 * rng.rand()
-        way = [0] * len(ops)
-        for n in range(len(ops) - 1, -1, -1):
-            way[n] = 1 + (min(cost[n].values()) + late[n]) * shake[n] + max([way[m] + hop for m in users[n]] + [0])
+        shake, spare = 1.0 + (0.3 if attempt else 0.0) * (rng.rand(count) - 0.5), 4.0 * rng.rand()
+        way = [0] * count
+        for n in range(count - 1, -1, -1):
+            way[n] = 1 + (min(cost[n].values()) + late[n]) * shake[n] + max([way[m] + hop[0] for m in users[n]] + [0])
         for turn in range(OPT["turns"]):
-            at, done = lay(sorted(range(len(ops)), key=lambda n: -way[n]), deps, False, spare, *tune)
-            out = [(n, at[n][1]) for n in sorted(range(len(ops)), key=lambda n: at[n][0])]
-            end = sum(replay(out, *k) for k in tunes)
+            out, done = lay(way, deps, False, spare, *tune)
+            end = sum(e[0] for e in judge(out, None))
             if best is None or end < best[0]:
                 best = (end, out)
-            way = lay(sorted(range(len(ops)), key=lambda n: -done[n]), users, True, spare, *tune)[1]
-    return _mend(best[1], best[0], deps, users, tunes, rng)
+            way = lay(done, users, True, spare, *tune)[1]
 
-
-def _mend(order, score, deps, users, tunes, rng):
-    def replay(order, cost, late, hop):
-        done, why, free, last = [0] * len(order), [None] * len(order), {}, {}
-        for n, q in order:
-            t, w = free.get(q, 0), (last.get(q), True)
-            for m in deps[n]:
-                if done[m] + hop > t:
-                    t, w = done[m] + hop, (m, False)
-            free[q], last[q], why[n] = t + cost[n][q], n, w
-            done[n] = free[q] + late[n]
-        n, chain = max(range(len(order)), key=lambda n: done[n]), []
-        end = done[n]
-        while n is not None:
-            if why[n][1] and why[n][0] is not None:
-                chain.append((why[n][0], n))
-            n = why[n][0]
-        return end, chain
-
-    chains = [replay(order, *k)[1] for k in tunes]
+    order = best[1]
+    ends = judge(order, None)
     for step in range(OPT["mend"]):
-        chain = chains[rng.randint(len(chains))]
+        chain = ends[rng.randint(len(ends))][1]
         m, n = chain[rng.randint(len(chain))]
         at = {k[0]: i for i, k in enumerate(order)}
         a, b, trial, how = at[m], at[n], list(order), rng.randint(4)
         if how == 0 and max([at[d] for d in deps[n]] + [-1]) < a:
             trial.insert(a, trial.pop(b))
-        elif how == 1 and min([at[d] for d in users[m]] + [len(order)]) > b:
+        elif how == 1 and min([at[d] for d in users[m]] + [count]) > b:
             trial.insert(b, trial.pop(a))
-        elif how > 1 and len(tunes[0][0][(m, n)[how - 2]]) > 1:
+        elif how > 1 and len(ops[(m, n)[how - 2]]["q"]) > 1:
             i = (a, b)[how - 2]
-            trial[i] = (trial[i][0], [q for q in tunes[0][0][trial[i][0]] if q != trial[i][1]][0])
+            trial[i] = (trial[i][0], [q for q in ops[trial[i][0]]["q"] if q != trial[i][1]][0])
         else:
             continue
-        ends = [replay(trial, *k) for k in tunes]
-        if sum(e[0] for e in ends) <= score:
-            order, score, chains = trial, sum(e[0] for e in ends), [e[1] for e in ends]
+        now = judge(trial, [e[0] for e in ends])
+        if now and sum(e[0] for e in now) <= sum(e[0] for e in ends):
+            order, ends = trial, now
     return order
 
 
@@ -233,6 +234,9 @@ def rank_program(g, core, T, topo):
     def by(win, off):
         return ("by", win, off)
 
+    def trees(a, b):
+        return (lambda v: cut(v, 16 * a, 16 * b)), (lambda v: cut(v, a, b))
+
     def ap(v):
         if not isinstance(v, tuple):
             return v
@@ -258,7 +262,7 @@ def rank_program(g, core, T, topo):
         if ins[0][0] == "by":
             return base + 1.3 * n
         if rate is None:
-            rate = 0.5 if all(SCRATCH[v[0]][2] in (BF, U16) for v in ins + [out]) else 1.0
+            rate = 0.5 if all(SCRATCH[v[0]][2] in (BF, F16, U16) for v in ins + [out]) else 1.0
         return 0.83 * max(64, n * rate)
 
     def ts(out, a, s1, o0, s2=None, o1=None):
@@ -278,18 +282,15 @@ def rank_program(g, core, T, topo):
     def turn(out, a):
         op({"v": (lambda: V.transpose(ap(out), ap(a)), length(out, [a], 50))}, [a], [out])
 
-    def ramp(out, pat, base, mul=0):
-        flt = {} if SCRATCH[out[0]][2] == I32 else {"allow_small_or_imprecise_dtypes": True}
-        return (lambda: g.iota(ap(out), pat, base, mul, **flt), 130 + 1.66 * _n(out))
+    def mset(out, c):
+        op({"v": (lambda: V.memset(ap(out), c), length(out, [out], 50))}, [], [out])
 
     def iota(out, pat, base, mul=0):
-        op({"g": ramp(out, pat, base, mul)}, [], [out])
+        flt = {} if SCRATCH[out[0]][2] == I32 else {"allow_small_or_imprecise_dtypes": True}
+        op({"g": (lambda: g.iota(ap(out), pat, base, mul, **flt), 130 + 1.66 * _n(out))}, [], [out])
 
     def fill(out, c):
-        q = {"v": (lambda: V.memset(ap(out), c), length(out, [out], 50))}
-        if c == int(c):
-            q["g"] = ramp(out, [[0, _n(out)]], int(c))
-        op(q, [], [out])
+        iota(out, [[0, _n(out)]], c)
 
     def act(out, a, fn, scale=1.0, bias=0.0):
         op({"s": (lambda: S.activation(ap(out), ap(a), fn, bias=ap(bias), scale=ap(scale)), length(out, [a], 65, 1.0))},
@@ -313,11 +314,14 @@ def rank_program(g, core, T, topo):
         op({"v": (lambda: V.tensor_scalar(ap(out), ap(a), *vec), length(out, [a], 50)),
             "s": (lambda: S.activation(ap(out), ap(a), sca[0], bias=sca[2], scale=sca[1]), length(out, [a], 65, 1.0))}, [a], [out])
 
-    def pick(out, win, off, scale=1.0, bias=0.0, split=True, halves=False):
-        if _n(out) < C or not (split or halves):
-            return lin(out, by(win, off), scale, bias)
-        for h in (0, 1):
-            lin(cut(out, H * h, H * h + H), by(cut(win, H * h, H * h + H) if halves else win, cut(off, 10 * h, 10 * h + 10)), scale, bias)
+    def same(out, a, c):
+        act(out, a, AF.Abs, -1.0, c)
+        act(out, out, AF.Relu, -1.0, 1.0)
+
+    def pick(out, win, off, local=False):
+        for a, b in HALVES:
+            R, N = trees(a, b)
+            lin(R(out), by(R(win) if local else win, N(off)))
 
     def quant(q, s, a):
         op({"v": (lambda: V.quantize_mx(ap(q), ap(s), ap(a)), 12 + 0.22 * _n(a))}, [a], [q, s])
@@ -349,47 +353,40 @@ def rank_program(g, core, T, topo):
     ps = [cut(W["ps%d" % b], 0, C) for b in range(8)]
     fb, ub, wb = [1, 2, 3, 4], [5, 6, 7, 1], [5, 6, 7, 0]
 
-    def parts(key):
-        return [(0, TR)] if OPT[key] == 1 else [(0, TR // 2), (TR // 2, TR)]
-
-    (loc, k64r, iom, ios, l32, diag, sig, sigc, keep, keep32, d0s, maskv, mkg, mkl, mkc, mt, nodrep, b3, ks, ks2,
-     fsd) = news("pb", C, 21)
-    a1, iob, tm, tw, th, to, ta, tb = news("pb", 256, 8)
-    t16, srcw, fs = new("pb", 16), new("pb", WW), new("pb", C + 16)
+    loc, k64r, iom, ios, l32, diag, sig, sigc, keep, d0s, keep32, mkg, mkl, mkc, mt, nodrep, b3, ks, fsd, fs0 = news("pb", C, 20)
+    a1, iob, tm, to, ta, tb, tc, td = news("pb", 256, 8)
+    thw, tww, tvw = news("pb", 512, 3)
+    th, tw, te, tf = cut(thw, 0, 256), cut(tww, 0, 256), cut(tvw, 0, 256), cut(tvw, 256, 512)
+    t16, srcw, fs, w2 = new("pb", 16), new("pb", WW), new("pb", C + 16), new("pb", 8 * C)
     col = new("pf", 32)
-    names = "r nr r1 rm1 want cap msend mown o16 vsel m7 k3 te to h t0 r8 r16 r17 rh rm t1 nz v1".split()
+    names = "r nr r1 rm1 want cap cap1 msend mown o16 vsel v1 m7 k3 te to h t0 r8 rm8 r16 r17 rh t1 nz s7 s14 a14".split()
     cl = {k: cut(col, i, i + 1) for i, k in enumerate(names)}
-    i32, k32n = new("pf", 32), new("pf", 10)
-    k16n, self_, kpair, k3 = news("pf", TR, 4)
+    i32, k32n, d16, mh = new("pf", 32), new("pf", 10), new("pf", 16), new("pf", C)
+    k16n, self_, kpair, k3, kq = news("pf", TR, 5)
     nodu, invu, tsel, upk = new("pu", TR), new("pu", TR), new("pu", TR), new("pu", 8)
-    (la, lb, lc, cv1, cv2, cv4, m1, m2, m4, mm_, g2, g4, g8, g9, msum, cmp1, scs, pst, cvp, xx, sc1, sc2, kb, cmp2, rk,
-     hi, his, wd, wds, los, b4, ov, osrep, fs0, vb, vs, inv, invs, em, ems, yy, flag, tsc, lnkj, srcj, b2, b1,
-     b1s) = news("pb", C, 48)
-    ssb, neg, oprep, ysb, b1f, vsf = news("pf", C, 6)
-    sn = {p: new("pf", 16 * (p[1] - p[0]) + 32) for p in parts("st")}
-    tt2 = {p: new("pf", 32 * (p[1] - p[0]) + 32) for p in parts("st")}
-    j0f, j1f, n1, n2, n3, n4, szn, csz, st16, stm, nf, dl, pa, qb, na, own, lon, rel, cg, o2f, pr = news("pf", TR, 21)
-    j0, j1, j2, j4, m2u, stu, sou, keyu, idxw, cwu, ou, relu, idxu, tu, cgu, o2u, eu = news("pu", TR, 17)
-    vu = new("pu", 10)
-
-    def first(v, like):
-        return cut(v, 0, _n(like))
+    (la, lb, lc, cv1, cv2, cv4, m1, m2, m4, mm_, g2, g4, g8, g9, msum, cmp1, scs, pst, cvp, xx, sc1, sc2, kb, cmp2, rk, hi,
+     wd, wds, los, b4, ov, osrep, pcol, vb, vs, inv, invs, em, ems, yy, flag, tsc, lnkj, srcj, b2, b1) = news("pb", C, 46)
+    ssb, neg, his, oprep, ysb = news("pf", C, 5)
+    sn, both = {p: new("pf", H + 32) for p in HALVES}, {p: new("pf", C + 32) for p in HALVES}
+    j0f, j1f, n1, n2, n3, n4, szn, csz, st16, stq, nf, dl, pa, qb, na, dj, pj, pn, own, cg, o2f, pr = news("pf", TR, 22)
+    j0, j1, j2, j4, m2u, stu, sou, keyu, idxw, pnu, lou, ou, idxu, tu, cgu, o2u, eu = news("pu", TR, 17)
+    vu, b1h = new("pu", 10), W["ph"]
 
     def seg(out, a, o):
-        scan(out, first(keep, a), a, A.mult, o)
+        scan(out, cut(keep, 0, _n(a)), a, A.mult, o)
 
     def place(out, a, at):
         scan(out, at, a, A.max, A.add, -PO)
 
     def take(out, a, mask):
-        scan(out, a, first(mask, a), A.max, A.add, -1024.0)
+        scan(out, a, mask, A.max, A.add, -1024.0)
 
     dma("s", T.pari[:], T.par[:], [], [W["pari"]], "dpar")
     dma("y", T.ut[:], T.u[:], [], [W["ut"]], "du", 16, 400)
     dma("s", T.nodi[:], T.nod[:], [], [W["nodi"]], "dnod")
     for h in (0, 1):
-        dma("y", T.xt[:, 4 * H * h:4 * H * h + 4 * H], T.x[:, 4 * H * h:4 * H * h + 4 * H], [], [cut(W["xt"], 4 * H * h, 4 * H * h + 4 * H)],
-            "dx%d" % h, 16, 900 + 500 * h)
+        half = cut(W["xt"], 4 * H * h, 4 * H * h + 4 * H)
+        dma("y", ap(half), T.x[:, half[1]:half[2]], [], [half], "dx%d" % h, 16, 900 + 500 * h)
     dma("y", T.wq[:].bitcast(dt.uint8), T.wc[:], [W["pari"]], [W["wq"]], "dw", 16, 2000)
     dma("y", T.wsb[:], T.ws[:], [W["pari"]], [W["wsb"]], "dws", 16, 2000)
     dma("y", T.vt0[:], T.v[:], [W["pari"]], [W["vt0"]], "dv", 16, 2000)
@@ -398,24 +395,26 @@ def rank_program(g, core, T, topo):
     l256, d256 = cut(loc, 0, 256), cut(diag, 0, 256)
     iota(pi, [[0, 1]], 0, 1)
     iota(i32, [[1, 32]], 0)
-    iota(loc, [[0, TR], [1, 16]], 0)
+    mset(keep, 1.0)
+    mset(starts(keep), 0.0)
+    scan(loc, keep, keep, A.mult, A.add)
     iota(iom, [[1, C]], -int(PO))
     iota(a1, [[1, 16], [0, 16]], 1)
-    fill(W["ebuf"], 0.5)
-    op({"g": (lambda: g.affine_select(T.ebuf[:], T.ebuf[:], [[1, 528]], A.is_equal, 0.0, -3, -4), 1050)}, [W["ebuf"]], [W["ebuf"]])
+    fill(W["ebuf"], 0)
+    op({"g": (lambda: g.affine_select(T.ebuf[:], T.ebuf[:], [[1, 528]], A.not_equal, 0.5, -3, -4), 1050)}, [W["ebuf"]], [W["ebuf"]])
     iota(iob, [[1, 256]], 0)
     iota(ios, [[1, C]], -int(SO))
     iota(k64r, [[16, TR], [0, 16]], -int(PO))
     iota(l32, [[0, TR // 2], [1, 32]], 0)
     iota(cut(srcw, C, WW), [[1, VW]], C - int(SO))
-    fill(ks, 0.0)
-    iota(mt, [[0, C]], -1)
-    iota(fsd, [[0, C]], 16)
-    iota(fs0, [[0, C]], 8)
-    iota(cut(fs, C, C + 16), [[0, 16]], 16)
-    for p in sn:
-        fill(cut(sn[p], 0, 16), 0.0)
-        fill(cut(sn[p], _n(sn[p]) - 16, _n(sn[p])), 0.0)
+    fill(ks, 0)
+    fill(mt, -1)
+    fill(fsd, 16)
+    fill(fs0, 8)
+    fill(cut(fs, C, C + 16), 16)
+    for p in HALVES:
+        mset(cut(sn[p], 0, 16), 0.0)
+        mset(cut(sn[p], H + 16, H + 32), 0.0)
     ts(r0, pi, 15, A.bitwise_and)
     ts(r1, pi, 16, A.bitwise_and)
     cp(cl["r"], r0)
@@ -432,23 +431,21 @@ def rank_program(g, core, T, topo):
     lin(self_, k16n, 1.0, cl["r"])
     lin(kpair, k16n, -1.0, cl["r16"])
     ts(diag, loc, cl["r"], A.is_equal)
-    ts(mkl, loc, cl["rm1"], A.is_equal, -512.0, A.mult)
-    lin(mkc, diag, 16.0)
-    tt(mkg, mkl, mkc, A.add)
+    ts(mkl, loc, cl["rm1"], A.not_equal, 512.0, A.mult)
+    lin(mkc, diag, 16.0, -512.0)
+    scan(mkg, mkl, mkc, A.max, A.add)
     lin(ends(mkg), ends(mkg), 1.0, -16.0)
     lin(mkl, mkg, 16.0)
     lin(ends(mkl), ends(mkl), 1.0, -256.0)
     lin(mkc, mkl, 2.0)
-    wide = C // len(sn)
-    lin(cl["te"], cl["h"], wide / 16 + 1.0, cl["r"])
-    lin(cl["to"], cl["h"], -wide / 16 - 1.0, cl["r"])
-    for a, b in sn:
-        ts(cut(tsel, a, b, 2), cut(k32n, 0, (b - a) // 2), cl["te"], A.add)
-        ts(cut(tsel, a + 1, b, 2), cut(k32n, 0, (b - a) // 2), cl["to"], A.add, wide + 32.0, A.add)
+    lin(cl["te"], cl["h"], H / 16 + 1.0, cl["r"])
+    lin(cl["to"], cl["h"], -H / 16 - 1.0, cl["r"])
+    for a, b in HALVES:
+        ts(cut(tsel, a, b, 2), cut(k32n, 0, 5), cl["te"], A.add)
+        ts(cut(tsel, a + 1, b, 2), cut(k32n, 0, 5), cl["to"], A.add, H + 32.0, A.add)
     cp(upk, cut(k16n, 0, 8))
     cp(nodu, W["nodi"])
     act(sig, loc, AF.Sign, 1.0, cl["nr"])
-    ts(keep, loc, 1.0, A.min)
     lin(d0s, diag, -2.0, 1.0)
     lin(starts(d0s), k16n, 0.0)
     tt(j0f, W["pari"], k16n, A.add)
@@ -456,19 +453,19 @@ def rank_program(g, core, T, topo):
     pick(lc, iom, j0)
     pick(lb, lc, j0)
     take(cv1, lb, mkg)
-    tt(n1, self_, j0f, A.subtract)
-    act(n2, n1, AF.Relu)
     lin(n3, self_, 1.0, -PO)
     tt(n4, ends(cv1), n3, A.is_equal)
-    tt(n1, n4, n2, A.mult)
-    tt(j1f, n1, j0f, A.add)
+    tt(n1, n4, self_, A.mult)
+    tt(j1f, n1, j0f, A.max)
     cp(j1, j1f)
     tt(pr, j1f, kpair, A.add)
+    tt(dj, j1f, self_, A.subtract)
     cp(m2u, pr)
     pick(la, iom, j1)
     ts(ta, a1, cl["r1"], A.is_equal)
-    tt(tm, ta, d256, A.max)
-    lin(tm, tm, -2.0, 64.0)
+    lin(tb, ta, -2.0, 2.0)
+    lin(td, d256, -2.0, 62.0)
+    scan(tm, tb, td, A.min, A.add, 64.0)
     quant(W["qu0"], W["su0"], W["ut"])
     for h in (0, 1):
         quant(cut(W["qx"], H * h, H * h + H), cut(W["sx"], H * h, H * h + H), cut(W["xt"], 4 * H * h, 4 * H * h + 4 * H))
@@ -478,52 +475,61 @@ def rank_program(g, core, T, topo):
     for b in range(4):
         quant(cut(W["qe"], 128 * b, 128 * b + 128), cut(W["se"], 128 * b, 128 * b + 128), cut(W["ebuf"], 3 - b, 515 - b))
     cp(by(b3, nodu), iom)
-    take(b1f, b3, mkc)
-    ts(invu, ends(b1f), PO + 512.0, A.add)
-    if OPT["sigc"]:
-        pick(sigc, sig, invu, split=False)
-    pick(nodrep, ios, nodu, split=False)
+    take(b1h, b3, mkc)
+    ts(invu, ends(b1h), PO + 512.0, A.add)
+    lin(sigc, by(sig, invu))
+    lin(nodrep, by(ios, nodu))
     lin(t16, cut(i32, 0, 16), 16.0, 16.0)
     act(cl["o16"], cl["r16"], AF.Relu, 1.0, -224.0)
     lin(cl["want"], cl["o16"], -0.125, cl["r1"])
-    lin(cl["cap"], cl["o16"], -0.125, 16.0)
+    lin(cl["cap"], cl["o16"], -0.125, 17.0)
+    lin(cl["cap1"], cl["o16"], -0.125, 16.0)
     lin(cl["rh"], cl["r"], -8.0, 8.0)
     lin(cl["t0"], cl["r16"], 1.0, -248.0)
-    ts(tw, l256, cl["want"], A.is_equal)
-    ts(tb, a1, -1.0, A.add, cl["cap"], A.min)
-    tt(tw, tw, tb, A.mult)
-    tt(to, d256, a1, A.mult)
-    act(th, l256, AF.Sign, 1.0, -7.5)
-    tt(ta, ta, l256, A.mult)
+    same(tc, l256, cl["want"])
+    act(tb, a1, AF.Relu, -1.0, cl["cap"])
+    lin(tb, tb, -1.0, cl["cap1"])
+    scan(tw, tb, tc, A.max, A.mult)
+    scan(to, a1, d256, A.max, A.mult)
+    lin(th, l256, float(C), -7.0 * C)
+    lin(td, l256, -1.0)
+    tt(th, th, td, A.max)
+    lin(cut(th, 7, 256, 16), cut(k16n, 0, 16), 0.0, -7.0)
+    lin(ends(th), cut(k16n, 0, 16), 0.0)
     tt(th, th, ta, A.mult)
-    ts(cl["nz"], cl["r"], 1.0, A.min)
-    ts(cl["t1"], cl["r"], 14.0, A.not_equal)
-    ts(cl["msend"], cl["r"], 7.0, A.is_ge, cl["t1"], A.mult)
-    ts(cl["r8"], cl["r"], 8.0, A.is_ge, 8.0, A.mult)
+    lin(cut(thw, 256, 512), th)
+    lin(cut(tww, 256, 512), tw)
+    lin(d16, cut(diag, 0, 16))
+    for h in range(1, 8):
+        lin(cut(w2, C * h, C * h + C), loc, cut(d16, h + 7, h + 8), cut(d16, h + 7, h + 8))
+    lin(mh, loc, 0.0)
+    lin(ends(mh), self_, 1.0, -4096.0)
+    for i in (0, 1):
+        lin(cut(kq, i, TR, 2), k32n, 0.0, 256.0 * i)
+    act(cl["nz"], cl["r"], AF.Sign)
+    act(cl["s7"], cl["r"], AF.Sign, 1.0, -6.5)
+    act(cl["a14"], cl["r"], AF.Abs, 1.0, -14.0)
+    act(cl["t1"], cl["a14"], AF.Sign)
+    act(cl["msend"], cl["s7"], AF.Relu, cl["t1"])
     lin(cl["mown"], cl["msend"], -1.0, 1.0)
-    ts(cl["vsel"], cl["r8"], cl["r"], A.add, 7.0, A.add)
-    if OPT["vcap"]:
-        lin(cl["v1"], cl["vsel"], 1.0, -1.0)
-        ts(keep32, l32, cl["v1"], A.is_equal, -2048.0, A.mult)
-        ts(maskv, l32, cl["vsel"], A.is_equal, 512.0, A.mult)
-        tt(maskv, maskv, keep32, A.add)
-        lin(cut(maskv, 31, C, 32), k32n, 0.0, -1024.0)
-    else:
-        ts(keep32, l32, 1.0, A.min)
-        ts(maskv, l32, cl["vsel"], A.is_equal)
+    act(cl["r8"], cl["r"], AF.Sign, 1.0, -7.5)
+    lin(cl["v1"], cl["r"], 1.0, 8.0)
+    lin(cl["rm8"], cl["r"], 1.0, -8.0)
+    lin(cl["vsel"], cl["r8"], 8.0, cl["rm8"])
+    same(te, l256, cl["v1"])
+    same(tf, l256, cl["vsel"])
+    act(keep32, l32, AF.Sign)
     lin(cl["k3"], cl["r"], 1.0, C - 7 - PO + 1024.0)
-    ts(cl["m7"], cl["r"], 14.0, A.is_lt, cl["msend"], A.mult)
+    act(cl["s14"], cl["r"], AF.Sign, -1.0, 13.5)
+    act(cl["m7"], cl["s14"], AF.Relu, cl["msend"])
     lin(k3, k16n, 0.5, cl["k3"])
     lin(k3, k3, cl["m7"], -1024.0)
-    for h in (0, 1):
-        lin(ends(cut(mt, H * h, H * h + H)), cut(k16n, 0, 10), 1.0, 31.0)
+    for a, b in HALVES:
+        lin(ends(cut(mt, 16 * a, 16 * b)), cut(k16n, 0, b - a), 1.0, 31.0)
     quant(W["qv"], W["sv"], W["vt0"])
 
     def plane(b):
         return cut(W["win"], WW * b, WW * b + C)
-
-    def lane(name, b):
-        return cut(W[name], b, _n(W[name]), 4)
 
     def block(name, b, n):
         return cut(W[name], n * b, n * b + n)
@@ -538,56 +544,57 @@ def rank_program(g, core, T, topo):
             mm(ps[fb[b]], block("qe", b, 128), block("se", b, 128), W["qx"], W["sx"])
             lin(plane(b), ps[fb[b]])
         for b in (0, 1):
-            dma("y", ap(block("fo", b, C)), ap(plane(b)), [plane(b)], [block("fo", b, C)], "df" + "ab"[b] + str(rnd))
+            dma("y", ap(block("fo", b, C)), ap(plane(b)), [plane(b)], [block("fo", b, C)], "df" + "ab"[b] + str(rnd), 16, 1000)
 
-        pick(lb, la, j1, split=start)
-        pick(m1, tm, m2u, split=start)
-        take(cv2, lb, mkg)
-        ts(j2, ends(cv2), PO, A.add)
-        pick(lc, lb, j2, split=start)
-        pick(g2, m1, j2, -1.0, 192.0, split=start)
-        take(cv4, lc, mkg)
-        ts(j4, ends(cv4), PO, A.add)
-        scan(m2, g2, m1, A.max, A.subtract)
-        pick(g4, m2, j4, -1.0, 192.0, split=start)
-        scan(m4, g4, m2, A.max, A.subtract)
-        pick(g8, m4, j4, split=start)
-        pick(g9, g8, j4, -1.0, 127.0, split=start)
-        scan(mm_, g9, m4, A.max, A.subtract)
-        seg(msum, mm_, A.add)
-        lin(szn, ends(msum), 0.5, 8.0)
-        lin(csz, ends(msum), -0.5, 8.0)
+        for a, b in HALVES if start else WHOLE:
+            (R, N), U = trees(a, b), trees(0, b)[0]
+            lin(R(lb), by(U(la), N(j1)))
+            lin(R(m1), by(tm, N(m2u)))
+            take(R(cv2), R(lb), R(mkg))
+            ts(N(j2), ends(R(cv2)), PO, A.add)
+            lin(R(lc), by(U(lb), N(j2)))
+            lin(R(g2), by(U(m1), N(j2)), -1.0, 192.0)
+            take(R(cv4), R(lc), R(mkg))
+            ts(N(j4), ends(R(cv4)), PO, A.add)
+            scan(R(m2), R(g2), R(m1), A.max, A.subtract)
+            lin(R(g4), by(U(m2), N(j4)), -1.0, 192.0)
+            scan(R(m4), R(g4), R(m2), A.max, A.subtract)
+            lin(R(g8), by(U(m4), N(j4)))
+            lin(R(g9), by(U(g8), N(j4)), -1.0, 127.0)
+            scan(R(mm_), R(g9), R(m4), A.max, A.subtract)
+            seg(R(msum), R(mm_), A.add)
+            lin(N(szn), ends(R(msum)), 0.5, 8.0)
+            lin(N(csz), ends(R(msum)), -0.5, 8.0)
 
-        signed = OPT["sigc"] and not start
-        for c, d in parts("sc"):
-            R, out = (lambda v: cut(v, 16 * c, 16 * d)), cut(ps[0 if d == TR else 5], 0, 16 * (d - c))
+        for a, b in HALVES:
+            R, out = trees(a, b)[0], cut(ps[0 if a else 5], 0, H)
             mm(out, W["qu"], W["su"], R(W["qx"]), R(W["sx"]))
-            if signed:
-                tt(R(ssb), out, R(sigc), A.mult)
-            else:
+            if start:
                 lin(R(ssb), out)
-        for a, b in parts("st"):
-            R, N, n = (lambda v: cut(v, 16 * a, 16 * b)), (lambda v: cut(v, a, b)), 16 * (b - a)
-            snm, both = cut(sn[a, b], 16, n + 16), tt2[a, b]
-            if signed:
-                pick(snm, ssb, N(nodu))
             else:
+                tt(R(ssb), out, R(sigc), A.mult)
+        for p in HALVES:
+            (R, N), snm = trees(*p), cut(sn[p], 16, H + 16)
+            if start:
                 tt(snm, by(ssb, N(nodu)), R(sig), A.mult)
+            else:
+                lin(snm, by(ssb, N(nodu)))
             lin(R(neg), snm, -1.0)
-            turn(cut(both, 0, n), snm)
-            turn(cut(both, n, 2 * n + 32), sn[a, b])
-            tt(R(cmp1), by(both, N(tsel)), R(neg), A.is_gt)
+            turn(cut(both[p], 0, H), snm)
+            turn(cut(both[p], H, C + 32), sn[p])
+            tt(R(cmp1), by(both[p], N(tsel)), R(neg), A.is_gt)
             scan(R(scs), R(d0s), R(cmp1), A.mult, A.add)
             ts(N(stu), ends(R(scs)), cl["r"], A.add)
         ts(sou, ends(scs), cl["r17"], A.add)
         lin(st16, ends(scs), 16.0, cl["t0"])
+        tt(stq, st16, kq, A.add)
         lin(cut(fsd, 1, C, 16), ends(scs), -8.0, cl["rh"])
 
-        for a, b in parts("wd"):
-            R, N = (lambda v: cut(v, 16 * a, 16 * b)), (lambda v: cut(v, a, b))
+        for a, b in HALVES:
+            R, N = trees(a, b)
             tt(R(xx), by(t16, N(stu)), R(mm_), A.mult)
-            pick(R(pst), cut(xx, 0, 16 * b), N(j1), -1.0, -8.0, split=False)
-            take(R(cvp), R(pst), mkl)
+            lin(R(pst), by(cut(xx, 0, 16 * b), N(j1)), -1.0, -8.0)
+            take(R(cvp), R(pst), R(mkl))
             tt(N(dl), ends(R(cvp)), N(st16), A.subtract)
             seg(R(sc1), R(xx), A.max)
             seg(R(sc2), R(xx), A.min)
@@ -597,44 +604,44 @@ def rank_program(g, core, T, topo):
             ts(N(keyu), starts(R(ks)), 0.0, A.add)
             seg(R(kb), R(ks), A.add)
             tt(R(cmp2), by(iob, N(keyu)), R(kb), A.is_lt)
-            seg(R(rk), R(cmp2), A.add)
             act(N(nf), ends(R(sc2)), AF.Relu, -1.0, -255.0)
             tt(N(pa), N(nf), N(dl), A.mult)
-            tt(N(qb), N(pa), N(st16), A.add)
+            tt(N(qb), N(pa), N(stq), A.add)
+            seg(R(rk), R(cmp2), A.add)
             tt(N(na), ends(R(rk)), N(qb), A.add)
             ts(N(idxw), N(na), 248.0, A.add)
-            pick(R(hi), th, N(idxw))
-            seg(R(his), R(hi), A.max)
-        lin(sa, ends(his))
+            lin(R(hi), by(thw, N(idxw)))
+            take(R(his), R(hi), R(mh))
+        ts(sa, ends(his), 4096.0, A.add)
         remote(lda, sa, "aa%d" % rnd, peer, 0)
-        pick(wd, tw, idxw)
+        pick(wd, tww, idxw)
         place(wds, wd, k64r)
         lin(sb, ends(wds), cl["msend"])
         remote(ldb, sb, "ab%d" % rnd, peer, 0)
 
-        seg(los, hi, A.min)
-        lin(lon, ends(los), -1.0)
-        pick(b4, to, sou, split=False)
-        place(ov, b4, k64r)
-        ts(ou, ends(ov), PO - 1.0, A.add)
-        pick(cut(srcw, 0, C), nodrep, ou, split=False)
-        pick(osrep, loc if final else iom, ou, split=False)
-        scan(cut(fs, 0, C), fs0, fsd, A.add, A.min)
-        ts(cwu, ends(wds), PO, A.add)
-        lin(own, ends(wds), cl["mown"])
-        if OPT["vcap"]:
-            pick(vb, cut(srcw, 0, C), cwu)
-            take(vsf, vb, maskv)
-            ts(vu, cut(vsf, 31, C, 32), SO + 512.0, A.add)
-        else:
-            tt(vb, by(cut(srcw, 0, C), cwu), maskv, A.mult)
-            scan(vs, keep32, vb, A.mult, A.add)
-            ts(vu, cut(vs, 31, C, 32), SO, A.add)
+        tt(pj, nf, dj, A.mult)
+        tt(pn, pj, self_, A.add)
+        cp(pnu, pn)
+        lin(pcol, by(nodrep, pnu))
+        tt(vb, by(tvw, idxw), pcol, A.mult)
+        scan(vs, keep32, vb, A.mult, A.add)
+        ts(vu, cut(vs, 31, C, 32), SO, A.add)
         for b in range(4):
-            lin(lane("vt", b), by(plane(b), vu), 2.0)
+            lin(cut(W["vt"], b, 4 * VW, 4), by(plane(b), vu), 2.0)
         quant(qs, ss, W["vt"])
         remote(ql, qs, "av%d" % rnd, peer, 1100)
         remote(sl, ss, "av%d" % rnd, peer, 400)
+
+        seg(los, hi, A.min)
+        ts(lou, ends(los), -1.0, A.mult, cl["r16"], A.add)
+        lin(cut(w2, 0, C), by(to, lou), cl["nz"])
+        lin(b4, by(to, sou))
+        place(ov, b4, k64r)
+        ts(ou, ends(ov), PO - 1.0, A.add)
+        lin(cut(srcw, 0, C), by(nodrep, ou))
+        lin(osrep, by(loc if final else iom, ou))
+        scan(cut(fs, 0, C), fs0, fsd, A.add, A.min)
+        lin(own, ends(wds), cl["mown"])
 
         arrive([lda], "aa%d" % rnd, ne)
         arrive([ldb], "ab%d" % rnd, ne)
@@ -643,19 +650,16 @@ def rank_program(g, core, T, topo):
         tt(o2f, cg, k3, A.max)
         ts(o2u, o2f, PO, A.add)
         ts(cgu, cg, PO, A.add)
-        pick(srcj, srcw, o2u, split=False)
-        pick(lnkj, osrep, cgu, split=False)
+        lin(srcj, by(srcw, o2u))
+        lin(lnkj, by(osrep, cgu))
         if not final:
             lin(ends(lnkj), ends(osrep))
-        tt(rel, lon, lda, A.max)
-        ts(relu, rel, cl["r16"], A.add)
-        for a, b in parts("dec"):
-            R, N = (lambda v: cut(v, 16 * a, 16 * b)), (lambda v: cut(v, a, b))
-            pick(R(inv), to, N(relu), cl["nz"])
+        for a, b in HALVES:
+            R, N = trees(a, b)
+            lin(R(inv), by(w2, N(lda)))
             place(R(invs), R(inv), R(k64r))
             ts(N(idxu), ends(R(invs)), PO, A.add)
-            for c, d in ((a, b),) if b - a < TR else ((0, TR // 2), (TR // 2, TR)):
-                either(cut(em, 16 * c, 16 * d), by(fs, cut(idxu, c, d)), (0.0, None, A.max), (AF.Relu, 1.0, 0.0))
+            either(R(em), by(fs, N(idxu)), (0.0, None, A.max), (AF.Relu, 1.0, 0.0))
             seg(R(ems), R(em), A.add)
             tt(starts(R(ks)), N(st16), ends(R(ems)), A.add)
             scan(R(yy), R(ks), R(em), A.max, A.subtract)
@@ -665,43 +669,41 @@ def rank_program(g, core, T, topo):
         for b in range(4):
             mm(cut(ps[ub[b]], 0, VW), block("qe", b, 128), block("se", b, 128), ql, sl)
             lin(cut(W["win"], WW * b + C, WW * b + WW), cut(ps[ub[b]], 0, VW))
-        pick(b2, srcj, tu, halves=True)
-        if OPT["cap"]:
-            pick(b1, b2, invu)
-            take(b1f, b1, mkc)
-            ts(eu, ends(b1f), SO + 512.0, A.add)
-        else:
-            tt(b1, by(b2, invu), diag, A.mult)
-            seg(b1s, b1, A.add)
-            ts(eu, ends(b1s), SO, A.add)
-        pick(oprep if final else la, lnkj, tu, halves=True)
+        pick(b2, srcj, tu, local=True)
+        pick(b1, b2, invu)
+        for a, b in HALVES:
+            R, N = trees(a, b)
+            take(R(b1h), R(b1), R(mkc))
+            ts(N(eu), ends(R(b1h)), SO + 512.0, A.add)
+        pick(oprep if final else la, lnkj, tu, local=True)
         if final:
             dma("y", T.op[:], T.pf[0:128:16, oprep[1]:oprep[2]], [oprep], [], "dop")
         else:
             take(cv1, la, mkg)
             ts(j1, ends(cv1), PO, A.add)
             tt(pr, ends(cv1), kpair, A.add)
+            tt(dj, ends(cv1), n3, A.subtract)
             ts(m2u, pr, PO, A.add)
 
-        for c, d in parts("bl"):
-            R, L = (lambda v: cut(v, 16 * c, 16 * d)), (lambda k, b: cut(W[k], 64 * c + b, 64 * d, 4))
+        for a, c in HALVES:
+            (R, N), L = trees(a, c), (lambda b: cut(W["zt"], 64 * a + b, 64 * c, 4))
             for b in (3, 2):
-                lin(R(block("hh", b - 2, C)), by(block("win", b, WW), cut(eu, c, d)))
+                lin(R(block("hh", b - 2, C)), by(block("win", b, WW), N(eu)))
             for b in (0, 1):
-                tt(L("zt", b), by(block("win", b, WW), cut(eu, c, d)), R(block("fo", b, C)), A.add)
+                tt(L(b), by(block("win", b, WW), N(eu)), R(block("fo", b, C)), A.add)
             for b in (3, 2):
-                tt(L("zt", b), R(block("hh", b - 2, C)), R(ps[fb[b]]), A.add)
+                tt(L(b), R(block("hh", b - 2, C)), R(ps[fb[b]]), A.add)
             for b in range(4):
-                lin(R(block("z32", b, C)), L("zt", b), 32.0)
-            quant(R(W["qz"]), R(W["sz"]), cut(W["zt"], 64 * c, 64 * d))
-        for c, d in parts("xl"):
-            R, L = (lambda v: cut(v, 16 * c, 16 * d)), (lambda k, b: cut(W[k], 64 * c + b, 64 * d, 4))
+                lin(R(block("z32", b, C)), L(b), 32.0)
+            quant(R(W["qz"]), R(W["sz"]), cut(W["zt"], 64 * a, 64 * c))
+        for a, c in HALVES:
+            R = trees(a, c)[0]
             for b in range(4):
-                out = cut(ps[(fb if d == TR else wb)[b]], 0, 16 * (d - c))
+                out = cut(ps[(fb if a else wb)[b]], 0, H)
                 mm(out, block("wq", b, 128), block("wsb", b, 128), R(W["qz"]), R(W["sz"]))
                 tt(R(block("x32", b, C)), out, R(block("z32", b, C)), A.add)
-                lin(L("xt", b), R(block("x32", b, C)), 0.03125)
-            quant(R(W["qx"]), R(W["sx"]), cut(W["xt"], 64 * c, 64 * d))
+                lin(cut(W["xt"], 64 * a + b, 64 * c, 4), R(block("x32", b, C)), 0.03125)
+            quant(R(W["qx"]), R(W["sx"]), cut(W["xt"], 64 * a, 64 * c))
 
     for h in (0, 1):
         dma("y", T.oc[:, 4 * H * h:4 * H * h + 4 * H], ap(block("qx", h, H)).bitcast(dt.uint8), [block("qx", h, H)], [], "doc", 32, 500)

import numpy as np
from concourse.mybir import dt, AluOpType, ActivationFunctionType

A = AluOpType
AF = ActivationFunctionType
C, TR, VW = 320, 20, 160
WW = C + VW
H = C // 2
WHOLE, HALVES = ((0, TR),), ((0, TR // 2), (TR // 2, TR))
PO, SO = 64.0, 224.0
MASKS = [1, 2, 4]
Q4, U8, BF, F16, F32, I32, U16 = "float8_e4m3fn_x4", "uint8", "bfloat16", "float16", "float32", "int32", "uint16"
OPT = {"seed": 1, "tries": 10, "turns": 6, "mend": 6000, "give": 150}

SCRATCH = {}


def _decl(dtype, **kw):
    for k, n in kw.items():
        SCRATCH[k] = ("sbuf", [128, n], dtype)


_decl(Q4, qx=C, qz=C, qu0=128, qu=128, qv=128, wq=512, qe=512)
_decl(U8, sx=C, sz=C, su0=128, su=128, sv=128, wsb=512, se=512)
for _r in range(3):
    _decl(Q4, **{"qs%d" % _r: VW, "ql%d" % _r: VW})
    _decl(U8, **{"ss%d" % _r: VW, "sl%d" % _r: VW})
    _decl(U16, **{"sa%d" % _r: TR, "la%d" % _r: TR})
    _decl(BF, **{"sb%d" % _r: TR, "lb%d" % _r: TR})
_decl(BF, xt=4 * C, zt=4 * C, z32=4 * C, x32=4 * C, ut=512, vt0=512, ebuf=528, win=4 * WW, vt=4 * VW, hh=2 * C, fo=2 * C)
_decl(I32, pi=2, ri=2, nodi=TR, pari=TR)
_decl(BF, pb=32768)
_decl(F16, ph=C)
_decl(F32, pf=4608)
_decl(U16, pu=1024)
for _b in range(8):
    SCRATCH["ps%d" % _b] = ("psum", [128, 512], F32)

_DMAS = ["dx0", "dx1", "du", "dw", "dws", "dv", "dpar", "dnod", "dop", "doc", "dos", "dy0", "dy1"]
SEMAPHORES = ["cv", "cs", "ct", "cg", "sent"] + _DMAS + [n + str(r) for n in ("aa", "ab", "av", "dfa", "dfb") for r in range(3)]

TUNES = ((1.0, (210, 210), 1100, 1300, 1.0), (0.8, (150, 290), 900, 1000, 0.8), (1.2, (240, 150), 1500, 1700, 1.4),
         (1.0, (120, 140), 1200, 1300, 1.0))
CHOSEN = []


def _n(v):
    return 16 * _n(v[2]) if v[0] == "by" else len(range(v[1], v[2], v[3]))


def _bits(v):
    if v[0][:2] == "ps":
        return 1
    if v[3] == 1:
        return ((1 << (v[2] - v[1])) - 1) << v[1]
    return sum(1 << c for c in range(v[1], v[2], v[3]))


def _needs(ops):
    seen, deps = {}, []
    for n, o in enumerate(ops):
        d = set()
        for views, wr in ((o["rd"], False), (o["wr"], True)):
            for v in views:
                m, w = _bits(v), wr or v[0][:2] == "ps"
                l = seen.setdefault(v[0], [])
                d.update(e[0] for e in l if e[1] & m and (w or e[2]))
                if w:
                    l[:] = [(e[0], e[1] & ~m, e[2]) for e in l if e[1] & ~m]
                l.append((n, m, w))
        d.discard(n)
        deps.append(d)
    return deps


def _order(ops, deps):
    count, users = len(ops), [[] for o in ops]
    for n, d in enumerate(deps):
        for m in d:
            users[m].append(n)

    def lengths(pick, hop, far, load, slow):
        cost = [{q: c[1] * (pick if o["pick"] else 1.0) for q, c in o["q"].items()} for o in ops]
        late = [o["late"] * slow + (far if o["kind"] == "far" else load if o["kind"] == "dma" else 0) for o in ops]
        return cost, late, hop

    tunes = [lengths(*k) for k in TUNES]

    def replay(order, cost, late, hop):
        done, why, free, last, on = [0] * count, [None] * count, {}, {}, [None] * count
        for n, q in order:
            t, w = free.get(q, 0), (last.get(q), True)
            for m in deps[n]:
                if done[m] + hop[on[m] != q] > t:
                    t, w = done[m] + hop[on[m] != q], (m, False)
            free[q], last[q], why[n], on[n] = t + cost[n][q], n, w, q
            done[n] = free[q] + late[n]
        n, chain = max(range(count), key=lambda n: done[n]), []
        end = done[n]
        while n is not None:
            if why[n][1] and why[n][0] is not None:
                chain.append((why[n][0], n))
            n = why[n][0]
        return end, chain

    def judge(order, bound):
        ends, total = [], 0
        for k in tunes:
            ends.append(replay(order, *k))
            total += ends[-1][0]
            if bound and total > sum(bound[:len(ends)]) + OPT["give"]:
                return None
        return ends

    def lay(way, before, back, spare, cost, late, hop):
        done, at, busy = [0] * count, [None] * count, {}
        for n in sorted(range(count), key=lambda n: -way[n]):
            best = None
            for q, c in cost[n].items():
                t = max([0] + [done[m] + hop[at[m][1] != q] for m in before[n]]) + (late[n] if back else 0)
                s, l = t, busy.setdefault(q, [])
                i = len(l)
                while i and l[i - 1][1] > t:
                    i -= 1
                while i < len(l) and l[i][0] < s + c:
                    s = max(s, l[i][1])
                    i += 1
                if best is None or s + c * (1.0 + spare * (q == "v")) < best[0]:
                    best = (s + c * (1.0 + spare * (q == "v")), s, q, i)
            s, q, i = best[1:]
            busy[q].insert(i, (s, s + cost[n][q]))
            at[n], done[n] = (s, q), s + cost[n][q] + (0 if back else late[n])
        return [(n, at[n][1]) for n in sorted(range(count), key=lambda n: at[n][0])], done

    rng, best = np.random.RandomState(OPT["seed"]), None
    for attempt in range(OPT["tries"]):
        tune = tunes[attempt % len(tunes)]
        cost, late, hop = tune
        shake, spare = 1.0 + (0.3 if attempt else 0.0) * (rng.rand(count) - 0.5), 4.0 * rng.rand()
        way = [0] * count
        for n in range(count - 1, -1, -1):
            way[n] = 1 + (min(cost[n].values()) + late[n]) * shake[n] + max([way[m] + hop[0] for m in users[n]] + [0])
        for turn in range(OPT["turns"]):
            out, done = lay(way, deps, False, spare, *tune)
            end = sum(e[0] for e in judge(out, None))
            if best is None or end < best[0]:
                best = (end, out)
            way = lay(done, users, True, spare, *tune)[1]

    order = best[1]
    ends = judge(order, None)
    for step in range(OPT["mend"]):
        chain = ends[rng.randint(len(ends))][1]
        m, n = chain[rng.randint(len(chain))]
        at = {k[0]: i for i, k in enumerate(order)}
        a, b, trial, how = at[m], at[n], list(order), rng.randint(4)
        if how == 0 and max([at[d] for d in deps[n]] + [-1]) < a:
            trial.insert(a, trial.pop(b))
        elif how == 1 and min([at[d] for d in users[m]] + [count]) > b:
            trial.insert(b, trial.pop(a))
        elif how > 1 and len(ops[(m, n)[how - 2]]["q"]) > 1:
            i = (a, b)[how - 2]
            trial[i] = (trial[i][0], [q for q in ops[trial[i][0]]["q"] if q != trial[i][1]][0])
        else:
            continue
        now = judge(trial, [e[0] for e in ends])
        if now and sum(e[0] for e in now) <= sum(e[0] for e in ends):
            order, ends = trial, now
    return order


def _emit(g, T, ops, deps, order):
    qs = {"v": g.vector, "s": g.scalar, "t": g.tensor, "g": g, "y": g.sync}
    known, clock, waits, needed, pos, src, place = {q: {} for q in qs}, {}, {}, set(), {}, {}, {}
    for i, (n, q) in enumerate(order):
        place[n] = i
        sem = ops[n]["sem"]
        pos[q] = pos.get(q, 0) + (sem is None)
        src[n] = (q, pos[q]) if sem is None else (sem[0], 1)
        if q not in qs:
            clock[n] = {sem[0]: 1}
            continue
        waits[n] = []
        for d in sorted(deps[n], key=lambda d: -place[d]):
            if known[q].get(src[d][0], 0) >= src[d][1]:
                continue
            waits[n].append(d)
            needed.add(d)
            for k, v in clock[d].items():
                known[q][k] = max(known[q].get(k, 0), v)
        clock[n] = dict(known[q])
        clock[n][src[n][0]] = src[n][1]
    count, value = {}, {}
    for n, q in order:
        value[n] = ops[n]["sem"]
        if value[n] is None and n in needed:
            count[q] = count.get(q, 0) + 1
            value[n] = ("c" + q, count[q])
    for n, q in order:
        if q not in qs:
            continue
        for d in waits[n]:
            qs[q].wait_ge(T.sem[value[d][0]], value[d][1])
        ins = ops[n]["q"][q][0]()
        if ins is not None and value[n] is not None:
            ins.then_inc(T.sem[value[n][0]], 1 if ops[n]["sem"] is None else 16)


def rank_program(g, core, T, topo):
    rank = T.rank_of(core)
    if rank is None:
        return
    ops, used = [], {"pb": 0, "pf": 0, "pu": 0}
    V, S = g.vector, g.scalar

    def new(pool, n):
        a = used[pool]
        used[pool] += (n + 15) // 16 * 16
        assert used[pool] <= SCRATCH[pool][1][1]
        return (pool, a, a + n, 1)

    def news(pool, n, count):
        return [new(pool, n) for k in range(count)]

    def cut(v, a, b, step=1):
        return (v[0], v[1] + a, v[1] + b, step)

    def ends(v):
        return cut(v, 15, _n(v), 16)

    def starts(v):
        return cut(v, 0, _n(v), 16)

    def by(win, off):
        return ("by", win, off)

    def trees(a, b):
        return (lambda v: cut(v, 16 * a, 16 * b)), (lambda v: cut(v, a, b))

    def ap(v):
        if not isinstance(v, tuple):
            return v
        if v[0] == "by":
            return ap(v[1]).indirect(ap(v[2]))
        return T[v[0]][:, v[1]:v[2]:v[3]] if v[3] > 1 else T[v[0]][:, v[1]:v[2]]

    def flat(views):
        out = []
        for v in views:
            if isinstance(v, tuple):
                out.extend(v[1:] if v[0] == "by" else [v])
        return out

    def op(q, rd, wr, kind="", late=0, sem=None):
        pick = any(isinstance(v, tuple) and v[0] == "by" for v in rd + wr)
        ops.append({"q": q, "rd": flat(rd), "wr": flat(wr), "kind": kind, "late": late, "sem": sem, "pick": pick})

    def length(out, ins, base, rate=None):
        n = _n(out)
        if out[0] == "by":
            return base + 3.2 * n
        if ins[0][0] == "by":
            return base + 1.3 * n
        if rate is None:
            rate = 0.5 if all(SCRATCH[v[0]][2] in (BF, F16, U16) for v in ins + [out]) else 1.0
        return 0.83 * max(64, n * rate)

    def ts(out, a, s1, o0, s2=None, o1=None):
        more = (o0,) if o1 is None else (o0, o1)
        op({"v": (lambda: V.tensor_scalar(ap(out), ap(a), ap(s1), ap(s2), *more), length(out, [a], 50))}, [a, s1, s2], [out])

    def tt(out, a, b, o):
        rate = 1.0 if "ps" in (a[0][:2], b[0][:2]) or SCRATCH[out[0]][2] == BF == SCRATCH[b[0]][2] else 2.0
        op({"v": (lambda: V.tensor_tensor(ap(out), ap(a), ap(b), o), length(out, [a, b], 50, rate))}, [a, b], [out])

    def cp(out, a):
        op({"v": (lambda: V.tensor_copy(ap(out), ap(a)), length(out, [a], 50))}, [a], [out])

    def scan(out, d0, d1, o0, o1, ini=0.0):
        op({"v": (lambda: V.tensor_tensor_scan(ap(out), ap(d0), ap(d1), ini, o0, o1), length(out, [d0, d1], 50))}, [d0, d1], [out])

    def turn(out, a):
        op({"v": (lambda: V.transpose(ap(out), ap(a)), length(out, [a], 50))}, [a], [out])

    def mset(out, c):
        op({"v": (lambda: V.memset(ap(out), c), length(out, [out], 50))}, [], [out])

    def iota(out, pat, base, mul=0):
        flt = {} if SCRATCH[out[0]][2] == I32 else {"allow_small_or_imprecise_dtypes": True}
        op({"g": (lambda: g.iota(ap(out), pat, base, mul, **flt), 130 + 1.66 * _n(out))}, [], [out])

    def fill(out, c):
        iota(out, [[0, _n(out)]], c)

    def act(out, a, fn, scale=1.0, bias=0.0):
        op({"s": (lambda: S.activation(ap(out), ap(a), fn, bias=ap(bias), scale=ap(scale)), length(out, [a], 65, 1.0))},
           [a, scale, bias], [out])

    def lin(out, a, scale=1.0, bias=0.0):
        plain = bias == 0.0

        def vec():
            if plain:
                return V.tensor_copy(ap(out), ap(a)) if scale == 1.0 else V.tensor_scalar(ap(out), ap(a), ap(scale), None, A.mult)
            return V.tensor_scalar(ap(out), ap(a), ap(scale), ap(bias), A.mult, A.add)

        def sca():
            if plain and not isinstance(scale, tuple):
                return S.activation(ap(out), ap(a), AF.Copy, scale=scale)
            return S.activation(ap(out), ap(a), AF.Identity, bias=ap(bias), scale=ap(scale))
        op({"v": (vec, length(out, [a], 50)), "s": (sca, length(out, [a], 65, 1.0))}, [a, scale, bias], [out])

    def either(out, a, vec, sca):
        op({"v": (lambda: V.tensor_scalar(ap(out), ap(a), *vec), length(out, [a], 50)),
            "s": (lambda: S.activation(ap(out), ap(a), sca[0], bias=sca[2], scale=sca[1]), length(out, [a], 65, 1.0))}, [a], [out])

    def same(out, a, c):
        act(out, a, AF.Abs, -1.0, c)
        act(out, out, AF.Relu, -1.0, 1.0)

    def pick(out, win, off, local=False):
        for a, b in HALVES:
            R, N = trees(a, b)
            lin(R(out), by(R(win) if local else win, N(off)))

    def quant(q, s, a):
        op({"v": (lambda: V.quantize_mx(ap(q), ap(s), ap(a)), 12 + 0.22 * _n(a))}, [a], [q, s])

    def mm(out, lq, ls, rq, rs):
        op({"t": (lambda: g.tensor.matmul_mx(ap(out), ap(lq), ap(ls), ap(rq), ap(rs), True, True), 0.6 * (_n(out) + 16))},
           [lq, ls, rq, rs], [out], "", 60)

    def dma(q, out, a, rd, wr, sem, n=16, late=0):
        e = g.sync if q == "y" else g.scalar
        op({q: (lambda: e.dma_start(out, a), 60)}, rd, wr, "dma", late, (sem, n))

    sent = [0]

    def remote(out, a, sem, peer, late):
        rid, pid = topo.addr(peer, core)
        mask = topo.mask(core, peer)
        sent[0] += len(topo.engines(core, peer))
        cast = (lambda v: ap(v).bitcast(dt.uint8)) if SCRATCH[a[0]][2] == Q4 else ap

        def call():
            g.remote_dma(cast(out), cast(a), T.sem[sem], T.sem.sent, pid, rid, mask)
        op({"g": (call, 250 if sent[0] > len(topo.engines(core, peer)) else 1400)}, [a], [("r" + out[0], 0, 1, 1)], "far", late)

    def arrive(views, sem, n):
        op({"far": (None, 0)}, [("r" + v[0], 0, 1, 1) for v in views], views, "", 0, (sem, n))

    W = {k: (k, 0, SCRATCH[k][1][1], 1) for k in SCRATCH}
    ps = [cut(W["ps%d" % b], 0, C) for b in range(8)]
    fb, ub, wb = [1, 2, 3, 4], [5, 6, 7, 1], [5, 6, 7, 0]

    loc, k64r, iom, ios, l32, diag, sig, sigc, keep, d0s, keep32, mkg, mkl, mkc, mt, nodrep, b3, ks, fsd, fs0 = news("pb", C, 20)
    a1, iob, tm, to, ta, tb, tc, td = news("pb", 256, 8)
    thw, tww, tvw = news("pb", 512, 3)
    th, tw, te, tf = cut(thw, 0, 256), cut(tww, 0, 256), cut(tvw, 0, 256), cut(tvw, 256, 512)
    t16, srcw, fs, w2 = new("pb", 16), new("pb", WW), new("pb", C + 16), new("pb", 8 * C)
    col = new("pf", 32)
    names = "r nr r1 rm1 want cap cap1 msend mown o16 vsel v1 m7 k3 te to h t0 r8 rm8 r16 r17 rh t1 nz s7 s14 a14".split()
    cl = {k: cut(col, i, i + 1) for i, k in enumerate(names)}
    i32, k32n, d16, mh = new("pf", 32), new("pf", 10), new("pf", 16), new("pf", C)
    k16n, self_, kpair, k3, kq = news("pf", TR, 5)
    nodu, invu, tsel, upk = new("pu", TR), new("pu", TR), new("pu", TR), new("pu", 8)
    (la, lb, lc, cv1, cv2, cv4, m1, m2, m4, mm_, g2, g4, g8, g9, msum, cmp1, scs, pst, cvp, xx, sc1, sc2, kb, cmp2, rk, hi,
     wd, wds, los, b4, ov, osrep, pcol, vb, vs, inv, invs, em, ems, yy, flag, tsc, lnkj, srcj, b2, b1) = news("pb", C, 46)
    ssb, neg, his, oprep, ysb = news("pf", C, 5)
    sn, both = {p: new("pf", H + 32) for p in HALVES}, {p: new("pf", C + 32) for p in HALVES}
    j0f, j1f, n1, n2, n3, n4, szn, csz, st16, stq, nf, dl, pa, qb, na, dj, pj, pn, own, cg, o2f, pr = news("pf", TR, 22)
    j0, j1, j2, j4, m2u, stu, sou, keyu, idxw, pnu, lou, ou, idxu, tu, cgu, o2u, eu = news("pu", TR, 17)
    vu, b1h = new("pu", 10), W["ph"]

    def seg(out, a, o):
        scan(out, cut(keep, 0, _n(a)), a, A.mult, o)

    def place(out, a, at):
        scan(out, at, a, A.max, A.add, -PO)

    def take(out, a, mask):
        scan(out, a, mask, A.max, A.add, -1024.0)

    dma("s", T.pari[:], T.par[:], [], [W["pari"]], "dpar")
    dma("y", T.ut[:], T.u[:], [], [W["ut"]], "du", 16, 400)
    dma("s", T.nodi[:], T.nod[:], [], [W["nodi"]], "dnod")
    for h in (0, 1):
        half = cut(W["xt"], 4 * H * h, 4 * H * h + 4 * H)
        dma("y", ap(half), T.x[:, half[1]:half[2]], [], [half], "dx%d" % h, 16, 900 + 500 * h)
    dma("y", T.wq[:].bitcast(dt.uint8), T.wc[:], [W["pari"]], [W["wq"]], "dw", 16, 2000)
    dma("y", T.wsb[:], T.ws[:], [W["pari"]], [W["wsb"]], "dws", 16, 2000)
    dma("y", T.vt0[:], T.v[:], [W["pari"]], [W["vt0"]], "dv", 16, 2000)

    pi, r0, r1 = cut(W["pi"], 0, 1), cut(W["ri"], 0, 1), cut(W["ri"], 1, 2)
    l256, d256 = cut(loc, 0, 256), cut(diag, 0, 256)
    iota(pi, [[0, 1]], 0, 1)
    iota(i32, [[1, 32]], 0)
    mset(keep, 1.0)
    mset(starts(keep), 0.0)
    scan(loc, keep, keep, A.mult, A.add)
    iota(iom, [[1, C]], -int(PO))
    iota(a1, [[1, 16], [0, 16]], 1)
    fill(W["ebuf"], 0)
    op({"g": (lambda: g.affine_select(T.ebuf[:], T.ebuf[:], [[1, 528]], A.not_equal, 0.5, -3, -4), 1050)}, [W["ebuf"]], [W["ebuf"]])
    iota(iob, [[1, 256]], 0)
    iota(ios, [[1, C]], -int(SO))
    iota(k64r, [[16, TR], [0, 16]], -int(PO))
    iota(l32, [[0, TR // 2], [1, 32]], 0)
    iota(cut(srcw, C, WW), [[1, VW]], C - int(SO))
    fill(ks, 0)
    fill(mt, -1)
    fill(fsd, 16)
    fill(fs0, 8)
    fill(cut(fs, C, C + 16), 16)
    for p in HALVES:
        mset(cut(sn[p], 0, 16), 0.0)
        mset(cut(sn[p], H + 16, H + 32), 0.0)
    ts(r0, pi, 15, A.bitwise_and)
    ts(r1, pi, 16, A.bitwise_and)
    cp(cl["r"], r0)
    cp(cl["h"], r1)
    lin(k16n, cut(i32, 0, TR), 16.0)
    lin(k32n, cut(i32, 0, 10), 32.0)
    for i in (0, 1):
        lin(cut(fs0, i, C, 16), k16n, 0.0, 1024.0)
    lin(cl["r16"], cl["r"], 16.0)
    lin(cl["rm1"], cl["r"], 1.0, -1.0)
    lin(cl["r1"], cl["r"], 1.0, 1.0)
    lin(cl["nr"], cl["r"], -1.0)
    lin(cl["r17"], cl["r"], 17.0)
    lin(self_, k16n, 1.0, cl["r"])
    lin(kpair, k16n, -1.0, cl["r16"])
    ts(diag, loc, cl["r"], A.is_equal)
    ts(mkl, loc, cl["rm1"], A.not_equal, 512.0, A.mult)
    lin(mkc, diag, 16.0, -512.0)
    scan(mkg, mkl, mkc, A.max, A.add)
    lin(ends(mkg), ends(mkg), 1.0, -16.0)
    lin(mkl, mkg, 16.0)
    lin(ends(mkl), ends(mkl), 1.0, -256.0)
    lin(mkc, mkl, 2.0)
    lin(cl["te"], cl["h"], H / 16 + 1.0, cl["r"])
    lin(cl["to"], cl["h"], -H / 16 - 1.0, cl["r"])
    for a, b in HALVES:
        ts(cut(tsel, a, b, 2), cut(k32n, 0, 5), cl["te"], A.add)
        ts(cut(tsel, a + 1, b, 2), cut(k32n, 0, 5), cl["to"], A.add, H + 32.0, A.add)
    cp(upk, cut(k16n, 0, 8))
    cp(nodu, W["nodi"])
    act(sig, loc, AF.Sign, 1.0, cl["nr"])
    lin(d0s, diag, -2.0, 1.0)
    lin(starts(d0s), k16n, 0.0)
    tt(j0f, W["pari"], k16n, A.add)
    cp(j0, j0f)
    pick(lc, iom, j0)
    pick(lb, lc, j0)
    take(cv1, lb, mkg)
    lin(n3, self_, 1.0, -PO)
    tt(n4, ends(cv1), n3, A.is_equal)
    tt(n1, n4, self_, A.mult)
    tt(j1f, n1, j0f, A.max)
    cp(j1, j1f)
    tt(pr, j1f, kpair, A.add)
    tt(dj, j1f, self_, A.subtract)
    cp(m2u, pr)
    pick(la, iom, j1)
    ts(ta, a1, cl["r1"], A.is_equal)
    lin(tb, ta, -2.0, 2.0)
    lin(td, d256, -2.0, 62.0)
    scan(tm, tb, td, A.min, A.add, 64.0)
    quant(W["qu0"], W["su0"], W["ut"])
    for h in (0, 1):
        quant(cut(W["qx"], H * h, H * h + H), cut(W["sx"], H * h, H * h + H), cut(W["xt"], 4 * H * h, 4 * H * h + 4 * H))
    op({"v": (lambda: V.tensor_copy(T.qu[:].bitcast(dt.uint32), T.qu0[:].bitcast(dt.uint32).indirect(ap(upk))), 220)},
       [W["qu0"], upk], [W["qu"]])
    op({"s": (lambda: S.activation(T.su[:], T.su0[:].indirect(ap(upk)), AF.Copy), 230)}, [W["su0"], upk], [W["su"]])
    for b in range(4):
        quant(cut(W["qe"], 128 * b, 128 * b + 128), cut(W["se"], 128 * b, 128 * b + 128), cut(W["ebuf"], 3 - b, 515 - b))
    cp(by(b3, nodu), iom)
    take(b1h, b3, mkc)
    ts(invu, ends(b1h), PO + 512.0, A.add)
    lin(sigc, by(sig, invu))
    lin(nodrep, by(ios, nodu))
    lin(t16, cut(i32, 0, 16), 16.0, 16.0)
    act(cl["o16"], cl["r16"], AF.Relu, 1.0, -224.0)
    lin(cl["want"], cl["o16"], -0.125, cl["r1"])
    lin(cl["cap"], cl["o16"], -0.125, 17.0)
    lin(cl["cap1"], cl["o16"], -0.125, 16.0)
    lin(cl["rh"], cl["r"], -8.0, 8.0)
    lin(cl["t0"], cl["r16"], 1.0, -248.0)
    same(tc, l256, cl["want"])
    act(tb, a1, AF.Relu, -1.0, cl["cap"])
    lin(tb, tb, -1.0, cl["cap1"])
    scan(tw, tb, tc, A.max, A.mult)
    scan(to, a1, d256, A.max, A.mult)
    lin(th, l256, float(C), -7.0 * C)
    lin(td, l256, -1.0)
    tt(th, th, td, A.max)
    lin(cut(th, 7, 256, 16), cut(k16n, 0, 16), 0.0, -7.0)
    lin(ends(th), cut(k16n, 0, 16), 0.0)
    tt(th, th, ta, A.mult)
    lin(cut(thw, 256, 512), th)
    lin(cut(tww, 256, 512), tw)
    lin(d16, cut(diag, 0, 16))
    for h in range(1, 8):
        lin(cut(w2, C * h, C * h + C), loc, cut(d16, h + 7, h + 8), cut(d16, h + 7, h + 8))
    lin(mh, loc, 0.0)
    lin(ends(mh), self_, 1.0, -4096.0)
    for i in (0, 1):
        lin(cut(kq, i, TR, 2), k32n, 0.0, 256.0 * i)
    act(cl["nz"], cl["r"], AF.Sign)
    act(cl["s7"], cl["r"], AF.Sign, 1.0, -6.5)
    act(cl["a14"], cl["r"], AF.Abs, 1.0, -14.0)
    act(cl["t1"], cl["a14"], AF.Sign)
    act(cl["msend"], cl["s7"], AF.Relu, cl["t1"])
    lin(cl["mown"], cl["msend"], -1.0, 1.0)
    act(cl["r8"], cl["r"], AF.Sign, 1.0, -7.5)
    lin(cl["v1"], cl["r"], 1.0, 8.0)
    lin(cl["rm8"], cl["r"], 1.0, -8.0)
    lin(cl["vsel"], cl["r8"], 8.0, cl["rm8"])
    same(te, l256, cl["v1"])
    same(tf, l256, cl["vsel"])
    act(keep32, l32, AF.Sign)
    lin(cl["k3"], cl["r"], 1.0, C - 7 - PO + 1024.0)
    act(cl["s14"], cl["r"], AF.Sign, -1.0, 13.5)
    act(cl["m7"], cl["s14"], AF.Relu, cl["msend"])
    lin(k3, k16n, 0.5, cl["k3"])
    lin(k3, k3, cl["m7"], -1024.0)
    for a, b in HALVES:
        lin(ends(cut(mt, 16 * a, 16 * b)), cut(k16n, 0, b - a), 1.0, 31.0)
    quant(W["qv"], W["sv"], W["vt0"])

    def plane(b):
        return cut(W["win"], WW * b, WW * b + C)

    def block(name, b, n):
        return cut(W[name], n * b, n * b + n)

    for rnd in range(3):
        peer = T.cores[rank ^ MASKS[rnd]]
        ne = len(topo.engines(peer, core))
        start, final = rnd == 0, rnd == 2
        sa, lda, sb, ldb, qs, ss, ql, sl = (W[k + str(rnd)] for k in ("sa", "la", "sb", "lb", "qs", "ss", "ql", "sl"))

        for b in range(4):
            mm(ps[fb[b]], block("qe", b, 128), block("se", b, 128), W["qx"], W["sx"])
            lin(plane(b), ps[fb[b]])
        for b in (0, 1):
            dma("y", ap(block("fo", b, C)), ap(plane(b)), [plane(b)], [block("fo", b, C)], "df" + "ab"[b] + str(rnd), 16, 1000)

        for a, b in HALVES if start else WHOLE:
            (R, N), U = trees(a, b), trees(0, b)[0]
            lin(R(lb), by(U(la), N(j1)))
            lin(R(m1), by(tm, N(m2u)))
            take(R(cv2), R(lb), R(mkg))
            ts(N(j2), ends(R(cv2)), PO, A.add)
            lin(R(lc), by(U(lb), N(j2)))
            lin(R(g2), by(U(m1), N(j2)), -1.0, 192.0)
            take(R(cv4), R(lc), R(mkg))
            ts(N(j4), ends(R(cv4)), PO, A.add)
            scan(R(m2), R(g2), R(m1), A.max, A.subtract)
            lin(R(g4), by(U(m2), N(j4)), -1.0, 192.0)
            scan(R(m4), R(g4), R(m2), A.max, A.subtract)
            lin(R(g8), by(U(m4), N(j4)))
            lin(R(g9), by(U(g8), N(j4)), -1.0, 127.0)
            scan(R(mm_), R(g9), R(m4), A.max, A.subtract)
            seg(R(msum), R(mm_), A.add)
            lin(N(szn), ends(R(msum)), 0.5, 8.0)
            lin(N(csz), ends(R(msum)), -0.5, 8.0)

        for a, b in HALVES:
            R, out = trees(a, b)[0], cut(ps[0 if a else 5], 0, H)
            mm(out, W["qu"], W["su"], R(W["qx"]), R(W["sx"]))
            if start:
                lin(R(ssb), out)
            else:
                tt(R(ssb), out, R(sigc), A.mult)
        for p in HALVES:
            (R, N), snm = trees(*p), cut(sn[p], 16, H + 16)
            if start:
                tt(snm, by(ssb, N(nodu)), R(sig), A.mult)
            else:
                lin(snm, by(ssb, N(nodu)))
            lin(R(neg), snm, -1.0)
            turn(cut(both[p], 0, H), snm)
            turn(cut(both[p], H, C + 32), sn[p])
            tt(R(cmp1), by(both[p], N(tsel)), R(neg), A.is_gt)
            scan(R(scs), R(d0s), R(cmp1), A.mult, A.add)
            ts(N(stu), ends(R(scs)), cl["r"], A.add)
        ts(sou, ends(scs), cl["r17"], A.add)
        lin(st16, ends(scs), 16.0, cl["t0"])
        tt(stq, st16, kq, A.add)
        lin(cut(fsd, 1, C, 16), ends(scs), -8.0, cl["rh"])

        for a, b in HALVES:
            R, N = trees(a, b)
            tt(R(xx), by(t16, N(stu)), R(mm_), A.mult)
            lin(R(pst), by(cut(xx, 0, 16 * b), N(j1)), -1.0, -8.0)
            take(R(cvp), R(pst), R(mkl))
            tt(N(dl), ends(R(cvp)), N(st16), A.subtract)
            seg(R(sc1), R(xx), A.max)
            seg(R(sc2), R(xx), A.min)
            tt(N(n1), ends(R(sc1)), N(szn), A.add)
            tt(N(n2), N(csz), ends(R(sc2)), A.subtract)
            tt(starts(R(ks)), N(n1), N(n2), A.min)
            ts(N(keyu), starts(R(ks)), 0.0, A.add)
            seg(R(kb), R(ks), A.add)
            tt(R(cmp2), by(iob, N(keyu)), R(kb), A.is_lt)
            act(N(nf), ends(R(sc2)), AF.Relu, -1.0, -255.0)
            tt(N(pa), N(nf), N(dl), A.mult)
            tt(N(qb), N(pa), N(stq), A.add)
            seg(R(rk), R(cmp2), A.add)
            tt(N(na), ends(R(rk)), N(qb), A.add)
            ts(N(idxw), N(na), 248.0, A.add)
            lin(R(hi), by(thw, N(idxw)))
            take(R(his), R(hi), R(mh))
        ts(sa, ends(his), 4096.0, A.add)
        remote(lda, sa, "aa%d" % rnd, peer, 0)
        pick(wd, tww, idxw)
        place(wds, wd, k64r)
        lin(sb, ends(wds), cl["msend"])
        remote(ldb, sb, "ab%d" % rnd, peer, 0)

        tt(pj, nf, dj, A.mult)
        tt(pn, pj, self_, A.add)
        cp(pnu, pn)
        lin(pcol, by(nodrep, pnu))
        tt(vb, by(tvw, idxw), pcol, A.mult)
        scan(vs, keep32, vb, A.mult, A.add)
        ts(vu, cut(vs, 31, C, 32), SO, A.add)
        for b in range(4):
            lin(cut(W["vt"], b, 4 * VW, 4), by(plane(b), vu), 2.0)
        quant(qs, ss, W["vt"])
        remote(ql, qs, "av%d" % rnd, peer, 1100)
        remote(sl, ss, "av%d" % rnd, peer, 400)

        seg(los, hi, A.min)
        ts(lou, ends(los), -1.0, A.mult, cl["r16"], A.add)
        lin(cut(w2, 0, C), by(to, lou), cl["nz"])
        lin(b4, by(to, sou))
        place(ov, b4, k64r)
        ts(ou, ends(ov), PO - 1.0, A.add)
        lin(cut(srcw, 0, C), by(nodrep, ou))
        lin(osrep, by(loc if final else iom, ou))
        scan(cut(fs, 0, C), fs0, fsd, A.add, A.min)
        lin(own, ends(wds), cl["mown"])

        arrive([lda], "aa%d" % rnd, ne)
        arrive([ldb], "ab%d" % rnd, ne)
        arrive([ql, sl], "av%d" % rnd, 2 * ne)
        tt(cg, own, ldb, A.add)
        tt(o2f, cg, k3, A.max)
        ts(o2u, o2f, PO, A.add)
        ts(cgu, cg, PO, A.add)
        lin(srcj, by(srcw, o2u))
        lin(lnkj, by(osrep, cgu))
        if not final:
            lin(ends(lnkj), ends(osrep))
        for a, b in HALVES:
            R, N = trees(a, b)
            lin(R(inv), by(w2, N(lda)))
            place(R(invs), R(inv), R(k64r))
            ts(N(idxu), ends(R(invs)), PO, A.add)
            either(R(em), by(fs, N(idxu)), (0.0, None, A.max), (AF.Relu, 1.0, 0.0))
            seg(R(ems), R(em), A.add)
            tt(starts(R(ks)), N(st16), ends(R(ems)), A.add)
            scan(R(yy), R(ks), R(em), A.max, A.subtract)
            either(R(flag), R(yy), (-8.0, 15.0, A.not_equal, A.mult), (AF.Abs, 2.0, 16.0))
            scan(R(tsc), R(flag), R(mt), A.min, A.add, 64.0)
            ts(N(tu), ends(R(tsc)), -16.0, A.add)
        for b in range(4):
            mm(cut(ps[ub[b]], 0, VW), block("qe", b, 128), block("se", b, 128), ql, sl)
            lin(cut(W["win"], WW * b + C, WW * b + WW), cut(ps[ub[b]], 0, VW))
        pick(b2, srcj, tu, local=True)
        pick(b1, b2, invu)
        for a, b in HALVES:
            R, N = trees(a, b)
            take(R(b1h), R(b1), R(mkc))
            ts(N(eu), ends(R(b1h)), SO + 512.0, A.add)
        pick(oprep if final else la, lnkj, tu, local=True)
        if final:
            dma("y", T.op[:], T.pf[0:128:16, oprep[1]:oprep[2]], [oprep], [], "dop")
        else:
            take(cv1, la, mkg)
            ts(j1, ends(cv1), PO, A.add)
            tt(pr, ends(cv1), kpair, A.add)
            tt(dj, ends(cv1), n3, A.subtract)
            ts(m2u, pr, PO, A.add)

        for a, c in HALVES:
            (R, N), L = trees(a, c), (lambda b: cut(W["zt"], 64 * a + b, 64 * c, 4))
            for b in (3, 2):
                lin(R(block("hh", b - 2, C)), by(block("win", b, WW), N(eu)))
            for b in (0, 1):
                tt(L(b), by(block("win", b, WW), N(eu)), R(block("fo", b, C)), A.add)
            for b in (3, 2):
                tt(L(b), R(block("hh", b - 2, C)), R(ps[fb[b]]), A.add)
            for b in range(4):
                lin(R(block("z32", b, C)), L(b), 32.0)
            quant(R(W["qz"]), R(W["sz"]), cut(W["zt"], 64 * a, 64 * c))
        for a, c in HALVES:
            R = trees(a, c)[0]
            for b in range(4):
                out = cut(ps[(fb if a else wb)[b]], 0, H)
                mm(out, block("wq", b, 128), block("wsb", b, 128), R(W["qz"]), R(W["sz"]))
                tt(R(block("x32", b, C)), out, R(block("z32", b, C)), A.add)
                lin(cut(W["xt"], 64 * a + b, 64 * c, 4), R(block("x32", b, C)), 0.03125)
            quant(R(W["qx"]), R(W["sx"]), cut(W["xt"], 64 * a, 64 * c))

    for h in (0, 1):
        dma("y", T.oc[:, 4 * H * h:4 * H * h + 4 * H], ap(block("qx", h, H)).bitcast(dt.uint8), [block("qx", h, H)], [], "doc", 32, 500)
        half = cut(ysb, H * h, H * h + H)
        mm(cut(ps[5 + h], 0, H), W["qv"], W["sv"], block("qx", h, H), block("sx", h, H))
        lin(half, cut(ps[5 + h], 0, H))
        dma("ys"[h], T.y[:, H * h:H * h + H], ap(half), [half], [], "dy%d" % h, 16, 500)
    for k in range(4):
        dma("y", T.osc[4 * k:4 * k + 4, :], T.sx[32 * k:32 * k + 4, :], [W["sx"]], [], "dos", 64)
    if not CHOSEN:
        deps = _needs(ops)
        CHOSEN.extend([deps, _order(ops, deps)])
    _emit(g, T, ops, *CHOSEN)
    for s, n in (("dop", 16), ("doc", 32), ("dos", 64), ("dy0", 16)):
        g.sync.wait_ge(T.sem[s], n)
    g.scalar.wait_ge(T.sem.dy1, 16)
    g.wait_ge(T.sem.sent, sent[0])
